import numpy as np, ml_dtypes
CORES = [10,34,74,98]
N = 4
BF = ml_dtypes.bfloat16
def gentries(a):
    return np.ascontiguousarray(a.reshape(8, 16, -1).transpose(0, 2, 1)).reshape(8, -1)
def gtable(e):
    e = np.asarray(e); return np.ascontiguousarray(e.reshape(8, -1, 16).transpose(0, 2, 1)).reshape(128, -1).astype(np.int32)
D, B, W, K, NB, S, RO = 3, 4, 4096, 4096, 256, 16, 3
def parts(rng):
    return rng.integers(0, 256, (N, 8, 16, W)), rng.integers(0, W, (N, 8, K)), rng.integers(0, 256, (N, 8, 16, NB)), rng.integers(900, 1701, (N, 8, RO))
def pack(X, L, z, t):
    return {"x0": np.ascontiguousarray(X.reshape(N, 128, W)).astype(np.float32).astype(BF), "l0": np.stack([gtable(a) for a in L]),
            "z0": np.ascontiguousarray(z.reshape(N, 128, NB)).astype(np.float32).astype(BF), "th": np.ascontiguousarray(t).astype(np.int32)}
def setup_inputs(rng):
    return pack(*parts(rng))
def setup_inputs_spread(rng):
    X = np.minimum((np.exp2(8 * rng.random((N, 8, 1, W))) * rng.random((N, 8, 16, W))).astype(np.int64), 255)
    z = np.minimum((np.exp2(8 * rng.random((N, 8, 1, NB))) * rng.random((N, 8, 16, NB))).astype(np.int64), 255)
    L = np.minimum((W * rng.random((N, 8, K)) ** rng.choice(np.array([1.0, 2.0, 4.0]), (N, 8, 1))).astype(np.int64), W - 1)
    t = np.minimum(np.exp2(12 * rng.random((N, 8, RO))).astype(np.int64), 4080)
    return pack(X, L, z, t)
def setup_inputs_ends(rng):
    X = 255 * rng.integers(0, 2, (N, 8, 16, W)); X = np.where(rng.random((N, 8, 1, W)) < 0.5, 255 * rng.integers(0, 2, (N, 8, 1, W)), X)
    z = 255 * rng.integers(0, 2, (N, 8, 16, NB)); z = np.where(rng.random((N, 8, 1, NB)) < 0.5, 255 * rng.integers(0, 2, (N, 8, 1, NB)), z)
    sw = rng.integers(0, 2, (N, 8, 1)); X[..., 0] = 255 * sw; X[..., W - 1] = 255 * (1 - sw)
    z[..., 0] = 255 * rng.integers(0, 2, (N, 8, 1)); z[..., NB - 1] = 255 * rng.integers(0, 2, (N, 8, 1))
    L = (W - 1) * rng.integers(0, 2, (N, 8, K)); m = rng.random((N, 8, K)) < 0.25; m[:, 1::2] = False
    L = np.where(m, rng.integers(0, W, (N, 8, K)), L)
    L[..., 0] = W - 1; L[..., 1] = 0; L[..., K - 2] = 0; L[..., K - 1] = W - 1
    t = 4080 * rng.integers(0, 2, (N, 8, RO)); t[:, 0, 0] = 0; t[:, 1, 0] = 4080
    L[:, 5] = 0; L[:, 6] = W - 1; L[:, 7] = 0; X[:, 7] = 0; X[:, 7, :, 0] = 255; X[:, 7, :, W - 1] = 255; z[:, 7] = 0; t[:, 7, 0] = 0
    b = int(rng.integers(0, 2))
    for r in range(N):
        if (r + b) & 1: L[r, 7, K - 1] = 1
    return pack(X, L, z, t)
def setup_inputs_corners(rng):
    X, L, z, t = parts(rng); t = rng.integers(100, 3600, (N, 8, RO)); t[:, :, 0] = rng.integers(300, 2000, (N, 8))
    z = np.where(rng.random((N, 8, 1, NB)) < 0.5, 255 * rng.integers(0, 2, (N, 8, 1, NB)), z)
    for r in range(N):
        kinds = rng.permutation(8)
        for g in range(8):
            j = int(kinds[g]); beg = np.zeros(K, np.int64)
            if j == 0: t[r, g, 0] = rng.choice(np.array([300, 4080]))
            elif j == 1: beg[:] = 1; t[r, g, 0] = rng.choice(np.array([0, 3000]))
            elif j == 2: beg[K - 1] = 1
            elif j == 3: beg[1] = 1
            elif j == 4: beg[::2] = 1
            elif j == 5: beg[::3] = 1
            elif j == 6:
                c = np.add.accumulate(rng.choice(np.array([1, 2, 3, 4, 5, 15, 16, 17, 64, 255, 256, 257]), K)); beg[c[c < K]] = 1
            else: beg[K // 2 + 1] = 1
            beg[0] = 1; cl = np.add.accumulate(beg) & 1
            bit = rng.integers(0, 2, W); bit[0] = 0; bit[W - 1] = 1
            X[r, g] = rng.integers(0, 16, (16, W)) + 240 * bit
            a0 = np.flatnonzero(bit == 0); a1 = np.flatnonzero(bit == 1)
            n = np.where(cl == 1, a1[rng.integers(0, len(a1), K)], a0[rng.integers(0, len(a0), K)])
            L[r, g] = np.where(rng.random(K) < 0.2, (W - 1) * cl, n)
    return pack(X, L, z, t)
def late(rng, X, L, z, t, dg):
    k = np.arange(K); c = np.arange(W); h = B * (D - 1)
    n = 32 * int(rng.integers(0, 9)) + int(rng.integers(8, 25)); R = np.zeros(K, np.int64); R[rng.permutation(K)[:n]] = 1
    for g in range(8):
        r = (g - dg) % N
        a = 8 * rng.integers(0, 17, (8, 1)); e = 8 * rng.integers(4, 11, (8, 1)); v = 8 * rng.integers(4, 26, (7, 1)); q = int(np.sum(e))
        X[r, g] = np.concatenate([a + e * (((c >> h) & 1) ^ rng.integers(0, 2, (8, 1))), v * ((c >> (h + 1)) & 1), np.full((1, W), 4)])
        z[r, g, 8:15] = v * (g & 1)
        m = rng.integers(0, W, K)
        for j in range(D): m = (m & ~(1 << (B * j))) | ((k & 1) << (B * j))
        m = m & ~4
        L[r, g] = (m & ~(2 << h)) | (((g & 1) ^ R) << (h + 1))
        t[r, g, 0] = rng.integers(0, q); t[r, g, 1] = q - 1 - (n & 31); t[r, g, 2:] = q - rng.integers(1, 9, RO - 2)
def few(rng, X, L, z, t, dg):
    k = np.arange(K); c = np.arange(W); h = B * (D - 1); o = int(rng.integers(0, 8))
    rows = 16 * rng.permutation(NB)[:3] + rng.integers(0, 16, 3)
    b = np.zeros((8, 3), np.int64)
    for j, st in enumerate(((0, 3), (0, 3), (0, 5))):
        for s in st: b[(s + o) % 8, j] = 1; b[(s + 1 + o) % 8, j] = 1
    zb = b * (RO & 1); w = b; u = zb; n = np.zeros((8, RO), np.int64)
    for rnd in range(1, RO):
        take = (w != u) & (np.roll(w, 1, axis=0) == u); w = np.where(take, u, w); u = np.abs(w - u); n[:, rnd] = np.add.reduce(take.astype(np.int64), axis=1)
    for g in range(8):
        r = (g - dg) % N
        a = 8 * rng.integers(0, 2, (11, 1)); e = 8 * rng.integers(24, 31, (11, 1)); v = 8 * rng.integers(4, 26, (4, 1)); q = int(np.sum(e))
        X[r, g] = np.concatenate([a + e * (((c >> h) & 1) ^ rng.integers(0, 2, (11, 1))), v * ((c >> (h + 1)) & 1), np.full((1, W), 4)])
        zz = z[r, g]; zz[11:15, rows >> 4] = v * zb[g]
        bt = np.zeros(K, np.int64); bt[rows] = b[g]
        L[r, g] = (rng.integers(0, W, K) & ~(3 << h) & ~4) | ((k & 1) << h) | (bt << (h + 1))
        t[r, g, 0] = rng.integers(0, q); t[r, g, 1:] = q - 1 - n[g, 1:]; t[r, g, RO - 1] = q - max(int(n[g, RO - 1]), 1)
def setup_inputs_crowd(rng):
    X = rng.integers(0, 8, (N, 8, 16, W)); z = rng.integers(0, 8, (N, 8, 16, NB)); L = np.zeros((N, 8, K), np.int64)
    t = rng.choice(np.array([0, 10, 20]), (N, 8, RO)); t[:, :, 0] = 0; rep = (W - 1) // (2 ** B - 1)
    dg = int(rng.integers(0, N))
    for r in range(N):
        kinds = rng.permutation(np.array([0, 1, 2, 3, 4, 0, 1, 4])[:8 - 8 // N]); i = 0
        for g in range(8):
            if (g - r) % N == dg: continue
            p = g & 1; ds = np.arange(p + 2, 2 ** B, 2); xv = X[r, g]; kind = int(kinds[i]); i += 1
            xv[:, ds * rep] = rng.integers(128, 256, (16, len(ds))); xv[0, ds * rep] = 128 + ds
            if kind == 4:
                e = ds[rng.integers(0, len(ds), NB)] * rep; L[r, g] = np.repeat(e, 16); z[r, g] = xv[:, e]
            else:
                d = ds[rng.integers(0, len(ds), K)] * rep
                if kind > 0:
                    k0 = (K - 1, 0, int(rng.integers(1, K - 1)))[kind - 1]; d[k0] = p * rep; z[r, g, :, k0 // 16] = xv[:, p * rep]
                L[r, g] = d
    late(rng, X, L, z, t, dg)
    return pack(X, L, z, t)
def setup_inputs_ties(rng):
    X, L, z, t = parts(rng); odd = int(rng.integers(0, 2)); dg = int(rng.integers(0, N))
    for r in range(N):
        ring = np.flatnonzero((np.arange(8) - r) % N == dg); rest = rng.permutation(np.setdiff1d(np.arange(8), ring))
        p = np.concatenate([rest[:-1], ring, rest[-1:]]); tv = rng.permutation(np.array([0, 31, 4079, int(rng.integers(32, 4079))]))
        for i in range(4):
            g = int(p[i]); T = int(tv[i]); a = T // 16 + (np.arange(16) < T % 16); b = a + (np.arange(16) == T % 16)
            v = np.stack([np.zeros(16, np.int64), a, b])[:, rng.permutation(16)]
            X[r, g] = v[rng.integers(0, 3, W)].T
            t[r, g, 0] = T; t[r, g, 1:] = np.maximum(T - rng.integers(0, 32, RO - 1), 0)
        for i in range(4, 8):
            g = int(p[i]); c = np.arange(W); t[r, g] = rng.integers(700, 1300, RO)
            if i == 7:
                up = (r + odd) & 1; X[r, g] = 255 * up; z[r, g] = 255 * (1 - up)
                X[r, g, rng.integers(0, 16, W), c] += (1 - 2 * up) * rng.integers(0, 2, W)
                continue
            base = rng.integers(0, 201, 16)
            X[r, g] = base[(np.arange(16)[:, None] + rng.integers(0, 16, W)[None, :]) % 16]
            X[r, g, rng.integers(0, 16, W), c] += rng.integers(0, 2, W)
            z[r, g] = 255 * rng.integers(0, 2, (1, NB))
    few(rng, X, L, z, t, dg)
    return pack(X, L, z, t)
def check_inputs(d):
    bad = []
    for k, lo, hi in (("x0", 0, 255), ("l0", 0, W - 1), ("z0", 0, 255), ("th", 0, 4080)):
        v = np.asarray(d[k]).astype(np.float64)
        if not (np.min(v) >= lo and np.max(v) <= hi): bad.append("range of " + k)
        elif not np.all(v == np.floor(v)): bad.append("whole numbers in " + k)
    return bad
def reference(x0, l0, z0, th):
    X = x0.astype(np.float32).astype(np.int32).reshape(N, 8, 16, W); z = z0.astype(np.float32).astype(np.int32).reshape(N, 8, 16, NB)
    L = np.stack([gentries(a) for a in l0]).astype(np.int64); t = th.astype(np.int64); k = np.arange(K)
    x = np.take_along_axis(X, L[:, :, None, :], 3); A = np.zeros((N, 8), np.int64); low = 2 ** B - 1
    for rnd in range(RO):
        beg = np.ones((N, 8, K), bool)
        beg[..., 1:] = np.add.reduce(np.abs(x[..., 1:] - x[..., :-1]), axis=2) > (t[:, :, rnd] + (A & 31))[..., None]
        beg[..., 0] = True
        s = np.maximum.accumulate(np.where(beg, k, 0), axis=2)
        nx = np.minimum.accumulate(np.where(beg, k, K)[..., ::-1], axis=2)[..., ::-1]
        ln = np.concatenate([nx[..., 1:], np.full((N, 8, 1), K)], axis=2) - s
        P = np.zeros((N, 8, K), np.int64)
        for c in range(D):
            q = D * (k - s) + c; pl = np.zeros((N, 8, K), np.int64)
            for j in range(1, D): pl = pl + (q >= j * ln)
            P = (P << B) | ((np.take_along_axis(L, s + q - pl * ln, 2) >> (B * (D - 1 - pl))) & low)
        hi = np.roll(P >> (B * (D - 1)), (1, 1), axis=(0, 1)); lo = np.roll(P & low, (2, 2), axis=(0, 1))
        M = (hi << (B * (D - 1))) | (((P >> B) & (2 ** (B * (D - 2)) - 1)) << B) | lo
        y = np.take_along_axis(X, P[:, :, None, :], 3); y2 = np.take_along_axis(X, M[:, :, None, :], 3); zr = np.repeat(z, 16, axis=3)
        took = np.add.reduce(np.abs(y2 - zr), axis=2) < np.add.reduce(np.abs(y - zr), axis=2)
        L = np.where(took, M, P); x = np.where(took[:, :, None, :], y2, y); A = np.add.reduce(took.astype(np.int64), axis=2)
        Y = np.max(x.reshape(N, 8, 16, NB, 16), axis=4)
        if rnd < RO - 1:
            col = S * np.arange(NB) + (np.add.reduce(Y, axis=2) & (S - 1))
            np.put_along_axis(X, col[:, :, None, :].astype(np.int64), (Y + z) >> 1, 3)
        z = np.abs(Y - z)
    return {"ly": np.stack([gtable(a) for a in L]).astype(np.float32), "xy": x.reshape(N, 128, K).astype(np.float32).astype(BF), "zy": z.reshape(N, 128, NB).astype(np.float32).astype(BF)}

@@ -1,0 +1,574 @@
+from concourse.bass import DstId, RemoteDMATransfer
+from concourse.mybir import AluOpType as A, AxisListType, ActivationFunctionType as F
+
+WIN = 8 * 4096 + 16
+BIG = 32768.0
+M16 = 201326592.0
+M1 = 12582912.0
+f32, bf, i32, u16 = "float32", "bfloat16", "int32", "uint16"
+
+
+def sb(n, d):
+    return ("sbuf", [128, n], d)
+
+
+SCRATCH = {
+    "win": sb(WIN, bf), "tab": sb(4096, bf), "xb": sb(4112, bf), "ga": sb(4096, bf), "gb": sb(4096, bf),
+    "d3": sb(4096, bf), "a3b": sb(4096, bf), "d4": sb(4096, bf), "a4b": sb(4096, bf), "tmp": sb(4096, bf),
+    "zb": sb(1024, bf), "ym": sb(512, bf), "li": sb(256, i32), "thi": sb(4, i32), "th8": sb(4, f32), "thf": sb(4, f32),
+    "zc": sb(256, bf), "z2": sb(512, bf), "zd": sb(256, bf), "zs": sb(256, f32), "avg": sb(256, bf),
+    "pint": sb(4, i32), "pf": sb(16, f32), "colf": sb(16, f32), "colb": sb(256, bf), "c256": sb(256, bf), "pt": sb(16, u16), "fl": sb(16, u16),
+    "flf": sb(16, f32), "cb": sb(16, f32), "ib": sb(256, bf), "ib256": sb(256, bf), "nib": sb(128, bf), "nib256": sb(128, bf),
+    "sw": sb(128, f32), "sw2": sb(128, f32), "eb": sb(6 * 144, bf), "bo": sb(128, f32), "bob": sb(128, bf), "lt": sb(128, bf), "ut": sb(128, bf),
+    "m16": sb(16, f32), "cc": sb(32, bf), "ct": sb(80, f32), "ones": sb(256, f32),
+    "cm75": sb(256, bf), "cm05": sb(256, bf), "dinit": sb(256, bf), "mask0": sb(256, f32), "oneb": sb(256, bf),
+    "nu": sb(256, u16), "pu": sb(256, u16), "mu": sb(256, u16), "oa": sb(256, u16), "ob": sb(256, u16), "cu": sb(16, u16),
+    "ni": sb(256, i32), "digi": sb(768, i32), "dig": sb(768, bf),
+    "nb": sb(264, bf), "h1": sb(256, bf), "h2": sb(256, bf), "s1": sb(256, f32), "s2": sb(256, f32), "s3": sb(256, f32),
+    "s4": sb(256, f32), "s5": sb(256, f32), "s6": sb(256, f32), "s7": sb(256, f32), "s8": sb(256, f32), "pm": sb(256, i32),
+    "r12": sb(32, bf), "car": sb(4, f32), "thr": sb(4, f32), "acc": sb(4, f32), "ai": sb(4, i32), "ui": sb(32, i32), "uf": sb(16, f32),
+    "r16": sb(256, bf), "lyf": sb(256, f32),
+    "pb0": ("psum", [128, 512], f32), "pb1": ("psum", [128, 512], f32), "pd": ("psum", [128, 512], f32), "pp": ("psum", [128, 512], f32),
+    "pq": ("psum", [128, 512], f32), "pmm": ("psum", [128, 512], f32), "pv0": ("psum", [128, 512], f32), "pv1": ("psum", [128, 512], f32),
+}
+for _t in range(3):
+    for _n in ("hi", "lo", "hin", "lin"):
+        SCRATCH["%s%d" % (_n, _t)] = sb(256, bf)
+SEMAPHORES = ["cv", "cs", "ct", "cg", "ldx", "ldl", "ldz", "ldt", "fill", "oly", "ozy", "oxy"]
+for _t in range(3):
+    SEMAPHORES += ["la%d" % _t, "lb%d" % _t, "ah%d" % _t, "al%d" % _t, "loc%d" % _t]
+
+CELLS = [(3, 2, 1, 0), (3, 5, 2, 0), (4, 1, 1, 0), (4, 2, 1, 1), (4, 4, 2, 0), (4, 5, 2, 1),
+         (0, 1, 0, 0), (0, 2, 0, 0), (0, 4, 1, 0), (0, 5, 1, 0), (0, 7, 0, 0),
+         (1, 0, 0, 1), (1, 1, 0, 1), (1, 3, 1, 1), (1, 4, 1, 1), (1, 6, 2, 1), (1, 7, 1, 0),
+         (2, 0, 0, 2), (2, 3, 1, 2), (2, 6, 2, 2), (2, 7, 2, 0)]
+FILL = {"s": [0, 1, 2, 3, 12], "v1": [13, 14, 15, 24, 25, 26, 27], "v2": [4, 5, 6, 7, 29, 30, 31], "g": [20, 21, 22, 23, 28],
+        "y": [8, 9, 10, 11, 16, 17, 18, 19]}
+S0 = (62, 150, 150)
+NVA = (7, 7, 7)
+MODES = (("SS", 2), ("VV", 2), ("VS", 2), ("VS", 2))
+ORDER = ("d1", "a0", "a1", "a2", "a3")
+FINV = 96
+
+
+def rank_program(g, core, T, topo):
+    rank = T.rank_of(core)
+    if rank is None:
+        return
+    n = len(T.cores)
+    ops = []
+    lastw, readers, bank = {}, {}, {}
+
+    def op(eng, fn, r=(), w=(), b=(), sem=None, inc=16):
+        me = len(ops)
+        deps = set()
+        for t in r:
+            if t in lastw:
+                deps.add(lastw[t])
+        for t in w:
+            if t in lastw:
+                deps.add(lastw[t])
+            deps.update(readers.get(t, ()))
+        for t in b:
+            for e, i in bank.setdefault(t, {}).items():
+                if e != eng:
+                    deps.add(i)
+            bank[t][eng] = me
+        for t in r:
+            readers.setdefault(t, []).append(me)
+        for t in w:
+            lastw[t] = me
+            readers[t] = []
+        deps = [d for d in deps if not (eng == "t" and ops[d]["eng"] == "t") and not (sem is not None and ops[d]["sem"] == sem)]
+        ops.append({"eng": eng, "fn": fn, "deps": deps, "sem": sem, "inc": inc})
+
+    V, S, PE = g.vector, g.scalar, g.tensor
+
+    def ts(out, in0, s1, s2, o0, o1, r, w, b=()):
+        if o1 is None:
+            op("v", lambda: V.tensor_scalar(out, in0, s1, None, o0), r, w, b)
+        else:
+            op("v", lambda: V.tensor_scalar(out, in0, s1, s2, o0, o1), r, w, b)
+
+    def tt(out, a, c, o, r, w, b=()):
+        op("v", lambda: V.tensor_tensor(out, a, c, o), r, w, b)
+
+    def cp(out, a, r, w, b=()):
+        op("v", lambda: V.tensor_copy(out, a), r, w, b)
+
+    def ms(out, c, w):
+        op("v", lambda: V.memset(out, c), (), w)
+
+    def scan(out, d0, d1, ini, o0, o1, r, w, b=()):
+        op("v", lambda: V.tensor_tensor_scan(out, d0, d1, ini, o0, o1), r, w, b)
+
+    def red(out, a, o, r, w, b=()):
+        op("v", lambda: V.tensor_reduce(out, a, AxisListType.X, o), r, w, b)
+
+    def act(out, a, f, r, w, b=(), bias=0.0, scale=1.0, acc=None):
+        if acc is None:
+            op("s", lambda: S.activation(out, a, f, bias=bias, scale=scale), r, w, b)
+        else:
+            op("s", lambda: S.activation(out, a, f, bias=bias, scale=scale, accum_out=acc), r, w, b)
+
+    def mm(out, l, rh, st, sp, r, b):
+        op("t", lambda: PE.matmul(out, l, rh, st, sp), r, (), b)
+
+    def iota(out, pat, base, cm, w, flt=True):
+        if flt:
+            op("g", lambda: g.iota(out, pat, base, cm, allow_small_or_imprecise_dtypes=True), (), w)
+        else:
+            op("g", lambda: g.iota(out, pat, base, cm), (), w)
+
+    def sel(out, a, pat, o, base, cm, r, w):
+        op("g", lambda: g.affine_select(out, a, pat, o, 0.0, base, cm), r, w)
+
+    def dma(q, out, a, r, w, sem):
+        op(q, lambda: (g.sync if q == "y" else g.scalar).dma_start(out, a), r, w, sem=sem)
+
+    def xt(c0, c1):
+        return [("x", j) for j in range(c0 // 32, (c1 - 1) // 32 + 1)]
+
+    WT = [("W", j) for j in range(8)] + [("Wf", j) for j in range(32)]
+    I = T.ib[:, 0:128]
+    ID = F.Identity
+
+    def E(w, c):
+        return T.eb[:, 144 * w + 15 - c:144 * w + 143 - c]
+
+    def EW(w):
+        return T.eb[:, 144 * w + 15:144 * w + 143:16]
+
+    def runs(us):
+        out = []
+        for u in us:
+            if out and out[-1][1] == u:
+                out[-1][1] = u + 1
+            else:
+                out.append([u, u + 1])
+        return [(1024 * a, WIN if c == 32 else 1024 * c, [("Wf", j) for j in range(a, c)]) for a, c in out]
+
+    ms(T.zb[:], 0.0, ["zb"])
+    ms(T.thi[:], 0, ["thi"])
+    dma("s", T.li[:], T.l0[:], (), ["li"], "ldl")
+    dma("y", T.tab[:], T.x0[:], (), ["tab"], "ldx")
+    dma("y", T.thi[0:128:16, 0:3], T.th[:], (), ["thi"], "ldt")
+    dma("y", T.zc[:], T.z0[:], (), ["zc"], "ldz")
+    ms(T.oneb[:], 1.0, ["oneb"])
+    iota(T.pint[:, 0:1], [[0, 1]], 0, 1, ["p0"], False)
+    iota(T.colf[:], [[1, 16]], 0, 0, ["colf"])
+    iota(T.flf[:], [[32, 8], [-16, 2]], 16, 0, ["flf"])
+    sel(T.ib[:], T.oneb[:], [[0, 2], [-1, 128]], A.is_equal, 0, 1, ["oneb"], ["ib"])
+    iota(T.mask0[:], [[0, 8], [1, 2], [0, 16]], 0, 0, ["mask0"])
+    sel(T.bob[:], T.oneb[:, 0:128], [[-16, 8], [0, 16]], A.is_ge, 0, 1, ["oneb"], ["bob"])
+    sel(T.bob[:], T.bob[:], [[16, 8], [0, 16]], A.is_ge, 15, -1, ["bob"], ["bob"])
+    sel(T.lt[:], T.bob[:], [[1, 128]], A.is_gt, 0, -1, ["bob"], ["lt"])
+    sel(T.ut[:], T.bob[:], [[-1, 128]], A.is_gt, 0, 1, ["bob"], ["ut"])
+    iota(T.colb[:], [[1, 256]], 0, 0, ["colb"])
+    iota(T.ones[:], [[0, 256]], 1, 0, ["ones"])
+    for a, c, tk in runs(FILL["g"]):
+        iota(T.win[:, a:c], [[0, c - a]], 0, 0, tk)
+    B8 = T.bob[:, 0:128:16]
+    for j, u in enumerate(FILL["s"]):
+        act(T.win[:, 1024 * u:1024 * u + 1024], T.zb[:], F.Copy, ["zb"], [("Wf", u)])
+        if j == 0:
+            act(T.eb[:], T.zb[:, 0:864], F.Copy, ["zb"], ["eb0"])
+        if j == 3:
+            act(EW(0), B8, F.Copy, ["bob", "eb0"], ["eb"])
+            act(T.nib[:], I, F.Copy, ["ib"], ["nib"], scale=-1.0)
+            act(T.bo[:], T.bob[:], F.Copy, ["bob"], ["bo"])
+    for u in FILL["y"]:
+        dma("y", T.win[:, 1024 * u:1024 * u + 1024], T.zb[:], ["zb"], [("Wf", u)], "fill")
+    ts(T.pint[:, 1:2], T.pint[:, 0:1], 15, None, A.bitwise_and, None, ["p0"], ["p1"])
+    ts(T.pint[:, 3:4], T.pint[:, 0:1], 4, 1, A.arith_shift_right, A.bitwise_and, ["p0"], ["p3"])
+    cp(T.pf[:, 1:4:2], T.pint[:, 1:4:2], ["p1", "p3"], ["pf"])
+    ms(T.xb[:, 0:16], 0.0, ["xpad"])
+    ts(T.pf[:, 4:5], T.pf[:, 1:2], 16.0, None, A.mult, None, ["pf"], ["pf4"])
+    ts(T.pf[:, 6:7], T.pf[:, 3:4], -1.0, 1.0, A.mult, A.add, ["pf"], ["pf6"])
+    ts(T.fl[:], T.flf[:], T.pf[:, 1:2], None, A.add, None, ["flf", "pf"], ["fl"])
+    ts(T.pt[:], T.colf[:], T.pf[:, 4:5], None, A.add, None, ["colf", "pf4"], ["pt"])
+    ts(T.sw[:], T.ib[:, 16:144], T.pf[:, 3:4], None, A.mult, None, ["ib", "pf"], ["sw"])
+    ts(T.sw2[:], T.ib[:, 112:240], T.pf[:, 6:7], None, A.mult, None, ["ib", "pf6"], ["sw2"])
+    ts(T.mask0[:], T.mask0[:], T.pf[:, 3:4], None, A.is_equal, None, ["mask0", "pf"], ["mask0"])
+    tt(T.sw[:], T.sw[:], T.sw2[:], A.add, ["sw", "sw2"], ["sw"])
+
+    def turn(src, stok, dst, dtok):
+        op("v", lambda: V.transpose(T.s7[:], src), [stok], ["s7"])
+        tt(T.s8[:], T.s7[:].indirect(T.fl[:]), T.mask0[:], A.mult, ["s7", "fl", "mask0"], ["s8"])
+        mm(T.pmm[:, 0:256], T.sw[:], T.s8[:], True, True, ["sw", "s8"], ["pmm"])
+        tt(T.s6[:], T.s7[:], T.mask0[:], A.mult, ["s7", "mask0"], ["s6"])
+        tt(dst, T.pmm[:, 0:256], T.s6[:], A.add, ["s6"], [dtok], ["pmm"])
+
+    def digits(src, tok):
+        ts(T.digi[:, 256:512], T.ni[:], 4, 15, A.arith_shift_right, A.bitwise_and, ["ni"], ["dg1"])
+        ts(T.digi[:, 512:768], T.ni[:], 15, None, A.bitwise_and, None, ["ni"], ["dg2"])
+        ts(T.h1[:], src, 1.0 / 256.0, 191.502, A.mult, A.add, [tok], ["h1"])
+        cp(T.dig[:, 256:768], T.digi[:, 256:768], ["dg1", "dg2"], ["dig"])
+        ts(T.dig[:, 0:256], T.h1[:], -192.0, None, A.add, None, ["h1"], ["dig0"])
+
+    def window(t):
+        for pl in range(3):
+            dma("y", T.win[0:128:16, 12288 * pl:12288 * pl + 4096], T.dig[:, 256 * pl:256 * pl + 256],
+                ["dig", "dig0"] + [("Wf", 12 * pl + j) for j in range(4)], [("W", 3 * pl), ("mst", pl)], "la%d" % t)
+        for pa, rg, pl, sh in CELLS:
+            dma("y", T.win[pa:128:16, 4096 * rg:4096 * rg + 4096 - sh], T.win[0:128:16, 12288 * pl + sh:12288 * pl + 4096],
+                [("mst", pl)] + [("Wf", 4 * rg + j) for j in range(4)], [("W", rg)], "lb%d" % t)
+
+    cp(T.nu[:], T.li[:], ["li"], ["nu"])
+    cp(T.s5[:], T.li[:].indirect(T.pt[:]), ["li", "pt"], ["s5"])
+    turn(T.s5[:], "s5", T.ni[:], "ni")
+    digits(T.ni[:], "ni")
+    for a, c, tk in runs(FILL["v1"]):
+        ms(T.win[:, a:c], 0.0, tk)
+    ms(T.dinit[:], 0.0, ["dinit"])
+    cp(T.th8[:], T.thi[:], ["thi"], ["th8"])
+    ts(T.dinit[:, 0:1], T.pf[:, 1:2], 0.0, 8192.0, A.is_equal, A.mult, ["pf"], ["dinit"])
+    mm(T.pq[:, 0:4], T.bo[:], T.th8[:], True, True, ["bo", "th8"], ["pq"])
+    for a, c, tk in runs(FILL["v2"]):
+        ms(T.win[:, a:c], 0.0, tk)
+    window(0)
+
+    def consts_v():
+        d, x, y, q = T.ct[:, 0:16], T.ct[:, 16:32], T.ct[:, 32:48], T.pf[:, 14:15]
+        x2, y2 = T.ct[:, 48:64], T.ct[:, 64:80]
+        ts(d, T.colf[:], T.pf[:, 1:2], None, A.subtract, None, ["colf", "pf"], ["cd"])
+        ts(q, T.pf[:, 1:2], -256.0, 3840.0, A.mult, A.add, ["pf"], ["cq"])
+        ts(T.m16[:], d, 0.0, None, A.is_equal, None, ["cd"], ["m16"])
+        ts(x, d, -256.0, -256.0, A.mult, A.add, ["cd"], ["cx"])
+        ts(y, d, 0.0, 16384.0, A.is_ge, A.mult, ["cd"], ["cy"])
+        ts(x2, d, 256.0, -256.0, A.mult, A.add, ["cd"], ["cx2"])
+        ts(y2, d, 0.0, 16384.0, A.is_le, A.mult, ["cd"], ["cy2"])
+        tt(T.cc[:, 0:16], x, y, A.max, ["cx", "cy"], ["cc0"])
+        tt(x2, x2, y2, A.add, ["cx2", "cy2"], ["cx2"])
+        ms(T.nb[:, 256:264], BIG, ["nb"])
+        ts(T.cc[:, 16:32], x2, q, None, A.min, None, ["cx2", "cq"], ["cc1"])
+        ts(T.c256[:], T.oneb[:], T.pf[:, 1:2], 256.0, A.mult, A.mult, ["oneb", "pf"], ["c256"])
+        cp(T.thf[:], T.pq[:, 0:4], [], ["thf"], ["pq"])
+
+    def consts_s():
+        act(T.pf[:, 7:8], T.m16[:, 1:2], ID, ["m16"], ["w0"], bias=T.m16[:, 2:3], scale=16.0)
+        act(T.pf[:, 9:10], T.m16[:, 3:4], ID, ["m16"], ["wb"], bias=T.m16[:, 4:5], scale=16.0)
+        act(T.pf[:, 8:9], T.m16[:, 0:1], ID, ["m16", "w0"], ["wa"], bias=T.pf[:, 7:8], scale=256.0)
+        act(EW(5), B8, F.Copy, ["bob", "wb", "eb0"], ["eb2"], scale=T.pf[:, 9:10])
+        act(EW(4), B8, F.Copy, ["bob", "wa", "eb0"], ["eb3"], scale=T.pf[:, 8:9])
+        act(T.cm75[:], T.oneb[:], F.Copy, ["oneb"], ["cm75"], scale=-7.5)
+        for w, c in ((1, -1.0), (2, 2.0), (3, -2.0)):
+            act(EW(w), B8, F.Copy, ["bob", "eb0"], [("ebw", w)], scale=c)
+        act(T.ib256[:], T.ib[:], F.Copy, ["ib"], ["ib256"], scale=256.0)
+        act(T.nib256[:], I, F.Copy, ["ib"], ["nib256"], scale=-256.0)
+
+    def consts_s2():
+        act(T.cm05[:], T.oneb[:], F.Copy, ["oneb"], ["cm05"], scale=-0.5)
+        act(T.cb[:], T.colf[:], ID, ["colf", "pf4"], ["cb"], bias=T.pf[:, 4:5], scale=256.0)
+        act(T.ym[:], T.zb[:, 0:512], ID, ["zb"], ["ym"], bias=1.0)
+        act(T.ym[:, 0:512:16], T.zb[:, 0:32], F.Copy, ["zb"], ["ym"])
+
+    def gather_x(eng, c0, c1):
+        out, src = T.xb[:, 16 + 16 * c0:16 + 16 * c1], T.tab[:].indirect(T.nu[:, c0:c1])
+        if eng == "v":
+            cp(out, src, ["tab", "nu"], xt(16 * c0, 16 * c1))
+        else:
+            act(out, src, F.Copy, ["tab", "nu"], xt(16 * c0, 16 * c1))
+
+    def cuts(a, c):
+        e = [a] + [j for j in range(32, 256, 32) if a + 8 < j < c - 8] + [c]
+        return list(zip(e[:-1], e[1:]))
+
+    def stage_x(t, before_v):
+        nat = t == 0
+        for a, c in cuts(S0[t], 256):
+            gather_x("s", a, c)
+        before_v()
+        for a, c in cuts(0, S0[t]):
+            gather_x("v", a, c)
+        mm(T.pd[:, 0:256], I, T.dinit[:], True, False, ["ib", "dinit"], ["pd"])
+        first = (S0[t] + 2 + 31) // 32
+        order = list(range(first, 8)) + list(range(first))
+        done, pend = set(), []
+
+        def ext(u, last):
+            if nat:
+                for h in range(2):
+                    c = 2 * u + h
+                    mm(T.pd[:, 0:256], E(0, c), T.ga[:, 256 * c:256 * c + 256], False, last and h == 1, ["eb", ("ga", u)], ["pd"])
+            else:
+                for c in range(16):
+                    mm(T.pd[:, 64 * u:64 * u + 64], E(0, c), T.ga[:, 1024 * u + c:1024 * u + 1024:16], False, last and c == 15,
+                       ["eb", ("ga", 2 * u), ("ga", 2 * u + 1)], ["pd"])
+        for j, u in enumerate(order):
+            bn = "pb%d" % (j & 1)
+            pb, c0 = T[bn], 512 * u
+            mm(pb[:], I, T.xb[:, 16 + c0:16 + c0 + 512], True, False, ["ib"] + xt(c0, c0 + 512), [bn])
+            if nat:
+                mm(pb[:], T.nib[:], T.xb[:, 15 + c0:15 + c0 + 512], False, True, ["nib", "xpad"] + xt(max(c0 - 1, 0), c0 + 511), [bn])
+            elif u == 0:
+                mm(pb[:, 16:512], T.nib[:], T.xb[:, 16:512], False, False, ["nib"] + xt(0, 496), [bn])
+                mm(pb[:, 0:16], T.nib[:], T.xb[:, 16 + 4079:16 + 4095], False, True, ["nib"] + xt(4079, 4095), [bn])
+            else:
+                mm(pb[:], T.nib[:], T.xb[:, c0:c0 + 512], False, True, ["nib"] + xt(c0 - 16, c0 + 496), [bn])
+            for e in pend:
+                ext(e, False)
+            del pend[:]
+            act(T.ga[:, c0:c0 + 512], pb[:], F.Abs, [], [("ga", u)], [bn])
+            done.add(u)
+            if nat:
+                pend.append(u)
+            elif (u ^ 1) in done:
+                pend.append(u // 2)
+        for e in pend:
+            ext(e, e == pend[-1])
+
+    Y = T.tmp[:, 15:4096:16]
+    TY = [("tmp", c) for c in range(16)]
+
+    def yscan(c):
+        scan(T.tmp[:, 256 * c:256 * c + 256], T.ym[:, 0:256], T.xb[:, 16 + c:4112:16], 0.0, A.mult, A.max, ["ym"] + xt(0, 4096), [("tmp", c)])
+
+    def ztile():
+        for h in range(2):
+            act(T.z2[:, 256 * h:256 * h + 256], T.zc[:].indirect(T.pt[:]), F.Copy, ["zc", "pt"], [("z2", h)])
+    Z2 = [("z2", 0), ("z2", 1)]
+
+    def blocks_a():
+        for b in range(16):
+            mm(T.pmm[:, 256:272], E(0, b), T.tmp[:, 15 + 16 * b:4096:256], b == 0, b == 15, ["eb"] + TY, ["pmm"])
+        mm(T.pb0[:, 0:256], I, Y, True, False, ["ib"] + TY, ["pb0"])
+        mm(T.pb0[:, 0:256], T.nib[:], T.zc[:], False, True, ["nib", "zc"], ["pb0"])
+        mm(T.pb0[:, 256:512], I, Y, True, False, ["ib"] + TY, ["pb0"])
+        mm(T.pb0[:, 256:512], I, T.zc[:], False, False, ["ib", "zc"], ["pb0"])
+        mm(T.pb0[:, 256:512], I, T.cm05[:], False, True, ["ib", "cm05"], ["pb0"])
+        act(T.zs[:], T.pb0[:, 256:512], ID, [], ["zs"], ["pb0"], bias=M1, scale=0.5)
+        act(T.zc[:], T.pb0[:, 0:256], F.Abs, [], ["zc"], ["pb0"])
+        act(T.avg[:], T.zs[:], ID, ["zs"], ["avg"], bias=-M1)
+
+    def blocks_b():
+        cp(T.ui[:, 0:16], T.pmm[:, 256:272], [], ["ui0"], ["pmm"])
+        ts(T.ui[:, 16:32], T.ui[:, 0:16], 15, None, A.bitwise_and, None, ["ui0"], ["ui1"])
+        tt(T.uf[:], T.ui[:, 16:32], T.cb[:], A.add, ["ui1", "cb"], ["uf"])
+        cp(T.cu[:], T.uf[:], ["uf"], ["cu"])
+
+    def periods(t):
+        J, b2, s2, tp, ln = T.pv0[:, 0:256], T.pv0[:, 256:512], T.pv1[:, 0:256], T.pv1[:, 256:512], T.pmm[:, 0:256]
+        sp, kk = T.pq[:, 0:256], T.pb1[:, 0:256]
+        nb = T.nb[:, 0:256]
+        thr = T.thf[:, 0:1] if t == 0 else T.thr[:, 0:1]
+        ts(nb, T.pd[:, 0:256], thr, BIG, A.is_le, A.mult, ["thr", "thf"], ["nb"], ["pd"])
+        mm(kk, I, T.colb[:], True, False, ["ib", "colb"], ["pb1"])
+        mm(kk, I, T.c256[:], False, True, ["ib", "c256"], ["pb1"])
+        if t > 0:
+            blocks_a()
+        else:
+            consts_s()
+        scan(T.h1[:], T.oneb[:], nb, 8192.0, A.add, A.min, ["nb", "oneb"], ["h1"])
+        scan(T.h2[:, ::-1], T.oneb[:], T.nb[:, 255::-1], 8192.0, A.add, A.min, ["nb", "oneb"], ["h2"])
+        ts(T.r12[:, 0:16], T.m16[:], T.h1[:, 255:256], None, A.mult, None, ["m16", "h1"], ["r1"])
+        ts(T.r12[:, 16:32], T.m16[:], T.h2[:, 0:1], None, A.mult, None, ["m16", "h2"], ["r2"])
+        mm(T.pd[:, 256:288], I, T.cc[:], True, False, ["ib", "cc0", "cc1"], ["pd"])
+        mm(T.pd[:, 256:272], T.lt[:], T.r12[:, 0:16], False, False, ["lt", "r1"], ["pd"])
+        mm(T.pd[:, 272:288], T.ut[:], T.r12[:, 16:32], False, True, ["ut", "r2"], ["pd"])
+        red(T.car[:, 0:1], T.pd[:, 256:272], A.min, [], ["c0"], ["pd"])
+        red(T.car[:, 1:2], T.pd[:, 272:288], A.min, [], ["c1"], ["pd"])
+        scan(T.s1[:], T.ones[:], nb, T.car[:, 0:1], A.add, A.min, ["nb", "ones", "c0"], ["s1"])
+        act(T.s7[:], T.s1[:], ID, ["s1"], ["s7"], bias=3.0, scale=2.0)
+        scan(T.pv0[:, 255::-1], T.nb[:, 256:0:-1], T.ones[:], T.car[:, 1:2], A.min, A.add, ["nb", "ones", "c1"], ["J"], ["pv0"])
+        tt(ln, T.s1[:], J, A.add, ["J", "s1"], ["ln"], ["pv0", "pmm"])
+        tt(T.s3[:], T.s7[:], J, A.subtract, ["s7", "J"], ["s3"], ["pv0"])
+        act(T.s4[:], T.s3[:], F.Relu, ["s3"], ["s4"])
+        act(T.pb0[:, 0:256], T.s4[:], F.Relu, ["s4"], [], ["pb0"], bias=12288.0, scale=-4096.0)
+        tt(T.s2[:], kk, T.s1[:], A.subtract, ["s1"], ["s2"], ["pb1"])
+        tt(T.h1[:], T.s3[:], ln, A.subtract, ["s3", "ln"], ["h1"], ["pmm"])
+        act(sp, ln, F.Relu, [], [], ["pmm", "pq"], bias=32770.0, scale=-16385.0)
+        ztile()
+        ts(T.h2[:], T.h1[:], -1.0, -1.0, A.add, A.max, ["h1"], ["h2"])
+        ts(T.h1[:], T.h2[:], 2.0, 4096.0, A.min, A.mult, ["h2"], ["h1"])
+        tt(T.s6[:], T.h1[:], T.pb0[:, 0:256], A.subtract, ["h1"], ["s6"], ["pb0"])
+        tt(s2, T.s2[:], sp, A.add, ["s2"], ["s2p"], ["pq", "pv1"])
+        tt(T.s1[:], s2, T.s6[:], A.add, ["s2p", "s6"], ["s1"], ["pv1"])
+        ts(T.pm[:], T.s6[:], 1.0 / 12288.0, None, A.mult, None, ["s6"], ["pm"])
+        ts(T.ob[:], T.s1[:].indirect(T.pt[:]), 16384.0, None, A.add, None, ["s1", "pt"], ["ob"])
+        tt(tp, T.pm[:], ln, A.mult, ["pm", "ln"], ["tp"], ["pmm", "pv1"])
+        tt(tp, T.s3[:], tp, A.subtract, ["s3", "tp"], ["tp"], ["pv1"])
+        tt(T.s5[:], T.s1[:], tp, A.add, ["s1", "tp"], ["s5"], ["pv1"])
+        ts(T.oa[:], T.s5[:].indirect(T.pt[:]), 16381.0, None, A.add, None, ["s5", "pt"], ["oa"])
+
+    def names_p(t):
+        for q in range(4):
+            act(T.gb[:, 1024 * q:1024 * q + 1024], T.win[:].indirect(T.ob[:, 64 * q:64 * q + 64]), F.Copy, WT + ["ob"], [("gb", q)])
+        for u in range(8):
+            out, src = T.ga[:, 512 * u:512 * u + 512], T.win[:].indirect(T.oa[:, 32 * u:32 * u + 32])
+            if u < NVA[t]:
+                cp(out, src, WT + ["oa"], [("ga", u)])
+            else:
+                act(out, src, F.Copy, WT + ["oa"], [("ga", u)])
+        if t > 0:
+            blocks_b()
+        mm(T.pp[:, 0:256], I, T.cm75[:], True, False, ["ib", "cm75"], ["pp"])
+        for s in ("b0", "b1", "a0", "b2", "a1", "b3", "a2", "a3"):
+            q = int(s[1])
+            for c in range(16):
+                if s[0] == "b":
+                    mm(T.pp[:, 64 * q:64 * q + 64], E(5, c), T.gb[:, 1024 * q + c:1024 * q + 1024:16], False, False, ["eb2", ("gb", q)], ["pp"])
+                else:
+                    mm(T.pp[:, 64 * q:64 * q + 64], E(4, c), T.ga[:, 1024 * q + c:1024 * q + 1024:16], False, s == "a3" and c == 15,
+                       ["eb3", ("ga", 2 * q), ("ga", 2 * q + 1)], ["pp"])
+        hi, lo, P = T["hi%d" % t], T["lo%d" % t], T.pp[:, 0:256]
+        ts(T.r16[:], P, M16, M16, A.add, A.subtract, [], ["r16"], ["pp"])
+        act(hi[:], T.r16[:], ID, ["r16"], [("hi", t)], bias=191.53125, scale=1.0 / 256.0)
+        tt(lo[:], P, T.r16[:], A.subtract, ["r16"], [("lo", t)], ["pp"])
+        ts(T.pu[:], P, 7.5, None, A.add, None, [], ["pu"], ["pp"])
+        if t > 0:
+            cp(T.tab[:].indirect(T.cu[:]), T.avg[:], ["avg", "cu"], ["tab"])
+        d1, d2 = T.cores[(rank + 1) % n], T.cores[(rank + 2) % n]
+        e1, e2 = topo.engines(core, d1)[0::2], topo.engines(core, d2)[1::2]
+        trs = []
+        for d, es, src, dst, sm in ((d1, e1, hi, "hin%d", "ah%d"), (d2, e2, lo, "lin%d", "al%d")):
+            rid, pid = topo.addr(d)[0:2]
+            trs.append(RemoteDMATransfer(dst_ids=[DstId(rid=rid, pnc=pid)], dma_engine_mask=sum(1 << e for e in es),
+                                         remote_sem=T.sem[sm % t], src=src[:], dst=T[dst % t][:]))
+        op("r", lambda: g.remote_dma_fused(trs, local_sem=T.sem["loc%d" % t]), [("hi", t), ("lo", t)], [], sem="loc%d" % t, inc=len(e1) + len(e2))
+        p1, p2 = T.cores[(rank - 1) % n], T.cores[(rank - 2) % n]
+        op("x", None, [], [("hin", t)], sem="ah%d" % t, inc=len(topo.engines(p1, core)[0::2]))
+        op("x", None, [], [("lin", t)], sem="al%d" % t, inc=len(topo.engines(p2, core)[1::2]))
+
+    def dist(off, otok, dn, an, sg, first, last, mid):
+        d, a = T[dn], T[an]
+        wa, wr, wd = (0, 2, 1) if sg > 0 else (1, 3, 0)
+        if first:
+            mm(T.pq[:, 0:256], I, T.zb[:, 0:256], True, False, ["ib", "zb"], ["pq"])
+        chunks, mode, ends = [], [], {}
+        for md, k in MODES:
+            chunks.append((md, len(mode), len(mode) + k))
+            mode += [md] * k
+            ends[len(mode) - 1] = k
+        for u in range(8):
+            md, c0 = mode[u], 512 * u
+            if md == "SS":
+                act(d[:, c0:c0 + 512], T.tab[:].indirect(off[:, 32 * u:32 * u + 32]), F.Copy, ["tab", otok], [(dn, u)])
+        for u in range(8):
+            md, c0 = mode[u], 512 * u
+            if md == "SS":
+                bn = "pb%d" % (u & 1)
+                mm(T[bn][:], I, d[:, c0:c0 + 512], True, False, ["ib", (dn, u)], [bn])
+                mm(T[bn][:], T.nib[:], T.z2[:], False, True, ["nib"] + Z2, [bn])
+                act(a[:, c0:c0 + 512], T[bn][:], F.Abs, [], [(an, u)], [bn])
+            else:
+                tt(d[:, c0:c0 + 512], T.tab[:].indirect(off[:, 32 * u:32 * u + 32]), T.z2[:], A.subtract, ["tab", otok] + Z2, [(dn, u)])
+                if md == "VS":
+                    act(a[:, c0:c0 + 512], d[:, c0:c0 + 512], F.Abs, [(dn, u)], [(an, u)])
+                elif u in ends:
+                    u0 = u + 1 - ends[u]
+                    ts(a[:, 512 * u0:c0 + 512], d[:, 512 * u0:c0 + 512], 0.0, None, A.max, None, [(dn, j) for j in range(u0, u + 1)],
+                       [(an, j) for j in range(u0, u + 1)])
+        todo = []
+        for x in ORDER:
+            md, u0, u1 = chunks[int(x[1])]
+            todo.append((u0, u1, d, dn, wd) if x[0] == "d" else (u0, u1, a, an, wr if md == "VV" else wa))
+        for j, (u0, u1, buf, nm, w) in enumerate(todo):
+            if j == len(todo) - 2 and mid is not None:
+                mid()
+            for c in range(16):
+                mm(T.pq[:, 32 * u0:32 * u1], E(w, c), buf[:, 512 * u0 + c:512 * u1:16], False,
+                   last and j == len(todo) - 1 and c == 15, ["eb", ("ebw", w)] + [(nm, u) for u in range(u0, u1)], ["pq"])
+
+    def choice(t):
+        hi, lo, hin, lin = T["hi%d" % t], T["lo%d" % t], T["hin%d" % t], T["lin%d" % t]
+        Mp, Dp = T.pmm[:, 0:256], T.pd[:, 0:256]
+        mm(Mp, I, T.r16[:], True, False, ["ib", "r16"], ["pmm"])
+        mm(Mp, T.nib256[:], hi[:], False, False, ["nib256", ("hi", t)], ["pmm"])
+        mm(Dp, T.nib[:], lo[:], True, False, ["nib", ("lo", t)], ["pd"])
+        mm(Dp, T.nib256[:], hi[:], False, False, ["nib256", ("hi", t)], ["pd"])
+
+        def mid():
+            mm(Mp, T.ib256[:, 112:240], hin[:], False, False, ["ib256", ("hin", t)], ["pmm"])
+            mm(Mp, T.ib[:, 96:224], lin[:], False, True, ["ib", ("lin", t)], ["pmm"])
+            mm(Dp, T.ib256[:, 112:240], hin[:], False, False, ["ib256", ("hin", t)], ["pd"])
+            mm(Dp, T.ib[:, 96:224], lin[:], False, True, ["ib", ("lin", t)], ["pd"])
+        dist(T.pu, "pu", "d3", "a3b", -1, True, False, mid)
+        if t == 0:
+            consts_s2()
+        ts(T.mu[:], Mp, 7.5, None, A.add, None, [], ["mu"], ["pmm"])
+        dist(T.mu, "mu", "d4", "a4b", 1, False, True, None)
+        ts(T.s1[:], T.pq[:, 0:256], 0.0, None, A.is_lt, None, [], ["s1"], ["pq"])
+        tt(T.s2[:], T.s1[:], Dp, A.mult, ["s1"], ["s2"], ["pd"])
+        tt(T.s3[:], T.s2[:], T.pp[:, 0:256], A.add, ["s2"], ["s3"], ["pp"])
+
+    stage_x(0, consts_v)
+    for t in range(3):
+        periods(t)
+        names_p(t)
+        choice(t)
+        if t < 2:
+            act(T.s4[:], T.s1[:], ID, ["s1"], ["s4", "acc"], acc=T.acc[:, 0:1])
+            ts(T.nu[:], T.s3[:].indirect(T.pt[:]), 7.5, None, A.add, None, ["s3", "pt"], ["nu"])
+            mm(T.pd[:, 336:337], T.bo[:], T.acc[:, 0:1], True, True, ["bo", "acc"], ["pd"])
+
+            def prep(t=t):
+                cp(T.ai[:, 0:1], T.pd[:, 336:337], [], ["ai0"], ["pd"])
+                cp(T.ni[:], T.nu[:], ["nu"], ["ni"])
+                ts(T.ai[:, 1:2], T.ai[:, 0:1], 31, None, A.bitwise_and, None, ["ai0"], ["ai1"])
+                digits(T.nu[:], "nu")
+                window(t + 1)
+                tt(T.thr[:, 0:1], T.ai[:, 1:2], T.thf[:, t + 1:t + 2], A.add, ["ai1", "thf"], ["thr"])
+            stage_x(t + 1, prep)
+            for c in range(16):
+                yscan(c)
+    ts(T.s5[:], T.s3[:].indirect(T.pt[:]), 7.5, None, A.add, None, ["s3", "pt"], ["s5"])
+    turn(T.s5[:], "s5", T.s4[:], "s4")
+    cp(T.nu[:], T.s4[:].indirect(T.pt[:]), ["s4", "pt"], ["nu"])
+    parts = [("s", a, c) for a, c in cuts(FINV, 256)] + [("v", a, c) for a, c in cuts(0, FINV)]
+    for e, a, c in parts:
+        gather_x(e, a, c)
+    nv = FINV // 32
+    seq = []
+    for j in range(8):
+        seq += ([j] if j < nv else []) + ([nv + j] if nv + j < 8 else [])
+    for u in seq:
+        dma("y", T.xy[:, 512 * u:512 * u + 512], T.xb[:, 16 + 512 * u:16 + 512 * u + 512], xt(512 * u, 512 * u + 512), [], "oxy")
+    for u in range(8):
+        scan(T.tmp[:, 512 * u:512 * u + 512], T.ym[:], T.xb[:, 16 + 512 * u:16 + 512 * u + 512], 0.0, A.mult, A.max,
+             ["ym"] + xt(512 * u, 512 * u + 512), [("tmp", 2 * u), ("tmp", 2 * u + 1)])
+        if u == 5:
+            cp(T.lyf[:], T.s4[:].indirect(T.pt[:]), ["s4", "pt"], ["lyf"])
+            dma("y", T.ly[:], T.lyf[:], ["lyf"], [], "oly")
+    mm(T.pb0[:, 0:256], T.nib[:], T.zc[:], True, False, ["nib", "zc"], ["pb0"])
+    mm(T.pb0[:, 0:256], I, Y, False, True, ["ib"] + TY, ["pb0"])
+    act(T.zd[:], T.pb0[:, 0:256], F.Abs, [], ["zd"], ["pb0"])
+    dma("s", T.zy[:], T.zd[:], ["zd"], [], "ozy")
+
+    queue = {"v": V, "s": S, "t": PE, "g": g, "r": g, "y": g.sync}
+    esem = {"v": "cv", "s": "cs", "t": "ct", "g": "cg"}
+    total, need = {}, set()
+    for o in ops:
+        if o["sem"] is not None:
+            total[o["sem"]] = total.get(o["sem"], 0) + o["inc"]
+        best = {}
+        for d in o["deps"]:
+            if ops[d]["sem"] is None:
+                best[ops[d]["eng"]] = max(best.get(ops[d]["eng"], -1), d)
+        o["deps"] = [d for d in o["deps"] if ops[d]["sem"] is not None] + list(best.values())
+        need.update(best.values())
+    cnt, seen = {}, {}
+    for i, o in enumerate(ops):
+        if o["eng"] == "x":
+            continue
+        qn = "g" if o["eng"] == "r" else o["eng"]
+        q = queue[o["eng"]]
+        for d in o["deps"]:
+            p = ops[d]
+            sm, val = (p["sem"], total[p["sem"]]) if p["sem"] is not None else (esem[p["eng"]], p["n"])
+            if seen.get((qn, sm), 0) < val:
+                q.wait_ge(T.sem[sm], val)
+                seen[(qn, sm)] = val
+        ins = o["fn"]()
+        if o["eng"] == "r":
+            continue
+        if o["sem"] is not None:
+            ins.then_inc(T.sem[o["sem"]], 16)
+        elif i in need:
+            sm = esem[o["eng"]]
+            cnt[sm] = cnt.get(sm, 0) + 1
+            o["n"] = cnt[sm]
+            ins.then_inc(T.sem[sm], 1)
+    total.update(cnt)
+    for sm, val in total.items():
+        g.wait_ge(T.sem[sm], val)

@@ -1,10 +1,13 @@
 from concourse.bass import DstId, RemoteDMATransfer
 from concourse.mybir import AluOpType as A, AxisListType, ActivationFunctionType as F
 
-WIN = 8 * 4096 + 16
-BIG = 32768.0
+RG = 4096
+WIN = 10 * RG
+XO, GO = 6 * RG, 8 * RG
+BIG = 65536.0
 M16 = 201326592.0
 M1 = 12582912.0
+LOW = 1048576.0
 f32, bf, i32, u16 = "float32", "bfloat16", "int32", "uint16"
 
 
@@ -13,42 +16,97 @@ def sb(n, d):
 
 
 SCRATCH = {
-    "win": sb(WIN, bf), "tab": sb(4096, bf), "xb": sb(4112, bf), "ga": sb(4096, bf), "gb": sb(4096, bf),
-    "d3": sb(4096, bf), "a3b": sb(4096, bf), "d4": sb(4096, bf), "a4b": sb(4096, bf), "tmp": sb(4096, bf),
-    "zb": sb(1024, bf), "ym": sb(512, bf), "li": sb(256, i32), "thi": sb(4, i32), "th8": sb(4, f32), "thf": sb(4, f32),
-    "zc": sb(256, bf), "z2": sb(512, bf), "zd": sb(256, bf), "zs": sb(256, f32), "avg": sb(256, bf),
-    "pint": sb(4, i32), "pf": sb(16, f32), "colf": sb(16, f32), "colb": sb(256, bf), "c256": sb(256, bf), "pt": sb(16, u16), "fl": sb(16, u16),
-    "flf": sb(16, f32), "cb": sb(16, f32), "ib": sb(256, bf), "ib256": sb(256, bf), "nib": sb(128, bf), "nib256": sb(128, bf),
-    "sw": sb(128, f32), "sw2": sb(128, f32), "eb": sb(6 * 144, bf), "bo": sb(128, f32), "bob": sb(128, bf), "lt": sb(128, bf), "ut": sb(128, bf),
-    "m16": sb(16, f32), "cc": sb(32, bf), "ct": sb(80, f32), "ones": sb(256, f32),
-    "cm75": sb(256, bf), "cm05": sb(256, bf), "dinit": sb(256, bf), "mask0": sb(256, f32), "oneb": sb(256, bf),
+    "win": sb(WIN, bf), "tab": sb(4096, bf), "ga": sb(4096, bf), "gb": sb(4096, bf),
+    "d3": sb(4096, bf), "a3": sb(4096, bf), "d4": sb(4096, bf), "a4": sb(4096, bf), "tmp": sb(4096, bf),
+    "zb": sb(1024, bf), "ym8": sb(512, bf), "ym16": sb(512, bf), "li": sb(256, i32), "thi": sb(8, i32), "th8": sb(8, f32),
+    "thp": sb(8, f32), "thb": sb(8, f32), "zc": sb(256, bf), "z2": sb(512, bf), "zd": sb(256, bf), "zs": sb(256, f32), "avg": sb(256, bf),
+    "pint": sb(8, i32), "pf": sb(32, f32), "colf": sb(16, f32), "dupf": sb(32, f32), "selff": sb(16, f32), "tcol": sb(72, f32),
+    "pt": sb(16, u16), "pt2": sb(16, u16), "dup": sb(32, u16), "selc": sb(16, u16), "sell": sb(16, u16),
+    "cb": sb(16, f32), "ib": sb(256, bf), "ib256": sb(256, bf), "nib": sb(128, bf), "nib256": sb(128, bf), "ib2": sb(128, bf),
+    "ibh": sb(128, bf), "ib16": sb(128, bf), "nib16": sb(128, bf),
+    "eb": sb(7 * 144, bf), "bo": sb(128, f32), "bob": sb(128, bf), "oneb": sb(256, bf),
+    "c2040": sb(128, bf), "cm05": sb(256, bf), "dinit": sb(304, bf), "kt": sb(256, f32), "jj": sb(256, f32),
+    "three": sb(288, bf), "zadd": sb(288, bf), "cd": sb(72, f32), "ce": sb(72, f32), "nb": sb(320, bf), "hb": sb(576, bf),
+    "ht": sb(72, bf), "car": sb(72, f32), "dsb": sb(256, f32),
     "nu": sb(256, u16), "pu": sb(256, u16), "mu": sb(256, u16), "oa": sb(256, u16), "ob": sb(256, u16), "cu": sb(16, u16),
-    "ni": sb(256, i32), "digi": sb(768, i32), "dig": sb(768, bf),
-    "nb": sb(264, bf), "h1": sb(256, bf), "h2": sb(256, bf), "s1": sb(256, f32), "s2": sb(256, f32), "s3": sb(256, f32),
-    "s4": sb(256, f32), "s5": sb(256, f32), "s6": sb(256, f32), "s7": sb(256, f32), "s8": sb(256, f32), "pm": sb(256, i32),
-    "r12": sb(32, bf), "car": sb(4, f32), "thr": sb(4, f32), "acc": sb(4, f32), "ai": sb(4, i32), "ui": sb(32, i32), "uf": sb(16, f32),
-    "r16": sb(256, bf), "lyf": sb(256, f32),
-    "pb0": ("psum", [128, 512], f32), "pb1": ("psum", [128, 512], f32), "pd": ("psum", [128, 512], f32), "pp": ("psum", [128, 512], f32),
-    "pq": ("psum", [128, 512], f32), "pmm": ("psum", [128, 512], f32), "pv0": ("psum", [128, 512], f32), "pv1": ("psum", [128, 512], f32),
+    "dig": sb(768, bf), "r32": sb(256, bf), "hh": sb(256, bf), "sg": sb(256, bf),
+    "f2": sb(256, f32), "uu": sb(256, f32), "sp": sb(256, f32), "vv": sb(256, f32), "bu": sb(256, bf), "bv": sb(256, bf),
+    "s1": sb(256, f32), "s2": sb(256, f32), "s3": sb(256, f32), "s4": sb(256, f32), "w1": sb(512, f32), "w2": sb(512, f32),
+    "acc": sb(16, f32), "ai": sb(16, i32), "ui": sb(32, i32), "uf": sb(16, f32), "r16": sb(256, bf), "lyf": sb(256, f32),
+    "hi": sb(768, bf), "lo": sb(768, bf), "hin": sb(768, bf), "lin": sb(768, bf),
 }
+BANKS = ("pb0", "pb1", "pb2", "pb3", "px0", "px1", "pq0", "pq1")
+for _n in BANKS:
+    SCRATCH[_n] = ("psum", [128, 512], f32)
+SEMAPHORES = ["cv", "cs", "ct", "cg", "ldx", "ldl", "ldz", "ldt", "oly", "ozy", "oxy", "loc"] + ["fill%d" % _j for _j in range(8)]
 for _t in range(3):
-    for _n in ("hi", "lo", "hin", "lin"):
-        SCRATCH["%s%d" % (_n, _t)] = sb(256, bf)
-SEMAPHORES = ["cv", "cs", "ct", "cg", "ldx", "ldl", "ldz", "ldt", "fill", "oly", "ozy", "oxy"]
-for _t in range(3):
-    SEMAPHORES += ["la%d" % _t, "lb%d" % _t, "ah%d" % _t, "al%d" % _t, "loc%d" % _t]
+    SEMAPHORES += ["la%d%d" % (_t, _p) for _p in range(3)] + ["lb%d" % _t] + ["%s%d%d" % (_n, _t, _h) for _n in ("ah", "al") for _h in range(2)]
 
-CELLS = [(3, 2, 1, 0), (3, 5, 2, 0), (4, 1, 1, 0), (4, 2, 1, 1), (4, 4, 2, 0), (4, 5, 2, 1),
-         (0, 1, 0, 0), (0, 2, 0, 0), (0, 4, 1, 0), (0, 5, 1, 0), (0, 7, 0, 0),
-         (1, 0, 0, 1), (1, 1, 0, 1), (1, 3, 1, 1), (1, 4, 1, 1), (1, 6, 2, 1), (1, 7, 1, 0),
-         (2, 0, 0, 2), (2, 3, 1, 2), (2, 6, 2, 2), (2, 7, 2, 0)]
-FILL = {"s": [0, 1, 2, 3, 12], "v1": [13, 14, 15, 24, 25, 26, 27], "v2": [4, 5, 6, 7, 29, 30, 31], "g": [20, 21, 22, 23, 28],
-        "y": [8, 9, 10, 11, 16, 17, 18, 19]}
-S0 = (62, 150, 150)
-NVA = (7, 7, 7)
-MODES = (("SS", 2), ("VV", 2), ("VS", 2), ("VS", 2))
-ORDER = ("d1", "a0", "a1", "a2", "a3")
-FINV = 96
+MASTER = (0, 3, 9)
+CELLS = [(3, 1, 1, 0), (4, 2, 1, 0), (3, 2, 1, 1), (3, 5, 2, 0), (4, 7, 2, 0), (3, 7, 2, 1),
+         (1, 0, 0, 1), (2, 0, 0, 2), (0, 1, 0, 0), (1, 1, 0, 1), (0, 2, 0, 0), (0, 4, 0, 0), (1, 4, 1, 0), (2, 4, 2, 0),
+         (1, 3, 1, 1), (2, 3, 1, 2), (0, 5, 1, 0), (1, 5, 1, 1), (0, 7, 1, 0), (1, 9, 2, 1), (2, 9, 2, 2)]
+FILLED, FILLER, FIRST = (9, 0, 3, 1, 2, 4, 5, 7), "ssss" "yyyy" "gggg" "yyyy" "vvvv" "ssss" "gggv" "vvvs", 4
+DP = (("VS", "VS", "VS", "VS"), ("SS", "SS", "VS", "VS"))
+DM = (("VS", "VS", "VS", "VS"), ("SS", "VS", "VV", "VV"))
+DORDER = ((0, 0), (0, 1), (1, 0), (1, 1))
+PG = ({"b": "sSsSsSsS", "a": "vVvVvVvV"}, {"b": "sSsSsSsS", "a": "vVvVsSsS"})
+X0, XG, XL = "svvsvvsv", "svvsvvsv", "svsvsvsv"
+XORDER, DIGITS, DX = (7, 0, 1, 2, 3, 4, 5, 6), 3, "tttttttt"
+
+
+CYCLE, PECYCLE, GATHER, SCATTER, FIXV, FIXS, WAKE = 0.00083, 0.00042, 1.56, 3.5, 0.03, 0.06, 0.19
+DMA0, DMARATE, TRAVEL, EARLY, SWEEPS = 1.6, 250.0, 4.0, 0.0, 3
+INFO, PLAN = [], []
+
+
+def arrange(ops):
+    group = {}
+    for i, o in enumerate(ops):
+        if o["sem"] is not None:
+            group.setdefault(o["sem"], []).append(i)
+    pred = [set(o["after"]) | {j for d in o["deps"] for j in (group[ops[d]["sem"]] if ops[d]["sem"] is not None else [d])} for o in ops]
+    way = [0.0] * len(ops)
+    for i in range(len(ops) - 1, -1, -1):
+        o = ops[i]
+        way[i] += min(c for _, c in o["alt"].values()) + o["late"] + 1e-6 + o.get("early", 0.0)
+        for d in pred[i]:
+            way[d] = max(way[d], way[i] + (0 if d in o["after"] else WAKE))
+    before = [[(d, -ops[d]["late"] if d in o["after"] else WAKE) for d in pred[i]] for i, o in enumerate(ops)]
+    behind = [[] for _ in ops]
+    for i, lst in enumerate(before):
+        for d, gap in lst:
+            behind[d].append((i, gap))
+
+    def sweep(order, links, back):
+        busy, start, end, eng = {}, {}, {}, {}
+        for i in order:
+            o, best = ops[i], None
+            ready = max([end[d] + gap for d, gap in links[i]] + [0.0]) + (o["late"] if back else 0.0)
+            for e, (_, c) in o["alt"].items():
+                at, line = ready, busy.setdefault(e, [])
+                k = len(line)
+                while k > 0 and line[k - 1][1] > ready:
+                    k -= 1
+                while k < len(line) and line[k][0] < at + c - 1e-9:
+                    at = max(at, line[k][1])
+                    k += 1
+                if best is None or at + c < best[0]:
+                    best = (at + c, at, e, k)
+            busy[best[2]].insert(best[3], (best[1], best[0]))
+            eng[i], start[i], end[i] = best[2], best[1], best[0] + (0.0 if back else o["late"]) + 1e-6
+        return max(end.values()), start, end, eng
+
+    best = now = sweep(range(len(ops)), before, False)
+    INFO.append(best[0])
+    for _ in range(SWEEPS):
+        rev = sweep(sorted(range(len(ops)), key=lambda j: (-now[1][j], -j)), behind, True)
+        now = sweep(sorted(range(len(ops)), key=lambda j: (-rev[1][j], j)), before, False)
+        best = min(best, now, key=lambda x: x[0])
+        INFO.append(now[0])
+    for i, o in enumerate(ops):
+        o["eng"] = best[3][i]
+    return sorted(range(len(ops)), key=lambda j: (best[1][j], j))
 
 
 def rank_program(g, core, T, topo):
@@ -56,511 +114,613 @@ def rank_program(g, core, T, topo):
     if rank is None:
         return
     n = len(T.cores)
-    ops = []
-    lastw, readers, bank = {}, {}, {}
+    ops, marks, bank, sent = [], {}, {}, []
 
-    def op(eng, fn, r=(), w=(), b=(), sem=None, inc=16):
-        me = len(ops)
-        deps = set()
-        for t in r:
-            if t in lastw:
-                deps.add(lastw[t])
-        for t in w:
-            if t in lastw:
-                deps.add(lastw[t])
-            deps.update(readers.get(t, ()))
-        for t in b:
-            for e, i in bank.setdefault(t, {}).items():
-                if e != eng:
-                    deps.add(i)
-            bank[t][eng] = me
-        for t in r:
-            readers.setdefault(t, []).append(me)
-        for t in w:
-            lastw[t] = me
-            readers[t] = []
-        deps = [d for d in deps if not (eng == "t" and ops[d]["eng"] == "t") and not (sem is not None and ops[d]["sem"] == sem)]
-        ops.append({"eng": eng, "fn": fn, "deps": deps, "sem": sem, "inc": inc})
+    def v(name, a=None, b=None, s=None, p=None):
+        r = range(*slice(a, b, s).indices(SCRATCH[name][1][1]))
+        lo, hi = min(r[0], r[-1]), max(r[0], r[-1]) + 1
+        return (T[name][slice(None) if p is None else p, slice(a, b, s)], [(name, lo // 8 * 8, -(-hi // 8) * 8, p and p.start)], len(r), SCRATCH[name][2])
+
+    def ix(w, o):
+        return (w[0].indirect(o[0]), w[1] + o[1], 16 * o[2], "list")
+
+    def op(alt, r=(), w=(), sem=None, inc=16, late=0.0, after=()):
+        me, deps, after = len(ops), set(), list(after)
+        eng = list(alt)[0] if len(alt) == 1 else "f%d" % me
+        rs = [x for a in r if isinstance(a, tuple) for x in a[1]]
+        ws = [x for a in w for x in a[1]]
+        for lst, wr in ((rs, False), (ws, True)):
+            for nm, lo, hi, row in lst:
+                for m in marks.setdefault(nm, []):
+                    if m[0] < hi and lo < m[1] and (wr or m[3]) and (row is None or m[4] is None or row == m[4]):
+                        deps.add(m[2])
+                if nm in BANKS:
+                    if bank.setdefault(nm, (eng, [], []))[0] != eng:
+                        bank[nm] = (eng, bank[nm][2], [])
+                    deps.update(bank[nm][1])
+                    bank[nm][2].append(me)
+        for nm, lo, hi, row in rs:
+            marks[nm].append((lo, hi, me, False, row))
+        for nm, lo, hi, row in ws:
+            keep = [m for m in marks[nm] if m[0] < lo or m[1] > hi or sem is not None]
+            marks[nm] = keep + [(lo, hi, me, True, row)]
+        deps.discard(me)
+        deps = [d for d in deps if not (sem is not None and ops[d]["sem"] == sem)]
+        if eng == "t":
+            deps = [d for d in deps if ops[d]["eng"] != "t"]
+        ops.append({"eng": eng, "alt": alt, "deps": deps, "after": after, "sem": sem, "inc": inc, "late": late})
+        return me
 
     V, S, PE = g.vector, g.scalar, g.tensor
 
-    def ts(out, in0, s1, s2, o0, o1, r, w, b=()):
+    def ap(x):
+        return x[0] if isinstance(x, tuple) else x
+
+    def cv(out, *a):
+        if out[3] == "list" or a and a[0][3] == "list":
+            return FIXV + out[2] * CYCLE * (SCATTER if out[3] == "list" else GATHER)
+        return FIXV + max(64, out[2] * (0.5 if all(x[3] in (bf, u16) for x in (out,) + a) else 1)) * CYCLE
+
+    def cs(out, a):
+        return FIXS + (out[2] * GATHER if a[3] == "list" else max(64, out[2])) * CYCLE
+
+    def ts(out, a, s1, s2, o0, o1=None):
         if o1 is None:
-            op("v", lambda: V.tensor_scalar(out, in0, s1, None, o0), r, w, b)
+            op({"v": (lambda: V.tensor_scalar(out[0], a[0], ap(s1), None, o0), cv(out, a))}, [a, s1], [out])
         else:
-            op("v", lambda: V.tensor_scalar(out, in0, s1, s2, o0, o1), r, w, b)
+            op({"v": (lambda: V.tensor_scalar(out[0], a[0], ap(s1), ap(s2), o0, o1), cv(out, a))}, [a, s1, s2], [out])
 
-    def tt(out, a, c, o, r, w, b=()):
-        op("v", lambda: V.tensor_tensor(out, a, c, o), r, w, b)
+    def tt(out, a, c, o):
+        k = 1 if a[3] == "list" or a[1][0][0] in BANKS or c[1][0][0] in BANKS else 2
+        op({"v": (lambda: V.tensor_tensor(out[0], a[0], c[0], o), k * cv(out, a, c))}, [a, c], [out])
 
-    def cp(out, a, r, w, b=()):
-        op("v", lambda: V.tensor_copy(out, a), r, w, b)
+    def cp(out, a):
+        op({"v": (lambda: V.tensor_copy(out[0], a[0]), cv(out, a))}, [a, out] if out[3] == "list" else [a], [(None, out[1][:1])])
 
-    def ms(out, c, w):
-        op("v", lambda: V.memset(out, c), (), w)
+    def ms(out, c):
+        op({"v": (lambda: V.memset(out[0], c), cv(out))}, (), [out])
 
-    def scan(out, d0, d1, ini, o0, o1, r, w, b=()):
-        op("v", lambda: V.tensor_tensor_scan(out, d0, d1, ini, o0, o1), r, w, b)
+    def scan(out, d0, d1, ini, o0, o1):
+        op({"v": (lambda: V.tensor_tensor_scan(out[0], d0[0], d1[0], ap(ini), o0, o1), cv(out, d0, d1))}, [d0, d1, ini], [out])
 
-    def red(out, a, o, r, w, b=()):
-        op("v", lambda: V.tensor_reduce(out, a, AxisListType.X, o), r, w, b)
+    def vtr(out, a):
+        op({"v": (lambda: V.transpose(out[0], a[0]), cv(out, a))}, [a], [out])
 
-    def act(out, a, f, r, w, b=(), bias=0.0, scale=1.0, acc=None):
+    def act(out, a, f, bias=0.0, scale=1.0, acc=None):
         if acc is None:
-            op("s", lambda: S.activation(out, a, f, bias=bias, scale=scale), r, w, b)
+            op({"s": (lambda: S.activation(out[0], a[0], f, bias=ap(bias), scale=ap(scale)), cs(out, a))}, [a, bias, scale], [out])
         else:
-            op("s", lambda: S.activation(out, a, f, bias=bias, scale=scale, accum_out=acc), r, w, b)
+            op({"s": (lambda: S.activation(out[0], a[0], f, bias=ap(bias), scale=ap(scale), accum_out=acc[0]), cs(out, a))},
+               [a, bias, scale], [out, acc])
 
-    def mm(out, l, rh, st, sp, r, b):
-        op("t", lambda: PE.matmul(out, l, rh, st, sp), r, (), b)
+    def lin(out, a, scale=1.0, bias=0.0, who="vs"):
+        plain = not isinstance(scale, tuple) and not isinstance(bias, tuple) and scale == 1.0 and bias == 0.0
+        alt = {"v": ((lambda: V.tensor_copy(out[0], a[0])) if plain else
+                     (lambda: V.tensor_scalar(out[0], a[0], ap(scale), ap(bias), A.mult, A.add)), cv(out, a)),
+               "s": ((lambda: S.activation(out[0], a[0], F.Copy)) if plain else
+                     (lambda: S.activation(out[0], a[0], F.Identity, bias=ap(bias), scale=ap(scale))), cs(out, a))}
+        op({e: alt[e] for e in who}, [a, bias, scale], [out])
 
-    def iota(out, pat, base, cm, w, flt=True):
+    def zero(out, who):
+        z = v("zb", 0, out[2])
+        alt = {"v": (lambda: V.memset(out[0], 0.0), cv(out)), "s": (lambda: S.activation(out[0], z[0], F.Copy), cs(out, z)),
+               "g": (lambda: g.iota(out[0], [[0, out[2]]], 0, 0, allow_small_or_imprecise_dtypes=True), 0.13 + 2 * out[2] * CYCLE)}
+        op({who: alt[who]}, [z] if who == "s" else [], [out])
+
+    sums, ends = {}, {}
+
+    def mm(out, l, rh, st=False, sp=None):
+        gs, me = sums.setdefault(out[1][0][0], [[]]), len(ops)
+        if st:
+            gs.append([])
+        gs[-1].append(me)
+        op({"t": (lambda: PE.matmul(out[0], l[0], rh[0], me in ends["first"], me in ends["last"]),
+                  max(64, rh[2]) * (4 if l[3] == f32 else 1) * PECYCLE)}, [l, rh], [out], after=gs[-2])
+
+    def iota(out, pat, base, cm, flt=True):
         if flt:
-            op("g", lambda: g.iota(out, pat, base, cm, allow_small_or_imprecise_dtypes=True), (), w)
+            op({"g": (lambda: g.iota(out[0], pat, base, cm, allow_small_or_imprecise_dtypes=True), 0.13 + 2 * out[2] * CYCLE)}, (), [out])
         else:
-            op("g", lambda: g.iota(out, pat, base, cm), (), w)
+            op({"g": (lambda: g.iota(out[0], pat, base, cm), 0.13 + 2 * out[2] * CYCLE)}, (), [out])
 
-    def sel(out, a, pat, o, base, cm, r, w):
-        op("g", lambda: g.affine_select(out, a, pat, o, 0.0, base, cm), r, w)
+    def sel(out, a, pat, o, base, cm):
+        op({"g": (lambda: g.affine_select(out[0], a[0], pat, o, 0.0, base, cm), 0.17 + 2 * out[2] * CYCLE)}, [a], [out])
 
-    def dma(q, out, a, r, w, sem):
-        op(q, lambda: (g.sync if q == "y" else g.scalar).dma_start(out, a), r, w, sem=sem)
+    moved, copies = {}, []
 
-    def xt(c0, c1):
-        return [("x", j) for j in range(c0 // 32, (c1 - 1) // 32 + 1)]
+    def dma(q, out, a, sem, kb):
+        o, i = (out if isinstance(out, tuple) else (out, [])), (a if isinstance(a, tuple) else (a, []))
+        moved[sem] = moved.get(sem, 0) + kb
+        copies.append(op({q: (lambda: (g.sync if q == "y" else g.scalar).dma_start(o[0], i[0]), 0.06)}, [i], [o], sem=sem,
+                         late=DMA0 + moved[sem] / DMARATE, after=copies[-1:] if q == "y" and sem[0] != "o" else []))
 
-    WT = [("W", j) for j in range(8)] + [("Wf", j) for j in range(32)]
-    I = T.ib[:, 0:128]
-    ID = F.Identity
+    def gather(who, out, w, off):
+        lin(out, ix(w, off), who=who)
+
+    I, NI, ID = v("ib", 0, 128), v("nib"), F.Identity
+    turnb = [0]
+
+    def nextb():
+        turnb[0] += 1
+        return "pb%d" % (turnb[0] % 4)
+
+    def X(a, b, s=None):
+        return v("win", XO + a, XO + b, s)
+
+    def G(a, b, s=None):
+        return v("win", GO + a, GO + b, s)
 
     def E(w, c):
-        return T.eb[:, 144 * w + 15 - c:144 * w + 143 - c]
+        return v("eb", 144 * w + 15 - c, 144 * w + 143 - c)
 
     def EW(w):
-        return T.eb[:, 144 * w + 15:144 * w + 143:16]
+        return v("eb", 144 * w + 15, 144 * w + 143, 16)
 
-    def runs(us):
-        out = []
-        for u in us:
-            if out and out[-1][1] == u:
-                out[-1][1] = u + 1
+    def pc(j):
+        return v("pf", j, j + 1)
+
+    def col(name, j):
+        return (T[name][:, j:j + 1], [(name, j, j + 1, None)], 1, SCRATCH[name][2])
+
+    ms(v("zb"), 0.0)
+    ms(v("thi"), 0)
+    dma("s", v("li"), T.l0[:], "ldl", 128)
+    dma("y", v("tab"), T.x0[:], "ldx", 1024)
+    dma("y", v("thi", 0, 3, None, slice(0, 128, 16)), T.th[:], "ldt", 1024)
+    dma("y", v("zc"), T.z0[:], "ldz", 1100)
+    ms(v("oneb"), 1.0)
+    iota(v("pint", 0, 1), [[0, 1]], 0, 1, False)
+    iota(v("dupf"), [[1, 16], [0, 2]], 0, 0)
+    iota(v("selff"), [[32, 16]], 0, 0)
+    iota(v("colf"), [[1, 16]], 0, 0)
+    sel(v("ib"), v("oneb"), [[0, 2], [-1, 128]], A.is_equal, 0, 1)
+    sel(v("bob"), v("oneb", 0, 128), [[-16, 8], [0, 16]], A.is_ge, 0, 1)
+    sel(v("bob"), v("bob"), [[16, 8], [0, 16]], A.is_ge, 15, -1)
+    iota(v("tcol"), [[1, 72]], 0, 0)
+    iota(v("kt"), [[1, 256]], 0, 0)
+    B8 = v("bob", 0, 128, 16)
+    moved["fill"] = 1200
+
+    def fill(j0, j1):
+        for j in range(j0, j1):
+            u = 4 * FILLED[j // 4] + j % 4
+            if FILLER[j] == "y":
+                moved["fill%d" % (j // 4)] = 1200 + 256 * FILLER[:j].count("y")
+                dma("y", v("win", 1024 * u, 1024 * u + 1024), v("zb"), "fill%d" % (j // 4), 256)
             else:
-                out.append([u, u + 1])
-        return [(1024 * a, WIN if c == 32 else 1024 * c, [("Wf", j) for j in range(a, c)]) for a, c in out]
+                zero(v("win", 1024 * u, 1024 * u + 1024), FILLER[j])
 
-    ms(T.zb[:], 0.0, ["zb"])
-    ms(T.thi[:], 0, ["thi"])
-    dma("s", T.li[:], T.l0[:], (), ["li"], "ldl")
-    dma("y", T.tab[:], T.x0[:], (), ["tab"], "ldx")
-    dma("y", T.thi[0:128:16, 0:3], T.th[:], (), ["thi"], "ldt")
-    dma("y", T.zc[:], T.z0[:], (), ["zc"], "ldz")
-    ms(T.oneb[:], 1.0, ["oneb"])
-    iota(T.pint[:, 0:1], [[0, 1]], 0, 1, ["p0"], False)
-    iota(T.colf[:], [[1, 16]], 0, 0, ["colf"])
-    iota(T.flf[:], [[32, 8], [-16, 2]], 16, 0, ["flf"])
-    sel(T.ib[:], T.oneb[:], [[0, 2], [-1, 128]], A.is_equal, 0, 1, ["oneb"], ["ib"])
-    iota(T.mask0[:], [[0, 8], [1, 2], [0, 16]], 0, 0, ["mask0"])
-    sel(T.bob[:], T.oneb[:, 0:128], [[-16, 8], [0, 16]], A.is_ge, 0, 1, ["oneb"], ["bob"])
-    sel(T.bob[:], T.bob[:], [[16, 8], [0, 16]], A.is_ge, 15, -1, ["bob"], ["bob"])
-    sel(T.lt[:], T.bob[:], [[1, 128]], A.is_gt, 0, -1, ["bob"], ["lt"])
-    sel(T.ut[:], T.bob[:], [[-1, 128]], A.is_gt, 0, 1, ["bob"], ["ut"])
-    iota(T.colb[:], [[1, 256]], 0, 0, ["colb"])
-    iota(T.ones[:], [[0, 256]], 1, 0, ["ones"])
-    for a, c, tk in runs(FILL["g"]):
-        iota(T.win[:, a:c], [[0, c - a]], 0, 0, tk)
-    B8 = T.bob[:, 0:128:16]
-    for j, u in enumerate(FILL["s"]):
-        act(T.win[:, 1024 * u:1024 * u + 1024], T.zb[:], F.Copy, ["zb"], [("Wf", u)])
-        if j == 0:
-            act(T.eb[:], T.zb[:, 0:864], F.Copy, ["zb"], ["eb0"])
-        if j == 3:
-            act(EW(0), B8, F.Copy, ["bob", "eb0"], ["eb"])
-            act(T.nib[:], I, F.Copy, ["ib"], ["nib"], scale=-1.0)
-            act(T.bo[:], T.bob[:], F.Copy, ["bob"], ["bo"])
-    for u in FILL["y"]:
-        dma("y", T.win[:, 1024 * u:1024 * u + 1024], T.zb[:], ["zb"], [("Wf", u)], "fill")
-    ts(T.pint[:, 1:2], T.pint[:, 0:1], 15, None, A.bitwise_and, None, ["p0"], ["p1"])
-    ts(T.pint[:, 3:4], T.pint[:, 0:1], 4, 1, A.arith_shift_right, A.bitwise_and, ["p0"], ["p3"])
-    cp(T.pf[:, 1:4:2], T.pint[:, 1:4:2], ["p1", "p3"], ["pf"])
-    ms(T.xb[:, 0:16], 0.0, ["xpad"])
-    ts(T.pf[:, 4:5], T.pf[:, 1:2], 16.0, None, A.mult, None, ["pf"], ["pf4"])
-    ts(T.pf[:, 6:7], T.pf[:, 3:4], -1.0, 1.0, A.mult, A.add, ["pf"], ["pf6"])
-    ts(T.fl[:], T.flf[:], T.pf[:, 1:2], None, A.add, None, ["flf", "pf"], ["fl"])
-    ts(T.pt[:], T.colf[:], T.pf[:, 4:5], None, A.add, None, ["colf", "pf4"], ["pt"])
-    ts(T.sw[:], T.ib[:, 16:144], T.pf[:, 3:4], None, A.mult, None, ["ib", "pf"], ["sw"])
-    ts(T.sw2[:], T.ib[:, 112:240], T.pf[:, 6:7], None, A.mult, None, ["ib", "pf6"], ["sw2"])
-    ts(T.mask0[:], T.mask0[:], T.pf[:, 3:4], None, A.is_equal, None, ["mask0", "pf"], ["mask0"])
-    tt(T.sw[:], T.sw[:], T.sw2[:], A.add, ["sw", "sw2"], ["sw"])
+    for j in range(32):
+        if FILLER[j] in "yg":
+            fill(j, j + 1)
+    zero(v("eb"), "s")
+    lin(v("ib16"), I, 1.0 / 16.0)
+    lin(v("nib16"), I, -16.0)
+    lin(v("bo"), v("bob"))
+    lin(EW(0), B8)
+    lin(NI, I, -1.0)
+    ts(col("pint", 1), col("pint", 0), 15, None, A.bitwise_and)
+    ts(col("pint", 2), col("pint", 0), 31, None, A.bitwise_and)
+    ts(col("pint", 4), col("pint", 0), 15.0, None, A.add)
+    ts(col("pint", 3), col("pint", 4), 15, None, A.bitwise_and)
+    cp(v("pf", 0, 4), v("pint", 0, 4))
+    PC, PJ = col("pf", 1), col("pf", 2)
+    ts(v("pf", 8, 12), v("pf", 0, 4), 16.0, None, A.mult)
+    ts(v("dup"), v("dupf"), col("pf", 9), None, A.add)
+    ts(v("selc"), v("selff"), PJ, None, A.add)
+    ts(v("pt"), v("colf"), col("pf", 9), None, A.add)
 
-    def turn(src, stok, dst, dtok):
-        op("v", lambda: V.transpose(T.s7[:], src), [stok], ["s7"])
-        tt(T.s8[:], T.s7[:].indirect(T.fl[:]), T.mask0[:], A.mult, ["s7", "fl", "mask0"], ["s8"])
-        mm(T.pmm[:, 0:256], T.sw[:], T.s8[:], True, True, ["sw", "s8"], ["pmm"])
-        tt(T.s6[:], T.s7[:], T.mask0[:], A.mult, ["s7", "mask0"], ["s6"])
-        tt(dst, T.pmm[:, 0:256], T.s6[:], A.add, ["s6"], [dtok], ["pmm"])
+    def turn(src):
+        cp(v("w1"), ix(src, v("dup")))
+        vtr(v("w2"), v("w1"))
 
-    def digits(src, tok):
-        ts(T.digi[:, 256:512], T.ni[:], 4, 15, A.arith_shift_right, A.bitwise_and, ["ni"], ["dg1"])
-        ts(T.digi[:, 512:768], T.ni[:], 15, None, A.bitwise_and, None, ["ni"], ["dg2"])
-        ts(T.h1[:], src, 1.0 / 256.0, 191.502, A.mult, A.add, [tok], ["h1"])
-        cp(T.dig[:, 256:768], T.digi[:, 256:768], ["dg1", "dg2"], ["dig"])
-        ts(T.dig[:, 0:256], T.h1[:], -192.0, None, A.add, None, ["h1"], ["dig0"])
+    def digits(src, perm):
+        a = ix(src, v("pt")) if perm else src
+        ts(v("r32"), a, M16, M16, A.add, A.subtract)
+        lin(v("hh"), v("r32"), 1.0 / 256.0, 191.53125)
+        lin(v("dig", 0, 256), v("hh"), 1.0, -199.5)
+        tt(v("dig", 512, 768), a, v("r32"), A.subtract)
+        b = v(nextb(), 0, 256)
+        mm(b, v("ib16"), v("r32"), True, False)
+        mm(b, v("nib16"), v("dig", 0, 256), False, True)
+        lin(v("dig", 256, 512), b, 1.0, -127.5)
 
     def window(t):
-        for pl in range(3):
-            dma("y", T.win[0:128:16, 12288 * pl:12288 * pl + 4096], T.dig[:, 256 * pl:256 * pl + 256],
-                ["dig", "dig0"] + [("Wf", 12 * pl + j) for j in range(4)], [("W", 3 * pl), ("mst", pl)], "la%d" % t)
-        for pa, rg, pl, sh in CELLS:
-            dma("y", T.win[pa:128:16, 4096 * rg:4096 * rg + 4096 - sh], T.win[0:128:16, 12288 * pl + sh:12288 * pl + 4096],
-                [("mst", pl)] + [("Wf", 4 * rg + j) for j in range(4)], [("W", rg)], "lb%d" % t)
-
-    cp(T.nu[:], T.li[:], ["li"], ["nu"])
-    cp(T.s5[:], T.li[:].indirect(T.pt[:]), ["li", "pt"], ["s5"])
-    turn(T.s5[:], "s5", T.ni[:], "ni")
-    digits(T.ni[:], "ni")
-    for a, c, tk in runs(FILL["v1"]):
-        ms(T.win[:, a:c], 0.0, tk)
-    ms(T.dinit[:], 0.0, ["dinit"])
-    cp(T.th8[:], T.thi[:], ["thi"], ["th8"])
-    ts(T.dinit[:, 0:1], T.pf[:, 1:2], 0.0, 8192.0, A.is_equal, A.mult, ["pf"], ["dinit"])
-    mm(T.pq[:, 0:4], T.bo[:], T.th8[:], True, True, ["bo", "th8"], ["pq"])
-    for a, c, tk in runs(FILL["v2"]):
-        ms(T.win[:, a:c], 0.0, tk)
-    window(0)
-
-    def consts_v():
-        d, x, y, q = T.ct[:, 0:16], T.ct[:, 16:32], T.ct[:, 32:48], T.pf[:, 14:15]
-        x2, y2 = T.ct[:, 48:64], T.ct[:, 64:80]
-        ts(d, T.colf[:], T.pf[:, 1:2], None, A.subtract, None, ["colf", "pf"], ["cd"])
-        ts(q, T.pf[:, 1:2], -256.0, 3840.0, A.mult, A.add, ["pf"], ["cq"])
-        ts(T.m16[:], d, 0.0, None, A.is_equal, None, ["cd"], ["m16"])
-        ts(x, d, -256.0, -256.0, A.mult, A.add, ["cd"], ["cx"])
-        ts(y, d, 0.0, 16384.0, A.is_ge, A.mult, ["cd"], ["cy"])
-        ts(x2, d, 256.0, -256.0, A.mult, A.add, ["cd"], ["cx2"])
-        ts(y2, d, 0.0, 16384.0, A.is_le, A.mult, ["cd"], ["cy2"])
-        tt(T.cc[:, 0:16], x, y, A.max, ["cx", "cy"], ["cc0"])
-        tt(x2, x2, y2, A.add, ["cx2", "cy2"], ["cx2"])
-        ms(T.nb[:, 256:264], BIG, ["nb"])
-        ts(T.cc[:, 16:32], x2, q, None, A.min, None, ["cx2", "cq"], ["cc1"])
-        ts(T.c256[:], T.oneb[:], T.pf[:, 1:2], 256.0, A.mult, A.mult, ["oneb", "pf"], ["c256"])
-        cp(T.thf[:], T.pq[:, 0:4], [], ["thf"], ["pq"])
-
-    def consts_s():
-        act(T.pf[:, 7:8], T.m16[:, 1:2], ID, ["m16"], ["w0"], bias=T.m16[:, 2:3], scale=16.0)
-        act(T.pf[:, 9:10], T.m16[:, 3:4], ID, ["m16"], ["wb"], bias=T.m16[:, 4:5], scale=16.0)
-        act(T.pf[:, 8:9], T.m16[:, 0:1], ID, ["m16", "w0"], ["wa"], bias=T.pf[:, 7:8], scale=256.0)
-        act(EW(5), B8, F.Copy, ["bob", "wb", "eb0"], ["eb2"], scale=T.pf[:, 9:10])
-        act(EW(4), B8, F.Copy, ["bob", "wa", "eb0"], ["eb3"], scale=T.pf[:, 8:9])
-        act(T.cm75[:], T.oneb[:], F.Copy, ["oneb"], ["cm75"], scale=-7.5)
-        for w, c in ((1, -1.0), (2, 2.0), (3, -2.0)):
-            act(EW(w), B8, F.Copy, ["bob", "eb0"], [("ebw", w)], scale=c)
-        act(T.ib256[:], T.ib[:], F.Copy, ["ib"], ["ib256"], scale=256.0)
-        act(T.nib256[:], I, F.Copy, ["ib"], ["nib256"], scale=-256.0)
-
-    def consts_s2():
-        act(T.cm05[:], T.oneb[:], F.Copy, ["oneb"], ["cm05"], scale=-0.5)
-        act(T.cb[:], T.colf[:], ID, ["colf", "pf4"], ["cb"], bias=T.pf[:, 4:5], scale=256.0)
-        act(T.ym[:], T.zb[:, 0:512], ID, ["zb"], ["ym"], bias=1.0)
-        act(T.ym[:, 0:512:16], T.zb[:, 0:32], F.Copy, ["zb"], ["ym"])
-
-    def gather_x(eng, c0, c1):
-        out, src = T.xb[:, 16 + 16 * c0:16 + 16 * c1], T.tab[:].indirect(T.nu[:, c0:c1])
-        if eng == "v":
-            cp(out, src, ["tab", "nu"], xt(16 * c0, 16 * c1))
+        def row(pl, sh):
+            if t == 0:
+                return v("tmp", sh, RG, None, slice(pl, 128, 16))
+            return v("win", RG * MASTER[pl] + sh, RG * MASTER[pl] + RG, None, slice(0, 128, 16))
+        for pl in (2, 0, 1):
+            dma("y", row(pl, 0), v("dig", 256 * pl, 256 * pl + 256), "la%d%d" % (t, pl), 64)
+        if t == 0:
+            cells = sorted(CELLS + [(0, MASTER[pl], pl, 0) for pl in range(3)], key=lambda x: FILLED.index(x[1]))
         else:
-            act(out, src, F.Copy, ["tab", "nu"], xt(16 * c0, 16 * c1))
+            cells = sorted(CELLS, key=lambda x: (2, 0, 1).index(x[2]))
+        for pa, rg, pl, sh in cells:
+            moved["lb0"] = 256
+            dma("y", v("win", RG * rg, RG * rg + RG - sh, None, slice(pa, 128, 16)), row(pl, sh), "lb%d" % t, 64)
 
-    def cuts(a, c):
-        e = [a] + [j for j in range(32, 256, 32) if a + 8 < j < c - 8] + [c]
-        return list(zip(e[:-1], e[1:]))
-
-    def stage_x(t, before_v):
-        nat = t == 0
-        for a, c in cuts(S0[t], 256):
-            gather_x("s", a, c)
-        before_v()
-        for a, c in cuts(0, S0[t]):
-            gather_x("v", a, c)
-        mm(T.pd[:, 0:256], I, T.dinit[:], True, False, ["ib", "dinit"], ["pd"])
-        first = (S0[t] + 2 + 31) // 32
-        order = list(range(first, 8)) + list(range(first))
-        done, pend = set(), []
-
-        def ext(u, last):
-            if nat:
-                for h in range(2):
-                    c = 2 * u + h
-                    mm(T.pd[:, 0:256], E(0, c), T.ga[:, 256 * c:256 * c + 256], False, last and h == 1, ["eb", ("ga", u)], ["pd"])
-            else:
-                for c in range(16):
-                    mm(T.pd[:, 64 * u:64 * u + 64], E(0, c), T.ga[:, 1024 * u + c:1024 * u + 1024:16], False, last and c == 15,
-                       ["eb", ("ga", 2 * u), ("ga", 2 * u + 1)], ["pd"])
-        for j, u in enumerate(order):
-            bn = "pb%d" % (j & 1)
-            pb, c0 = T[bn], 512 * u
-            mm(pb[:], I, T.xb[:, 16 + c0:16 + c0 + 512], True, False, ["ib"] + xt(c0, c0 + 512), [bn])
-            if nat:
-                mm(pb[:], T.nib[:], T.xb[:, 15 + c0:15 + c0 + 512], False, True, ["nib", "xpad"] + xt(max(c0 - 1, 0), c0 + 511), [bn])
-            elif u == 0:
-                mm(pb[:, 16:512], T.nib[:], T.xb[:, 16:512], False, False, ["nib"] + xt(0, 496), [bn])
-                mm(pb[:, 0:16], T.nib[:], T.xb[:, 16 + 4079:16 + 4095], False, True, ["nib"] + xt(4079, 4095), [bn])
-            else:
-                mm(pb[:], T.nib[:], T.xb[:, c0:c0 + 512], False, True, ["nib"] + xt(c0 - 16, c0 + 496), [bn])
-            for e in pend:
-                ext(e, False)
-            del pend[:]
-            act(T.ga[:, c0:c0 + 512], pb[:], F.Abs, [], [("ga", u)], [bn])
-            done.add(u)
-            if nat:
-                pend.append(u)
-            elif (u ^ 1) in done:
-                pend.append(u // 2)
-        for e in pend:
-            ext(e, e == pend[-1])
-
-    Y = T.tmp[:, 15:4096:16]
-    TY = [("tmp", c) for c in range(16)]
-
-    def yscan(c):
-        scan(T.tmp[:, 256 * c:256 * c + 256], T.ym[:, 0:256], T.xb[:, 16 + c:4112:16], 0.0, A.mult, A.max, ["ym"] + xt(0, 4096), [("tmp", c)])
+    cp(v("nu"), v("li"))
+    turn(v("li"))
+    lin(v("s4"), ix(v("w2"), v("selc")), 1.0, -7.5)
+    digits(v("s4"), False)
+    for j in range(FIRST):
+        if FILLER[j] in "vs":
+            fill(j, j + 1)
+    ms(v("dinit"), 0.0)
+    cp(v("th8"), v("thi"))
+    ts(v("dinit", 0, 1), PC, 0.0, -4096 * BIG, A.is_equal, A.mult)
+    mm(v("pq0", 0, 8), v("bo"), v("th8"), True, True)
 
     def ztile():
-        for h in range(2):
-            act(T.z2[:, 256 * h:256 * h + 256], T.zc[:].indirect(T.pt[:]), F.Copy, ["zc", "pt"], [("z2", h)])
-    Z2 = [("z2", 0), ("z2", 1)]
+        lin(v("z2", 0, 256), ix(v("zc"), v("pt")))
+        lin(v("z2", 256, 512), v("z2", 0, 256))
+
+    def consts_v():
+        t, d, e = v("tcol", 0, 65), v("cd", 0, 65), v("ce", 0, 65)
+        ts(v("thp"), v("pq0", 0, 8), 0.5, None, A.add)
+        ts(col("thb", 0), col("thp", 0), BIG / 2, None, A.mult)
+        ts(col("pf", 12), PC, 256.0, None, A.mult)
+        ts(v("kt"), v("kt"), col("pf", 12), None, A.add)
+        ms(v("nb"), BIG)
+        ms(v("three"), 0.0)
+        ms(v("zadd"), 0.0)
+        ms(v("three", 0, 256), 2.0)
+        ms(v("zadd", 0, 256), 1.0)
+        ts(v("zadd", 256, 257), PC, 0.0, BIG, A.is_equal, A.mult)
+        tt(col("pf", 13), PJ, PC, A.subtract)
+        ts(col("pf", 14), PC, 0.0, -LOW, A.is_gt, A.mult)
+        ts(col("pf", 15), PJ, 33.0, None, A.add)
+        ts(col("pf", 16), PJ, 16.0, LOW, A.is_lt, A.mult)
+        ts(d, t, PJ, 512.0, A.is_lt, A.mult)
+        ms(v("cd", 33, 64), -256.0)
+        ts(e, t, col("pf", 13), 2 * BIG, A.is_equal, A.mult)
+        tt(d, d, e, A.add)
+        ts(e, t, PJ, col("pf", 14), A.is_equal, A.mult)
+        tt(d, d, e, A.add)
+        ts(e, t, col("pf", 15), 2 * BIG, A.is_equal, A.mult)
+        tt(d, d, e, A.add)
+        ts(col("cd", 32), col("pf", 14), -1.0, None, A.mult)
+        tt(col("cd", 48), col("cd", 48), col("pf", 16), A.subtract)
+        lin(col("pf", 18), PC, -256.0, 3584.0)
+        lin(col("pf", 19), col("pf", 16), 1.0 + 4096.0 / LOW, col("pf", 18))
+        tt(col("cd", 64), col("cd", 64), col("pf", 19), A.add)
+        lin(col("ht", 64), PC, -256.0, 3840.0)
+        lin(EW(2), B8, -BIG / 2)
+
+    def consts_s():
+        for j in range(5):
+            ts(col("pf", 20 + j), PC, float(j), (256.0, 16.0, 1.0, 1.0, 16.0)[j], A.is_equal, A.mult)
+        tt(col("pf", 26), col("pf", 23), col("pf", 24), A.add)
+        tt(col("pf", 25), col("pf", 20), col("pf", 21), A.add)
+        tt(col("pf", 27), col("pf", 25), col("pf", 22), A.add)
+        lin(EW(5), B8, col("pf", 26))
+        lin(EW(4), B8, col("pf", 27))
+        lin(v("c2040"), v("oneb", 0, 128), 2040.0)
+        ztile()
+        for w, c in ((1, -1.0), (3, -2.0), (6, 2.0)):
+            lin(EW(w), B8, c)
+        lin(v("nib256"), I, -256.0)
+        lin(v("ib256"), v("ib"), 256.0)
+        lin(v("cm05"), v("oneb"), -0.5)
+        lin(v("cb"), v("colf"), 256.0, col("pf", 9))
+        lin(v("ym16"), v("zb", 0, 512), 1.0, 1.0)
+        lin(v("ym16", 0, 512, 16), v("zb", 0, 32))
+        ts(col("pf", 17), PC, 31.0, PJ, A.mult, A.add)
+        ts(v("sell"), v("colf"), col("pf", 17), None, A.add)
+
+    def xg(u0, u1, who):
+        gather(who, X(512 * u0, 512 * u1), v("tab"), v("nu", 32 * u0, 32 * u1))
+
+    def calls(who, u0, u1):
+        out = []
+        for u in range(u0, u1):
+            if who[u].isupper():
+                out[-1][2] = u + 1
+            else:
+                out.append([who[u], u, u + 1])
+        return out
+
+    def first_x():
+        D = v("px0", 0, 256)
+        mm(D, I, v("dinit", 0, 256), True, False)
+        for who, u0, u1 in calls(X0, 0, 8):
+            xg(u0, u1, who)
+        for u in range(8):
+            bn, c1 = nextb(), int(u == 0)
+            mm(v(bn, c1, 512), I, X(512 * u + c1, 512 * u + 512), True, False)
+            if c1:
+                mm(v(bn, 0, 1), I, X(0, 1))
+            mm(v(bn, c1, 512), NI, X(512 * u - 1 + c1, 512 * u + 511), False, True)
+            act(G(512 * u, 512 * u + 512), v(bn), F.Abs)
+            for c in (2 * u, 2 * u + 1):
+                mm(D, E(2, c), G(256 * c, 256 * c + 256))
+        begins(0, 256, D)
+
+    def begins(c0, c1, D):
+        out, th = v("nb", 32 + c0, 32 + c1), col("thb", 0)
+        op({"v": (lambda: V.tensor_scalar(out[0], D[0], th[0], 0.0, A.add, A.max), cv(out, D)),
+            "s": (lambda: S.activation(out[0], D[0], F.Relu, bias=th[0]), cs(out, D))}, [D, th], [out])
+
+    def piece(u):
+        c0 = 512 * u
+        if DX[u] == "v":
+            tt(v("d3", c0, c0 + 512), X(c0, c0 + 512), X(c0 - 16, c0 + 496), A.subtract)
+            act(G(c0, c0 + 512), v("d3", c0, c0 + 512), F.Abs)
+            return
+        bn = nextb()
+        if u > 0:
+            mm(v(bn), I, X(c0, c0 + 512), True, False)
+            mm(v(bn), NI, X(c0 - 16, c0 + 496), False, True)
+        else:
+            mm(v(bn, 0, 16), I, X(0, 16), True, False)
+            mm(v(bn, 16, 512), I, X(16, 512), False, False)
+            mm(v(bn, 16, 512), NI, X(0, 496), False, False)
+            mm(v(bn, 0, 16), NI, X(4079, 4095), False, True)
+        act(G(c0, c0 + 512), v(bn), F.Abs)
+
+    def dsum(q):
+        out = v("px0", 64 * q, 64 * q + 64) if q < 3 else v("px1", 0, 64)
+        if q == 0:
+            mm(out, I, v("dinit", 0, 64), True, False)
+        for c in range(16):
+            mm(out, E(2, c), G(1024 * q + c, 1024 * q + 1024, 16), q == 3 and c == 0)
+
+    Y = v("tmp", 15, 4096, 16)
+
+    def yscan(c):
+        scan(v("tmp", 256 * c, 256 * c + 256), v("ym16", 0, 256), X(c, 4096, 16), 0.0, A.mult, A.max)
 
     def blocks_a():
+        b1, b2 = "pq0", "pq1"
+        mm(v(b1, 0, 256), I, Y, True, False)
+        mm(v(b1, 0, 256), NI, v("zc"))
+        mm(v(b2, 0, 256), I, Y, True, False)
+        mm(v(b2, 0, 256), I, v("zc"), False, False)
+        mm(v(b2, 0, 256), I, v("cm05"), False, True)
         for b in range(16):
-            mm(T.pmm[:, 256:272], E(0, b), T.tmp[:, 15 + 16 * b:4096:256], b == 0, b == 15, ["eb"] + TY, ["pmm"])
-        mm(T.pb0[:, 0:256], I, Y, True, False, ["ib"] + TY, ["pb0"])
-        mm(T.pb0[:, 0:256], T.nib[:], T.zc[:], False, True, ["nib", "zc"], ["pb0"])
-        mm(T.pb0[:, 256:512], I, Y, True, False, ["ib"] + TY, ["pb0"])
-        mm(T.pb0[:, 256:512], I, T.zc[:], False, False, ["ib", "zc"], ["pb0"])
-        mm(T.pb0[:, 256:512], I, T.cm05[:], False, True, ["ib", "cm05"], ["pb0"])
-        act(T.zs[:], T.pb0[:, 256:512], ID, [], ["zs"], ["pb0"], bias=M1, scale=0.5)
-        act(T.zc[:], T.pb0[:, 0:256], F.Abs, [], ["zc"], ["pb0"])
-        act(T.avg[:], T.zs[:], ID, ["zs"], ["avg"], bias=-M1)
+            mm(v(b2, 256, 272), E(0, b), v("tmp", 15 + 16 * b, 4096, 256))
+        act(v("zc"), v(b1, 0, 256), F.Abs)
+        ztile()
+        lin(v("zs"), v(b2, 0, 256), 0.5, M1)
+        lin(v("avg"), v("zs"), 1.0, -M1)
 
     def blocks_b():
-        cp(T.ui[:, 0:16], T.pmm[:, 256:272], [], ["ui0"], ["pmm"])
-        ts(T.ui[:, 16:32], T.ui[:, 0:16], 15, None, A.bitwise_and, None, ["ui0"], ["ui1"])
-        tt(T.uf[:], T.ui[:, 16:32], T.cb[:], A.add, ["ui1", "cb"], ["uf"])
-        cp(T.cu[:], T.uf[:], ["uf"], ["cu"])
+        cp(v("ui", 0, 16), v("pq1", 256, 272))
+        ts(v("ui", 16, 32), v("ui", 0, 16), 15, None, A.bitwise_and)
+        tt(v("uf"), v("ui", 16, 32), v("cb"), A.add)
+        cp(v("cu"), v("uf"))
+
+    def update():
+        cp(ix(v("tab"), v("cu")), v("avg"))
 
     def periods(t):
-        J, b2, s2, tp, ln = T.pv0[:, 0:256], T.pv0[:, 256:512], T.pv1[:, 0:256], T.pv1[:, 256:512], T.pmm[:, 0:256]
-        sp, kk = T.pq[:, 0:256], T.pb1[:, 0:256]
-        nb = T.nb[:, 0:256]
-        thr = T.thf[:, 0:1] if t == 0 else T.thr[:, 0:1]
-        ts(nb, T.pd[:, 0:256], thr, BIG, A.is_le, A.mult, ["thr", "thf"], ["nb"], ["pd"])
-        mm(kk, I, T.colb[:], True, False, ["ib", "colb"], ["pb1"])
-        mm(kk, I, T.c256[:], False, True, ["ib", "c256"], ["pb1"])
-        if t > 0:
-            blocks_a()
-        else:
-            consts_s()
-        scan(T.h1[:], T.oneb[:], nb, 8192.0, A.add, A.min, ["nb", "oneb"], ["h1"])
-        scan(T.h2[:, ::-1], T.oneb[:], T.nb[:, 255::-1], 8192.0, A.add, A.min, ["nb", "oneb"], ["h2"])
-        ts(T.r12[:, 0:16], T.m16[:], T.h1[:, 255:256], None, A.mult, None, ["m16", "h1"], ["r1"])
-        ts(T.r12[:, 16:32], T.m16[:], T.h2[:, 0:1], None, A.mult, None, ["m16", "h2"], ["r2"])
-        mm(T.pd[:, 256:288], I, T.cc[:], True, False, ["ib", "cc0", "cc1"], ["pd"])
-        mm(T.pd[:, 256:272], T.lt[:], T.r12[:, 0:16], False, False, ["lt", "r1"], ["pd"])
-        mm(T.pd[:, 272:288], T.ut[:], T.r12[:, 16:32], False, True, ["ut", "r2"], ["pd"])
-        red(T.car[:, 0:1], T.pd[:, 256:272], A.min, [], ["c0"], ["pd"])
-        red(T.car[:, 1:2], T.pd[:, 272:288], A.min, [], ["c1"], ["pd"])
-        scan(T.s1[:], T.ones[:], nb, T.car[:, 0:1], A.add, A.min, ["nb", "ones", "c0"], ["s1"])
-        act(T.s7[:], T.s1[:], ID, ["s1"], ["s7"], bias=3.0, scale=2.0)
-        scan(T.pv0[:, 255::-1], T.nb[:, 256:0:-1], T.ones[:], T.car[:, 1:2], A.min, A.add, ["nb", "ones", "c1"], ["J"], ["pv0"])
-        tt(ln, T.s1[:], J, A.add, ["J", "s1"], ["ln"], ["pv0", "pmm"])
-        tt(T.s3[:], T.s7[:], J, A.subtract, ["s7", "J"], ["s3"], ["pv0"])
-        act(T.s4[:], T.s3[:], F.Relu, ["s3"], ["s4"])
-        act(T.pb0[:, 0:256], T.s4[:], F.Relu, ["s4"], [], ["pb0"], bias=12288.0, scale=-4096.0)
-        tt(T.s2[:], kk, T.s1[:], A.subtract, ["s1"], ["s2"], ["pb1"])
-        tt(T.h1[:], T.s3[:], ln, A.subtract, ["s3", "ln"], ["h1"], ["pmm"])
-        act(sp, ln, F.Relu, [], [], ["pmm", "pq"], bias=32770.0, scale=-16385.0)
-        ztile()
-        ts(T.h2[:], T.h1[:], -1.0, -1.0, A.add, A.max, ["h1"], ["h2"])
-        ts(T.h1[:], T.h2[:], 2.0, 4096.0, A.min, A.mult, ["h2"], ["h1"])
-        tt(T.s6[:], T.h1[:], T.pb0[:, 0:256], A.subtract, ["h1"], ["s6"], ["pb0"])
-        tt(s2, T.s2[:], sp, A.add, ["s2"], ["s2p"], ["pq", "pv1"])
-        tt(T.s1[:], s2, T.s6[:], A.add, ["s2p", "s6"], ["s1"], ["pv1"])
-        ts(T.pm[:], T.s6[:], 1.0 / 12288.0, None, A.mult, None, ["s6"], ["pm"])
-        ts(T.ob[:], T.s1[:].indirect(T.pt[:]), 16384.0, None, A.add, None, ["s1", "pt"], ["ob"])
-        tt(tp, T.pm[:], ln, A.mult, ["pm", "ln"], ["tp"], ["pmm", "pv1"])
-        tt(tp, T.s3[:], tp, A.subtract, ["s3", "tp"], ["tp"], ["pv1"])
-        tt(T.s5[:], T.s1[:], tp, A.add, ["s1", "tp"], ["s5"], ["pv1"])
-        ts(T.oa[:], T.s5[:].indirect(T.pt[:]), 16381.0, None, A.add, None, ["s5", "pt"], ["oa"])
+        g1, hf, un, cl, cl2 = v("pb0", 0, 256), v("pb1", 0, 256), v("pb1", 256, 512), v("pb2", 0, 256), v("pb3", 0, 256)
+        s2, t1, xx = v("pb0", 256, 512), v("px0", 0, 256), v("px0", 256, 512)
+        f2, uu, sp, vv = v("f2"), v("uu"), v("sp"), v("vv")
+        scan(v("hb", 0, 288), v("three"), v("nb", 32, 320), BIG, A.add, A.min)
+        scan(v("hb", 575, 287, -1), v("zadd"), v("nb", 287, None, -1), BIG, A.add, A.min)
+        vtr(v("ht", 0, 64), v("hb", 256, 320))
+        scan(v("car", 0, 65), v("cd", 0, 65), v("ht", 0, 65), BIG, A.add, A.min)
+        scan(g1, v("three", 0, 256), v("nb", 32, 288), col("car", 32), A.add, A.min)
+        act(hf, g1, ID, bias=3.0 * RG, scale=-0.5)
+        scan(v("jj", 255, None, -1), v("nb", 288, 32, -1), v("oneb"), col("car", 64), A.min, A.add)
+        tt(uu, g1, v("jj"), A.subtract)
+        tt(cl, hf, v("jj"), A.subtract)
+        tt(vv, uu, cl, A.add)
+        act(v("bu"), uu, F.Relu, bias=3.0 * RG, scale=float(RG))
+        act(v("bv"), vv, F.Relu, bias=2.0 * RG * (3 - 3 * RG), scale=2.0 * RG)
+        tt(sp, v("kt"), hf, A.add)
+        act(un, uu, F.Relu, scale=-float(RG))
+        tt(f2, v("kt"), g1, A.add)
+        tt(s2, sp, un, A.subtract)
+        tt(t1, v("bu"), cl, A.min)
+        act(cl2, cl, ID, bias=3.0 * RG)
+        tt(v("s1"), v("bv"), s2, A.add)
+        ts(v("ob"), ix(v("s1"), v("pt")), 9.0 * RG, None, A.min)
+        tt(xx, f2, t1, A.add)
+        tt(v("s2"), v("bv"), cl2, A.min)
+        tt(v("s4"), v("s2"), xx, A.add)
+        cp(v("oa"), ix(v("s4"), v("pt")))
 
-    def names_p(t):
-        for q in range(4):
-            act(T.gb[:, 1024 * q:1024 * q + 1024], T.win[:].indirect(T.ob[:, 64 * q:64 * q + 64]), F.Copy, WT + ["ob"], [("gb", q)])
-        for u in range(8):
-            out, src = T.ga[:, 512 * u:512 * u + 512], T.win[:].indirect(T.oa[:, 32 * u:32 * u + 32])
-            if u < NVA[t]:
-                cp(out, src, WT + ["oa"], [("ga", u)])
-            else:
-                act(out, src, F.Copy, WT + ["oa"], [("ga", u)])
-        if t > 0:
-            blocks_b()
-        mm(T.pp[:, 0:256], I, T.cm75[:], True, False, ["ib", "cm75"], ["pp"])
-        for s in ("b0", "b1", "a0", "b2", "a1", "b3", "a2", "a3"):
-            q = int(s[1])
-            for c in range(16):
-                if s[0] == "b":
-                    mm(T.pp[:, 64 * q:64 * q + 64], E(5, c), T.gb[:, 1024 * q + c:1024 * q + 1024:16], False, False, ["eb2", ("gb", q)], ["pp"])
-                else:
-                    mm(T.pp[:, 64 * q:64 * q + 64], E(4, c), T.ga[:, 1024 * q + c:1024 * q + 1024:16], False, s == "a3" and c == 15,
-                       ["eb3", ("ga", 2 * q), ("ga", 2 * q + 1)], ["pp"])
-        hi, lo, P = T["hi%d" % t], T["lo%d" % t], T.pp[:, 0:256]
-        ts(T.r16[:], P, M16, M16, A.add, A.subtract, [], ["r16"], ["pp"])
-        act(hi[:], T.r16[:], ID, ["r16"], [("hi", t)], bias=191.53125, scale=1.0 / 256.0)
-        tt(lo[:], P, T.r16[:], A.subtract, ["r16"], [("lo", t)], ["pp"])
-        ts(T.pu[:], P, 7.5, None, A.add, None, [], ["pu"], ["pp"])
-        if t > 0:
-            cp(T.tab[:].indirect(T.cu[:]), T.avg[:], ["avg", "cu"], ["tab"])
+    def pg(w, eng, u0, u1):
+        gather(eng, v("g" + w, 512 * u0, 512 * u1), v("win"), v("o" + w, 32 * u0, 32 * u1))
+
+    def psum_(w, q, first=False, last=False):
+        bn = "px%d" % (q // 2)
+        if w == "b":
+            mm(v(bn, 64 * (q & 1), 64 * (q & 1) + 64), I, v("c2040", 0, 64), first)
+        for c in range(16):
+            mm(v(bn, 64 * (q & 1), 64 * (q & 1) + 64), E(4 if w == "a" else 5, c), v("g" + w, 1024 * q + c, 1024 * q + 1024, 16),
+               False, last and c == 15)
+
+    def half(name, t, h):
+        return v(name, 256 * t + 128 * h, 256 * t + 128 * h + 128)
+
+    def send(t, h):
+        bn = "px%d" % h
+        P, r16, hi, lo = v(bn, 0, 128), half("r16", 0, h), half("hi", t, h), half("lo", t, h)
+        ts(r16, P, M16, M16, A.add, A.subtract)
+        lin(hi, r16, 1.0 / 256.0, 191.53125)
+        tt(lo, P, r16, A.subtract)
         d1, d2 = T.cores[(rank + 1) % n], T.cores[(rank + 2) % n]
         e1, e2 = topo.engines(core, d1)[0::2], topo.engines(core, d2)[1::2]
         trs = []
-        for d, es, src, dst, sm in ((d1, e1, hi, "hin%d", "ah%d"), (d2, e2, lo, "lin%d", "al%d")):
+        for d, es, src, dst, sm in ((d1, e1, hi, "hin", "ah"), (d2, e2, lo, "lin", "al")):
             rid, pid = topo.addr(d)[0:2]
             trs.append(RemoteDMATransfer(dst_ids=[DstId(rid=rid, pnc=pid)], dma_engine_mask=sum(1 << e for e in es),
-                                         remote_sem=T.sem[sm % t], src=src[:], dst=T[dst % t][:]))
-        op("r", lambda: g.remote_dma_fused(trs, local_sem=T.sem["loc%d" % t]), [("hi", t), ("lo", t)], [], sem="loc%d" % t, inc=len(e1) + len(e2))
+                                         remote_sem=T.sem["%s%d%d" % (sm, t, h)], src=src[0], dst=half(dst, t, h)[0]))
+        sent.append(op({"g": (lambda: g.remote_dma_fused(trs, local_sem=T.sem.loc), 0.2)}, [hi, lo], [], sem="loc",
+                       inc=len(e1) + len(e2), after=sent[-1:]))
         p1, p2 = T.cores[(rank - 1) % n], T.cores[(rank - 2) % n]
-        op("x", None, [], [("hin", t)], sem="ah%d" % t, inc=len(topo.engines(p1, core)[0::2]))
-        op("x", None, [], [("lin", t)], sem="al%d" % t, inc=len(topo.engines(p2, core)[1::2]))
+        for nm, sm, es in (("hin", "ah", topo.engines(p1, core)[0::2]), ("lin", "al", topo.engines(p2, core)[1::2])):
+            op({"x": (None, 0.0)}, [], [half(nm, t, h)], sem="%s%d%d" % (sm, t, h), inc=len(es), late=TRAVEL, after=sent[-1:])
+        ts(half("pu", 0, h), P, 7.5, None, A.add)
+        M, D = v(bn, 128, 256), v(bn, 384, 512)
+        mm(M, I, r16, True, False)
+        mm(D, NI, lo, False, False)
+        for o in (M, D):
+            mm(o, v("nib256"), hi, False, False)
 
-    def dist(off, otok, dn, an, sg, first, last, mid):
-        d, a = T[dn], T[an]
-        wa, wr, wd = (0, 2, 1) if sg > 0 else (1, 3, 0)
-        if first:
-            mm(T.pq[:, 0:256], I, T.zb[:, 0:256], True, False, ["ib", "zb"], ["pq"])
-        chunks, mode, ends = [], [], {}
-        for md, k in MODES:
-            chunks.append((md, len(mode), len(mode) + k))
-            mode += [md] * k
-            ends[len(mode) - 1] = k
-        for u in range(8):
-            md, c0 = mode[u], 512 * u
-            if md == "SS":
-                act(d[:, c0:c0 + 512], T.tab[:].indirect(off[:, 32 * u:32 * u + 32]), F.Copy, ["tab", otok], [(dn, u)])
-        for u in range(8):
-            md, c0 = mode[u], 512 * u
-            if md == "SS":
-                bn = "pb%d" % (u & 1)
-                mm(T[bn][:], I, d[:, c0:c0 + 512], True, False, ["ib", (dn, u)], [bn])
-                mm(T[bn][:], T.nib[:], T.z2[:], False, True, ["nib"] + Z2, [bn])
-                act(a[:, c0:c0 + 512], T[bn][:], F.Abs, [], [(an, u)], [bn])
+    def arrive(t, h):
+        bn = "px%d" % h
+        for c0 in (128, 384):
+            mm(v(bn, c0, c0 + 128), v("ib256", 112, 240), half("hin", t, h), False, False)
+            mm(v(bn, c0, c0 + 128), v("ib", 96, 224), half("lin", t, h), False, c0 == 384)
+
+    def moff(h):
+        ts(half("mu", 0, h), v("px%d" % h, 128, 256), 7.5, None, A.add)
+
+    def dgather(k, h, who):
+        off, d, a = (("pu", "d3", "a3"), ("mu", "d4", "a4"))[k]
+        for j, md in enumerate((DP, DM)[k][h]):
+            u = 4 * h + j
+            c0 = 512 * u
+            src = ix(v("tab"), v(off, 32 * u, 32 * u + 32))
+            if md[0] != who:
+                continue
+            if who == "S":
+                act(v(d, c0, c0 + 512), src, F.Copy)
             else:
-                tt(d[:, c0:c0 + 512], T.tab[:].indirect(off[:, 32 * u:32 * u + 32]), T.z2[:], A.subtract, ["tab", otok] + Z2, [(dn, u)])
-                if md == "VS":
-                    act(a[:, c0:c0 + 512], d[:, c0:c0 + 512], F.Abs, [(dn, u)], [(an, u)])
-                elif u in ends:
-                    u0 = u + 1 - ends[u]
-                    ts(a[:, 512 * u0:c0 + 512], d[:, 512 * u0:c0 + 512], 0.0, None, A.max, None, [(dn, j) for j in range(u0, u + 1)],
-                       [(an, j) for j in range(u0, u + 1)])
-        todo = []
-        for x in ORDER:
-            md, u0, u1 = chunks[int(x[1])]
-            todo.append((u0, u1, d, dn, wd) if x[0] == "d" else (u0, u1, a, an, wr if md == "VV" else wa))
-        for j, (u0, u1, buf, nm, w) in enumerate(todo):
-            if j == len(todo) - 2 and mid is not None:
-                mid()
+                tt(v(d, c0, c0 + 512), src, v("z2"), A.subtract)
+                if md == "VV" and j & 1:
+                    ts(v(a, c0 - 512, c0 + 512), v(d, c0 - 512, c0 + 512), 0.0, None, A.max)
+
+    def dabs(k, h):
+        d, a = (("d3", "a3"), ("d4", "a4"))[k]
+        for j, md in enumerate((DP, DM)[k][h]):
+            c0 = 512 * (4 * h + j)
+            if md == "SS":
+                b = v(nextb())
+                mm(b, I, v(d, c0, c0 + 512), True, False)
+                mm(b, NI, v("z2"), False, True)
+                act(v(a, c0, c0 + 512), b, F.Abs)
+            elif md == "VS":
+                act(v(a, c0, c0 + 512), v(d, c0, c0 + 512), F.Abs)
+
+    def dsums(k, h):
+        d, a = (("d3", "a3"), ("d4", "a4"))[k]
+        wa, wr, wd = ((1, 3, 0), (0, 6, 1))[k]
+        bn, modes = "pq%d" % h, (DP, DM)[k][h]
+        todo = [(q, d, wd) for q in range(2) if modes[2 * q] == "VV"]
+        todo += [(q, a, wr if modes[2 * q] == "VV" else wa) for q in range(2)]
+        for j, (q, buf, w) in enumerate(todo):
+            c0 = 2048 * h + 1024 * q
             for c in range(16):
-                mm(T.pq[:, 32 * u0:32 * u1], E(w, c), buf[:, 512 * u0 + c:512 * u1:16], False,
-                   last and j == len(todo) - 1 and c == 15, ["eb", ("ebw", w)] + [(nm, u) for u in range(u0, u1)], ["pq"])
+                mm(v(bn, 64 * q, 64 * q + 64), E(w, c), v(buf, c0 + c, c0 + 1024, 16), k == 0 and j == 0 and c == 0)
 
-    def choice(t):
-        hi, lo, hin, lin = T["hi%d" % t], T["lo%d" % t], T["hin%d" % t], T["lin%d" % t]
-        Mp, Dp = T.pmm[:, 0:256], T.pd[:, 0:256]
-        mm(Mp, I, T.r16[:], True, False, ["ib", "r16"], ["pmm"])
-        mm(Mp, T.nib256[:], hi[:], False, False, ["nib256", ("hi", t)], ["pmm"])
-        mm(Dp, T.nib[:], lo[:], True, False, ["nib", ("lo", t)], ["pd"])
-        mm(Dp, T.nib256[:], hi[:], False, False, ["nib256", ("hi", t)], ["pd"])
+    def choose(h):
+        bn = "px%d" % h
+        ts(half("sg", 0, h), v("pq%d" % h, 0, 128), 0.0, None, A.is_lt)
+        tt(half("s2", 0, h), half("sg", 0, h), v(bn, 384, 512), A.mult)
+        tt(half("s3", 0, h), half("s2", 0, h), v(bn, 0, 128), A.add)
 
-        def mid():
-            mm(Mp, T.ib256[:, 112:240], hin[:], False, False, ["ib256", ("hin", t)], ["pmm"])
-            mm(Mp, T.ib[:, 96:224], lin[:], False, True, ["ib", ("lin", t)], ["pmm"])
-            mm(Dp, T.ib256[:, 112:240], hin[:], False, False, ["ib256", ("hin", t)], ["pd"])
-            mm(Dp, T.ib[:, 96:224], lin[:], False, True, ["ib", ("lin", t)], ["pd"])
-        dist(T.pu, "pu", "d3", "a3b", -1, True, False, mid)
-        if t == 0:
-            consts_s2()
-        ts(T.mu[:], Mp, 7.5, None, A.add, None, [], ["mu"], ["pmm"])
-        dist(T.mu, "mu", "d4", "a4b", 1, False, True, None)
-        ts(T.s1[:], T.pq[:, 0:256], 0.0, None, A.is_lt, None, [], ["s1"], ["pq"])
-        tt(T.s2[:], T.s1[:], Dp, A.mult, ["s1"], ["s2"], ["pd"])
-        tt(T.s3[:], T.s2[:], T.pp[:, 0:256], A.add, ["s2"], ["s3"], ["pp"])
+    def threshold(t):
+        b = v(nextb(), 0, 1)
+        act(v("hh"), v("sg"), ID, acc=col("acc", 0))
+        mm(b, v("bo"), col("acc", 0), True, False)
+        cp(col("ai", 0), b)
+        ts(col("ai", 8), col("ai", 0), 31, None, A.bitwise_and)
+        ts(col("thb", 0), col("ai", 8), col("thp", t), BIG / 2, A.add, A.mult)
 
-    stage_x(0, consts_v)
+    consts_v()
+    first_x()
+    for j in range(FIRST, 32):
+        if FILLER[j] in "vs":
+            fill(j, j + 1)
+    window(0)
+    consts_s()
     for t in range(3):
         periods(t)
-        names_p(t)
-        choice(t)
+        for h in range(2):
+            if t > 0 and h == 1:
+                blocks_a()
+                blocks_b()
+                update()
+            for w in "ba":
+                for who, u0, u1 in calls(PG[min(t, 1)][w], 4 * h, 4 * h + 4):
+                    pg(w, who, u0, u1)
+            for q in (2 * h, 2 * h + 1):
+                for w in "ba":
+                    psum_(w, q, first=w == "b" and q == 2 * h)
+            send(t, h)
+        for k, h in DORDER:
+            if k == 1:
+                arrive(t, h)
+                moff(h)
+            dgather(k, h, "S")
+            dgather(k, h, "V")
+            dabs(k, h)
+            dsums(k, h)
+            if k == 1:
+                choose(h)
         if t < 2:
-            act(T.s4[:], T.s1[:], ID, ["s1"], ["s4", "acc"], acc=T.acc[:, 0:1])
-            ts(T.nu[:], T.s3[:].indirect(T.pt[:]), 7.5, None, A.add, None, ["s3", "pt"], ["nu"])
-            mm(T.pd[:, 336:337], T.bo[:], T.acc[:, 0:1], True, True, ["bo", "acc"], ["pd"])
-
-            def prep(t=t):
-                cp(T.ai[:, 0:1], T.pd[:, 336:337], [], ["ai0"], ["pd"])
-                cp(T.ni[:], T.nu[:], ["nu"], ["ni"])
-                ts(T.ai[:, 1:2], T.ai[:, 0:1], 31, None, A.bitwise_and, None, ["ai0"], ["ai1"])
-                digits(T.nu[:], "nu")
-                window(t + 1)
-                tt(T.thr[:, 0:1], T.ai[:, 1:2], T.thf[:, t + 1:t + 2], A.add, ["ai1", "thf"], ["thr"])
-            stage_x(t + 1, prep)
+            ts(v("nu"), ix(v("s3"), v("pt")), 7.5, None, A.add)
+            for j, u in enumerate(XORDER):
+                xg(u, u + 1, XG[j])
+                if j == DIGITS:
+                    digits(v("s3"), True)
+                    window(t + 1)
+                    threshold(t + 1)
+            for j in range(8):
+                piece(j)
+                if j & 1:
+                    dsum(j // 2)
+            begins(0, 192, v("px0", 0, 192))
+            begins(192, 256, v("px1", 0, 64))
             for c in range(16):
                 yscan(c)
-    ts(T.s5[:], T.s3[:].indirect(T.pt[:]), 7.5, None, A.add, None, ["s3", "pt"], ["s5"])
-    turn(T.s5[:], "s5", T.s4[:], "s4")
-    cp(T.nu[:], T.s4[:].indirect(T.pt[:]), ["s4", "pt"], ["nu"])
-    parts = [("s", a, c) for a, c in cuts(FINV, 256)] + [("v", a, c) for a, c in cuts(0, FINV)]
-    for e, a, c in parts:
-        gather_x(e, a, c)
-    nv = FINV // 32
-    seq = []
-    for j in range(8):
-        seq += ([j] if j < nv else []) + ([nv + j] if nv + j < 8 else [])
-    for u in seq:
-        dma("y", T.xy[:, 512 * u:512 * u + 512], T.xb[:, 16 + 512 * u:16 + 512 * u + 512], xt(512 * u, 512 * u + 512), [], "oxy")
+    turn(v("s3"))
+    ts(v("nu"), ix(v("w2"), v("sell")), 7.5, None, A.add)
+    lin(v("lyf"), ix(v("w2"), v("sell")), 1.0, 7.5)
+    dma("y", T.ly[:], v("lyf"), "oly", 128)
+    for who, u0, u1 in calls(XL, 0, 8):
+        xg(u0, u1, who)
     for u in range(8):
-        scan(T.tmp[:, 512 * u:512 * u + 512], T.ym[:], T.xb[:, 16 + 512 * u:16 + 512 * u + 512], 0.0, A.mult, A.max,
-             ["ym"] + xt(512 * u, 512 * u + 512), [("tmp", 2 * u), ("tmp", 2 * u + 1)])
-        if u == 5:
-            cp(T.lyf[:], T.s4[:].indirect(T.pt[:]), ["s4", "pt"], ["lyf"])
-            dma("y", T.ly[:], T.lyf[:], ["lyf"], [], "oly")
-    mm(T.pb0[:, 0:256], T.nib[:], T.zc[:], True, False, ["nib", "zc"], ["pb0"])
-    mm(T.pb0[:, 0:256], I, Y, False, True, ["ib"] + TY, ["pb0"])
-    act(T.zd[:], T.pb0[:, 0:256], F.Abs, [], ["zd"], ["pb0"])
-    dma("s", T.zy[:], T.zd[:], ["zd"], [], "ozy")
+        moved["oxy"] = 0
+        dma("y", T.xy[:, 512 * u:512 * u + 512], X(512 * u, 512 * u + 512), "oxy", 128)
+        scan(v("tmp", 512 * u, 512 * u + 512), v("ym16"), X(512 * u, 512 * u + 512), 0.0, A.mult, A.max)
+    mm(v("pb0", 0, 256), NI, v("zc"), True, False)
+    mm(v("pb0", 0, 256), I, v("tmp", 15, 4096, 16), False, True)
+    act(v("zd"), v("pb0", 0, 256), F.Abs)
+    dma("s", T.zy[:], v("zd"), "ozy", 64)
 
     queue = {"v": V, "s": S, "t": PE, "g": g, "r": g, "y": g.sync}
     esem = {"v": "cv", "s": "cs", "t": "ct", "g": "cg"}
+    if not PLAN:
+        PLAN.extend([arrange(ops), [o["eng"] for o in ops]])
+    order = PLAN[0]
+    for o, e in zip(ops, PLAN[1]):
+        o["eng"] = e
+    place = {i: j for j, i in enumerate(order)}
+    ends["first"] = {min(x, key=place.get) for gs in sums.values() for x in gs if x}
+    ends["last"] = {max(x, key=place.get) for gs in sums.values() for x in gs if x}
     total, need = {}, set()
     for o in ops:
         if o["sem"] is not None:
             total[o["sem"]] = total.get(o["sem"], 0) + o["inc"]
         best = {}
         for d in o["deps"]:
-            if ops[d]["sem"] is None:
-                best[ops[d]["eng"]] = max(best.get(ops[d]["eng"], -1), d)
+            e = ops[d]["eng"]
+            if ops[d]["sem"] is None and (e not in best or place[d] > place[best[e]]):
+                best[e] = d
         o["deps"] = [d for d in o["deps"] if ops[d]["sem"] is not None] + list(best.values())
         need.update(best.values())
     cnt, seen = {}, {}
-    for i, o in enumerate(ops):
+    for i in order:
+        o = ops[i]
         if o["eng"] == "x":
             continue
-        qn = "g" if o["eng"] == "r" else o["eng"]
-        q = queue[o["eng"]]
+        qn = o["eng"]
+        q = queue[qn]
         for d in o["deps"]:
             p = ops[d]
             sm, val = (p["sem"], total[p["sem"]]) if p["sem"] is not None else (esem[p["eng"]], p["n"])
             if seen.get((qn, sm), 0) < val:
                 q.wait_ge(T.sem[sm], val)
                 seen[(qn, sm)] = val
-        ins = o["fn"]()
-        if o["eng"] == "r":
+        ins = o["alt"][qn][0]()
+        if o["sem"] == "loc":
             continue
         if o["sem"] is not None:
             ins.then_inc(T.sem[o["sem"]], 16)

@@ -19,9 +19,9 @@ SCRATCH = {
     "win": sb(WIN, bf), "tab": sb(4096, bf), "ga": sb(4096, bf), "gb": sb(4096, bf),
     "d3": sb(4096, bf), "a3": sb(4096, bf), "d4": sb(4096, bf), "a4": sb(4096, bf), "tmp": sb(4096, bf),
     "zb": sb(1024, bf), "ym8": sb(512, bf), "ym16": sb(512, bf), "li": sb(256, i32), "thi": sb(8, i32), "th8": sb(8, f32),
-    "thp": sb(8, f32), "thb": sb(8, f32), "zc": sb(256, bf), "z2": sb(512, bf), "zd": sb(256, bf), "zs": sb(256, f32), "avg": sb(256, bf),
+    "thp": sb(8, f32), "thb": sb(8, f32), "zc": sb(256, bf), "z2": sb(2048, bf), "avi": sb(256, i32), "zd": sb(256, bf), "zs": sb(256, f32), "avg": sb(256, bf),
     "pint": sb(8, i32), "pf": sb(32, f32), "colf": sb(16, f32), "dupf": sb(32, f32), "selff": sb(16, f32), "tcol": sb(72, f32),
-    "pt": sb(16, u16), "pt2": sb(16, u16), "dup": sb(32, u16), "selc": sb(16, u16), "sell": sb(16, u16),
+    "pt": sb(16, u16), "pta": sb(16, u16), "ptb": sb(16, u16), "dup2": sb(32, u16), "lf": sb(64, f32), "dup": sb(32, u16), "selc": sb(16, u16), "sell": sb(16, u16),
     "cb": sb(16, f32), "ib": sb(256, bf), "ib256": sb(256, bf), "nib": sb(128, bf), "nib256": sb(128, bf), "ib2": sb(128, bf),
     "ibh": sb(128, bf), "ib16": sb(128, bf), "nib16": sb(128, bf),
     "eb": sb(7 * 144, bf), "bo": sb(128, f32), "bob": sb(128, bf), "oneb": sb(256, bf),
@@ -47,17 +47,18 @@ CELLS = [(3, 1, 1, 0), (4, 2, 1, 0), (3, 2, 1, 1), (3, 5, 2, 0), (4, 7, 2, 0), (
          (1, 0, 0, 1), (2, 0, 0, 2), (0, 1, 0, 0), (1, 1, 0, 1), (0, 2, 0, 0), (0, 4, 0, 0), (1, 4, 1, 0), (2, 4, 2, 0),
          (1, 3, 1, 1), (2, 3, 1, 2), (0, 5, 1, 0), (1, 5, 1, 1), (0, 7, 1, 0), (1, 9, 2, 1), (2, 9, 2, 2)]
 FILLED, FILLER, FIRST = (9, 0, 3, 1, 2, 4, 5, 7), "ssss" "yyyy" "gggg" "yyyy" "vvvv" "ssss" "gggv" "vvvs", 4
-DP = (("VS", "VS", "VS", "VS"), ("SS", "SS", "VS", "VS"))
-DM = (("VS", "VS", "VS", "VS"), ("SS", "VS", "VV", "VV"))
-DORDER = ((0, 0), (0, 1), (1, 0), (1, 1))
-PG = ({"b": "sSsSsSsS", "a": "vVvVvVvV"}, {"b": "sSsSsSsS", "a": "vVvVsSsS"})
-X0, XG, XL = "svvsvvsv", "svvsvvsv", "svsvsvsv"
-XORDER, DIGITS, DX = (7, 0, 1, 2, 3, 4, 5, 6), 3, "tttttttt"
+DP = (("SS", "VS", "SS", "VS"), ("VS", "VS", "VS", "VS"))
+DM = (("SS", "VS", "VS", "VS"), ("VS", "VS", "VV", "VV"))
+DORDER, JOIN = ((0, 0), (0, 1), (1, 0), (1, 1)), "11110011"
+STORES = ((0, 2), (2, 4), (4, 6), (6, 7), (7, 8))
+PG = ({"b": "sSsSsSsS", "a": "vVvVvVvV"}, {"b": "sssSsSsS", "a": "svvVvVsS"})
+X0, XG, XL, ZCUT = "svsvsvsv", "ssssvssv", "vsvsvsss", 192
+XORDER, DIGITS, DX = (0, 1, 2, 3, 7, 4, 5, 6), 2, "tttttttt"
 
 
 CYCLE, PECYCLE, GATHER, SCATTER, FIXV, FIXS, WAKE = 0.00083, 0.00042, 1.56, 3.5, 0.03, 0.06, 0.19
 DMA0, DMARATE, TRAVEL, EARLY, SWEEPS = 1.6, 250.0, 4.0, 0.0, 3
-INFO, PLAN = [], []
+INFO, PLAN, STARTS = [], [], 1
 
 
 def arrange(ops):
@@ -71,7 +72,7 @@ def arrange(ops):
         o = ops[i]
         way[i] += min(c for _, c in o["alt"].values()) + o["late"] + 1e-6 + o.get("early", 0.0)
         for d in pred[i]:
-            way[d] = max(way[d], way[i] + (0 if d in o["after"] else WAKE))
+            way[d] = max(way[d], way[i] + (-ops[d]["late"] if d in o["after"] else WAKE))
     before = [[(d, -ops[d]["late"] if d in o["after"] else WAKE) for d in pred[i]] for i, o in enumerate(ops)]
     behind = [[] for _ in ops]
     for i, lst in enumerate(before):
@@ -97,13 +98,14 @@ def arrange(ops):
             eng[i], start[i], end[i] = best[2], best[1], best[0] + (0.0 if back else o["late"]) + 1e-6
         return max(end.values()), start, end, eng
 
-    best = now = sweep(range(len(ops)), before, False)
-    INFO.append(best[0])
-    for _ in range(SWEEPS):
-        rev = sweep(sorted(range(len(ops)), key=lambda j: (-now[1][j], -j)), behind, True)
-        now = sweep(sorted(range(len(ops)), key=lambda j: (-rev[1][j], j)), before, False)
-        best = min(best, now, key=lambda x: x[0])
-        INFO.append(now[0])
+    best = None
+    for first in (range(len(ops)), sorted(range(len(ops)), key=lambda j: (-way[j], j)))[:STARTS]:
+        now = sweep(first, before, False)
+        for _ in range(SWEEPS):
+            rev = sweep(sorted(range(len(ops)), key=lambda j: (-now[1][j], -j)), behind, True)
+            now = sweep(sorted(range(len(ops)), key=lambda j: (-rev[1][j], j)), before, False)
+            best = min(best or now, now, key=lambda x: x[0])
+            INFO.append(now[0])
     for i, o in enumerate(ops):
         o["eng"] = best[3][i]
     return sorted(range(len(ops)), key=lambda j: (best[1][j], j))
@@ -278,6 +280,9 @@ def rank_program(g, core, T, topo):
     sel(v("bob"), v("bob"), [[16, 8], [0, 16]], A.is_ge, 15, -1)
     iota(v("tcol"), [[1, 72]], 0, 0)
     iota(v("kt"), [[1, 256]], 0, 0)
+    iota(v("lf", 0, 16), [[128, 2], [2, 8]], 0, 0)
+    iota(v("lf", 16, 32), [[128, 2], [1, 8]], 0, 0)
+    iota(v("lf", 32, 64), [[128, 2], [1, 8], [0, 2]], 0, 0)
     B8 = v("bob", 0, 128, 16)
     moved["fill"] = 1200
 
@@ -301,8 +306,7 @@ def rank_program(g, core, T, topo):
     lin(NI, I, -1.0)
     ts(col("pint", 1), col("pint", 0), 15, None, A.bitwise_and)
     ts(col("pint", 2), col("pint", 0), 31, None, A.bitwise_and)
-    ts(col("pint", 4), col("pint", 0), 15.0, None, A.add)
-    ts(col("pint", 3), col("pint", 4), 15, None, A.bitwise_and)
+    ts(col("pint", 3), col("pint", 0), 7, None, A.bitwise_and)
     cp(v("pf", 0, 4), v("pint", 0, 4))
     PC, PJ = col("pf", 1), col("pf", 2)
     ts(v("pf", 8, 12), v("pf", 0, 4), 16.0, None, A.mult)
@@ -310,20 +314,20 @@ def rank_program(g, core, T, topo):
     ts(v("selc"), v("selff"), PJ, None, A.add)
     ts(v("pt"), v("colf"), col("pf", 9), None, A.add)
 
-    def turn(src):
-        cp(v("w1"), ix(src, v("dup")))
-        vtr(v("w2"), v("w1"))
+    def turn(src, dup, c0, c1):
+        lin(v("w1", c0, c1), ix(src, dup), who="vs" if src[3] == f32 else "v")
+        vtr(v("w2", c0, c1), v("w1", c0, c1))
 
-    def digits(src, perm):
-        a = ix(src, v("pt")) if perm else src
-        ts(v("r32"), a, M16, M16, A.add, A.subtract)
-        lin(v("hh"), v("r32"), 1.0 / 256.0, 191.53125)
-        lin(v("dig", 0, 256), v("hh"), 1.0, -199.5)
-        tt(v("dig", 512, 768), a, v("r32"), A.subtract)
-        b = v(nextb(), 0, 256)
-        mm(b, v("ib16"), v("r32"), True, False)
-        mm(b, v("nib16"), v("dig", 0, 256), False, True)
-        lin(v("dig", 256, 512), b, 1.0, -127.5)
+    def digits(a, c0, c1):
+        r, d0 = v("r32", c0, c1), v("dig", c0, c1)
+        ts(r, a, M16, M16, A.add, A.subtract)
+        lin(v("hh", c0, c1), r, 1.0 / 256.0, 191.53125)
+        lin(d0, v("hh", c0, c1), 1.0, -199.5)
+        tt(v("dig", 512 + c0, 512 + c1), a, r, A.subtract)
+        b = v(nextb(), c0, c1)
+        mm(b, v("ib16"), r, True, False)
+        mm(b, v("nib16"), d0, False, True)
+        lin(v("dig", 256 + c0, 256 + c1), b, 1.0, -127.5)
 
     def window(t):
         def row(pl, sh):
@@ -341,9 +345,9 @@ def rank_program(g, core, T, topo):
             dma("y", v("win", RG * rg, RG * rg + RG - sh, None, slice(pa, 128, 16)), row(pl, sh), "lb%d" % t, 64)
 
     cp(v("nu"), v("li"))
-    turn(v("li"))
+    turn(v("li"), v("dup"), 0, 512)
     lin(v("s4"), ix(v("w2"), v("selc")), 1.0, -7.5)
-    digits(v("s4"), False)
+    digits(v("s4"), 0, 256)
     for j in range(FIRST):
         if FILLER[j] in "vs":
             fill(j, j + 1)
@@ -353,15 +357,19 @@ def rank_program(g, core, T, topo):
     mm(v("pq0", 0, 8), v("bo"), v("th8"), True, True)
 
     def ztile():
-        lin(v("z2", 0, 256), ix(v("zc"), v("pt")))
-        lin(v("z2", 256, 512), v("z2", 0, 256))
+        for h in range(2):
+            c0 = 1024 * h
+            lin(v("z2", c0, c0 + 128), ix(v("zc"), v("pt", 8 * h, 8 * h + 8)))
+            for w in (128, 256, 512):
+                sel(v("z2", c0 + w, c0 + 2 * w), v("z2", c0, c0 + w), [[0, w]], A.is_gt, 1, 0)
 
     def consts_v():
         t, d, e = v("tcol", 0, 65), v("cd", 0, 65), v("ce", 0, 65)
         ts(v("thp"), v("pq0", 0, 8), 0.5, None, A.add)
         ts(col("thb", 0), col("thp", 0), BIG / 2, None, A.mult)
         ts(col("pf", 12), PC, 256.0, None, A.mult)
-        ts(v("kt"), v("kt"), col("pf", 12), None, A.add)
+        for h in range(2):
+            lin(v("px%d" % h, 256, 384), v("kt", 128 * h, 128 * h + 128), 1.0, col("pf", 12))
         ms(v("nb"), BIG)
         ms(v("three"), 0.0)
         ms(v("zadd"), 0.0)
@@ -387,6 +395,8 @@ def rank_program(g, core, T, topo):
         tt(col("cd", 64), col("cd", 64), col("pf", 19), A.add)
         lin(col("ht", 64), PC, -256.0, 3840.0)
         lin(EW(2), B8, -BIG / 2)
+        ts(col("pf", 28), PC, 8.0, col("pf", 11), A.is_ge, A.add)
+        ts(v("pta"), v("lf", 0, 16), col("pf", 28), None, A.add)
 
     def consts_s():
         for j in range(5):
@@ -406,6 +416,9 @@ def rank_program(g, core, T, topo):
         lin(v("cb"), v("colf"), 256.0, col("pf", 9))
         lin(v("ym16"), v("zb", 0, 512), 1.0, 1.0)
         lin(v("ym16", 0, 512, 16), v("zb", 0, 32))
+        lin(col("pf", 29), PC, 8.0)
+        ts(v("ptb"), v("lf", 16, 32), col("pf", 29), None, A.add)
+        ts(v("dup2"), v("lf", 32, 64), col("pf", 29), None, A.add)
         ts(col("pf", 17), PC, 31.0, PJ, A.mult, A.add)
         ts(v("sell"), v("colf"), col("pf", 17), None, A.add)
 
@@ -462,9 +475,9 @@ def rank_program(g, core, T, topo):
     def dsum(q):
         out = v("px0", 64 * q, 64 * q + 64) if q < 3 else v("px1", 0, 64)
         if q == 0:
-            mm(out, I, v("dinit", 0, 64), True, False)
+            mm(out, I, v("dinit", 0, 64))
         for c in range(16):
-            mm(out, E(2, c), G(1024 * q + c, 1024 * q + 1024, 16), q == 3 and c == 0)
+            mm(out, E(2, c), G(1024 * q + c, 1024 * q + 1024, 16), q & 1 and c == 0)
 
     Y = v("tmp", 15, 4096, 16)
 
@@ -482,8 +495,7 @@ def rank_program(g, core, T, topo):
             mm(v(b2, 256, 272), E(0, b), v("tmp", 15 + 16 * b, 4096, 256))
         act(v("zc"), v(b1, 0, 256), F.Abs)
         ztile()
-        lin(v("zs"), v(b2, 0, 256), 0.5, M1)
-        lin(v("avg"), v("zs"), 1.0, -M1)
+        ts(v("avi"), v(b2, 0, 256), 0.5, None, A.mult)
 
     def blocks_b():
         cp(v("ui", 0, 16), v("pq1", 256, 272))
@@ -492,36 +504,38 @@ def rank_program(g, core, T, topo):
         cp(v("cu"), v("uf"))
 
     def update():
-        cp(ix(v("tab"), v("cu")), v("avg"))
+        cp(ix(v("tab"), v("cu")), v("avi"))
 
     def periods(t):
-        g1, hf, un, cl, cl2 = v("pb0", 0, 256), v("pb1", 0, 256), v("pb1", 256, 512), v("pb2", 0, 256), v("pb3", 0, 256)
-        s2, t1, xx = v("pb0", 256, 512), v("px0", 0, 256), v("px0", 256, 512)
-        f2, uu, sp, vv = v("f2"), v("uu"), v("sp"), v("vv")
         scan(v("hb", 0, 288), v("three"), v("nb", 32, 320), BIG, A.add, A.min)
         scan(v("hb", 575, 287, -1), v("zadd"), v("nb", 287, None, -1), BIG, A.add, A.min)
         vtr(v("ht", 0, 64), v("hb", 256, 320))
         scan(v("car", 0, 65), v("cd", 0, 65), v("ht", 0, 65), BIG, A.add, A.min)
-        scan(g1, v("three", 0, 256), v("nb", 32, 288), col("car", 32), A.add, A.min)
-        act(hf, g1, ID, bias=3.0 * RG, scale=-0.5)
-        scan(v("jj", 255, None, -1), v("nb", 288, 32, -1), v("oneb"), col("car", 64), A.min, A.add)
-        tt(uu, g1, v("jj"), A.subtract)
-        tt(cl, hf, v("jj"), A.subtract)
-        tt(vv, uu, cl, A.add)
-        act(v("bu"), uu, F.Relu, bias=3.0 * RG, scale=float(RG))
-        act(v("bv"), vv, F.Relu, bias=2.0 * RG * (3 - 3 * RG), scale=2.0 * RG)
-        tt(sp, v("kt"), hf, A.add)
-        act(un, uu, F.Relu, scale=-float(RG))
-        tt(f2, v("kt"), g1, A.add)
-        tt(s2, sp, un, A.subtract)
-        tt(t1, v("bu"), cl, A.min)
-        act(cl2, cl, ID, bias=3.0 * RG)
-        tt(v("s1"), v("bv"), s2, A.add)
-        ts(v("ob"), ix(v("s1"), v("pt")), 9.0 * RG, None, A.min)
-        tt(xx, f2, t1, A.add)
-        tt(v("s2"), v("bv"), cl2, A.min)
-        tt(v("s4"), v("s2"), xx, A.add)
-        cp(v("oa"), ix(v("s4"), v("pt")))
+        scan(v("jj"), v("three", 0, 256), v("nb", 32, 288), col("car", 32), A.add, A.min)
+        scan(v("pb0", 255, None, -1), v("nb", 288, 32, -1), v("oneb"), col("car", 64), A.min, A.add)
+        for h in range(2):
+            i2, hf, uu, vv, f2, un, bu, bv, s1, s2, s4 = [half(x, 0, h) for x in "jj sp uu vv f2 hh bu bv s1 s2 s4".split()]
+            J, sp, k = half("pb0", 0, h), half("pb0", 1, h), v("px%d" % h, 256, 384)
+            cl, cl2, t1 = v("pb%d" % (2 + h), 0, 128), v("pb%d" % (2 + h), 128, 256), half("pb1", 0, h)
+            upto = (lambda x: v(x, 0, 128 * h + 128))
+            lin(hf, i2, -0.5, 3.0 * RG)
+            tt(uu, i2, J, A.subtract)
+            tt(cl, hf, J, A.subtract)
+            tt(vv, uu, cl, A.add)
+            act(un, uu, F.Relu, scale=-float(RG))
+            act(bv, vv, F.Relu, bias=2.0 * RG * (3 - 3 * RG), scale=2.0 * RG)
+            act(bu, uu, F.Relu, bias=3.0 * RG, scale=float(RG))
+            tt(sp, hf, k, A.add)
+            tt(sp, sp, un, A.subtract)
+            tt(s1, bv, sp, A.add)
+            ts(half("ob", 0, h), ix(upto("s1"), v("pta", 8 * h, 8 * h + 8)), 9.0 * RG, None, A.min)
+            tt(f2, i2, k, A.add)
+            tt(t1, bu, cl, A.min)
+            lin(cl2, cl, 1.0, 3.0 * RG)
+            tt(t1, f2, t1, A.add)
+            tt(s2, bv, cl2, A.min)
+            tt(s4, s2, t1, A.add)
+            cp(half("oa", 0, h), ix(upto("s4"), v("pta", 8 * h, 8 * h + 8)))
 
     def pg(w, eng, u0, u1):
         gather(eng, v("g" + w, 512 * u0, 512 * u1), v("win"), v("o" + w, 32 * u0, 32 * u1))
@@ -573,30 +587,39 @@ def rank_program(g, core, T, topo):
 
     def dgather(k, h, who):
         off, d, a = (("pu", "d3", "a3"), ("mu", "d4", "a4"))[k]
-        for j, md in enumerate((DP, DM)[k][h]):
-            u = 4 * h + j
-            c0 = 512 * u
-            src = ix(v("tab"), v(off, 32 * u, 32 * u + 32))
+        for md, u0, u1 in spans(k, h):
+            c0, c1 = 512 * u0, 512 * u1
+            src = ix(v("tab"), v(off, 32 * u0, 32 * u1))
             if md[0] != who:
                 continue
             if who == "S":
-                act(v(d, c0, c0 + 512), src, F.Copy)
+                act(v(d, c0, c1), src, F.Copy)
             else:
-                tt(v(d, c0, c0 + 512), src, v("z2"), A.subtract)
-                if md == "VV" and j & 1:
-                    ts(v(a, c0 - 512, c0 + 512), v(d, c0 - 512, c0 + 512), 0.0, None, A.max)
+                tt(v(d, c0, c1), src, v("z2", 1024 * h, 1024 * h + c1 - c0), A.subtract)
+                if md == "VV" and not u1 & 1:
+                    ts(v(a, c1 - 1024, c1), v(d, c1 - 1024, c1), 0.0, None, A.max)
+
+    def spans(k, h):
+        modes, out = (DP, DM)[k][h], []
+        for q in range(2):
+            u = 4 * h + 2 * q
+            if modes[2 * q] == modes[2 * q + 1] and JOIN[4 * k + 2 * h + q] == "1":
+                out.append((modes[2 * q], u, u + 2))
+            else:
+                out += [(modes[2 * q], u, u + 1), (modes[2 * q + 1], u + 1, u + 2)]
+        return out
 
     def dabs(k, h):
         d, a = (("d3", "a3"), ("d4", "a4"))[k]
-        for j, md in enumerate((DP, DM)[k][h]):
-            c0 = 512 * (4 * h + j)
+        for md, u0, u1 in spans(k, h):
             if md == "SS":
-                b = v(nextb())
-                mm(b, I, v(d, c0, c0 + 512), True, False)
-                mm(b, NI, v("z2"), False, True)
-                act(v(a, c0, c0 + 512), b, F.Abs)
+                for c0 in range(512 * u0, 512 * u1, 512):
+                    b = v(nextb())
+                    mm(b, I, v(d, c0, c0 + 512), True, False)
+                    mm(b, NI, v("z2", 1024 * h, 1024 * h + 512), False, True)
+                    act(v(a, c0, c0 + 512), b, F.Abs)
             elif md == "VS":
-                act(v(a, c0, c0 + 512), v(d, c0, c0 + 512), F.Abs)
+                act(v(a, 512 * u0, 512 * u1), v(d, 512 * u0, 512 * u1), F.Abs)
 
     def dsums(k, h):
         d, a = (("d3", "a3"), ("d4", "a4"))[k]
@@ -634,6 +657,8 @@ def rank_program(g, core, T, topo):
         periods(t)
         for h in range(2):
             if t > 0 and h == 1:
+                for c in range(16):
+                    yscan(c)
                 blocks_a()
                 blocks_b()
                 update()
@@ -654,35 +679,39 @@ def rank_program(g, core, T, topo):
             dsums(k, h)
             if k == 1:
                 choose(h)
+                names = ix(half("s3", 0, 0) if h == 0 else v("s3"), v("ptb", 8 * h, 8 * h + 8))
+                if t == 2:
+                    turn(half("s3", 0, 0) if h == 0 else v("s3"), v("dup2", 16 * h, 16 * h + 16), 256 * h, 256 * h + 256)
+                    continue
+                ts(half("nu", 0, h), names, 7.5, None, A.add)
+                for j in range(4 * h, 4 * h + 4):
+                    xg(XORDER[j], XORDER[j] + 1, XG[j])
+                    if j % 4 == DIGITS:
+                        digits(names, 128 * h, 128 * h + 128)
+                        if h == 1:
+                            window(t + 1)
+                            threshold(t + 1)
+                for j in ((1, 2, 3), (0, 4, 5, 6, 7))[h]:
+                    piece(j)
+                    if j in (0, 3, 5, 7):
+                        dsum(j // 2)
         if t < 2:
-            ts(v("nu"), ix(v("s3"), v("pt")), 7.5, None, A.add)
-            for j, u in enumerate(XORDER):
-                xg(u, u + 1, XG[j])
-                if j == DIGITS:
-                    digits(v("s3"), True)
-                    window(t + 1)
-                    threshold(t + 1)
-            for j in range(8):
-                piece(j)
-                if j & 1:
-                    dsum(j // 2)
             begins(0, 192, v("px0", 0, 192))
             begins(192, 256, v("px1", 0, 64))
-            for c in range(16):
-                yscan(c)
-    turn(v("s3"))
     ts(v("nu"), ix(v("w2"), v("sell")), 7.5, None, A.add)
     lin(v("lyf"), ix(v("w2"), v("sell")), 1.0, 7.5)
     dma("y", T.ly[:], v("lyf"), "oly", 128)
-    for who, u0, u1 in calls(XL, 0, 8):
-        xg(u0, u1, who)
     for u in range(8):
+        xg(u, u + 1, XL[u])
+    for u0, u1 in STORES:
         moved["oxy"] = 0
-        dma("y", T.xy[:, 512 * u:512 * u + 512], X(512 * u, 512 * u + 512), "oxy", 128)
+        dma("y", T.xy[:, 512 * u0:512 * u1], X(512 * u0, 512 * u1), "oxy", 128 * (u1 - u0))
+    for u in range(8):
         scan(v("tmp", 512 * u, 512 * u + 512), v("ym16"), X(512 * u, 512 * u + 512), 0.0, A.mult, A.max)
-    mm(v("pb0", 0, 256), NI, v("zc"), True, False)
-    mm(v("pb0", 0, 256), I, v("tmp", 15, 4096, 16), False, True)
-    act(v("zd"), v("pb0", 0, 256), F.Abs)
+    for bn, c0, c1 in (("pb0", 0, ZCUT), ("pb1", ZCUT, 256)):
+        mm(v(bn, c0, c1), NI, v("zc", c0, c1), True, False)
+        mm(v(bn, c0, c1), I, v("tmp", 15 + 16 * c0, 16 * c1, 16), False, True)
+        act(v("zd", c0, c1), v(bn, c0, c1), F.Abs)
     dma("s", T.zy[:], v("zd"), "ozy", 64)
 
     queue = {"v": V, "s": S, "t": PE, "g": g, "r": g, "y": g.sync}

@@ -26,8 +26,9 @@ SCRATCH = {
     "ibh": sb(128, bf), "ib16": sb(128, bf), "nib16": sb(128, bf),
     "eb": sb(7 * 144, bf), "bo": sb(128, f32), "bob": sb(128, bf), "oneb": sb(256, bf),
     "c2040": sb(128, bf), "cm05": sb(256, bf), "dinit": sb(304, bf), "kt": sb(256, f32), "jj": sb(256, f32),
-    "three": sb(288, bf), "zadd": sb(288, bf), "cd": sb(72, f32), "ce": sb(72, f32), "nb": sb(320, bf), "hb": sb(576, bf),
-    "ht": sb(72, bf), "car": sb(72, f32), "dsb": sb(256, f32),
+    "three": sb(288, bf), "zadd": sb(288, bf), "cd": sb(136, f32), "ce": sb(72, f32), "nb": sb(320, bf), "hb": sb(576, bf),
+    "hc": sb(576, bf), "bb": sb(288, bf), "va": sb(576, bf), "st": sb(1024, bf), "ip16": sb(128, bf), "i32": sb(128, f32), "c19": sb(256, bf),
+    "cr": sb(16, f32), "ht": sb(72, bf), "car": sb(72, f32), "ht2": sb(64, bf), "cd2": sb(64, f32), "car2": sb(64, f32), "dsb": sb(256, f32),
     "nu": sb(256, u16), "pu": sb(256, u16), "mu": sb(256, u16), "oa": sb(256, u16), "ob": sb(256, u16), "cu": sb(16, u16),
     "dig": sb(768, bf), "r32": sb(256, bf), "hh": sb(256, bf), "sg": sb(256, bf),
     "f2": sb(256, f32), "uu": sb(256, f32), "sp": sb(256, f32), "vv": sb(256, f32), "bu": sb(256, bf), "bv": sb(256, bf),
@@ -40,25 +41,28 @@ for _n in BANKS:
     SCRATCH[_n] = ("psum", [128, 512], f32)
 SEMAPHORES = ["cv", "cs", "ct", "cg", "ldx", "ldl", "ldz", "ldt", "oly", "ozy", "oxy", "loc"] + ["fill%d" % _j for _j in range(8)]
 for _t in range(3):
-    SEMAPHORES += ["la%d%d" % (_t, _p) for _p in range(3)] + ["lb%d" % _t] + ["%s%d%d" % (_n, _t, _h) for _n in ("ah", "al") for _h in range(2)]
+    SEMAPHORES += ["la%d%d" % (_t, _p) for _p in range(3)] + ["lb%d" % _t, "lc%d" % _t] + ["%s%d%d" % (_n, _t, _h) for _n in ("ah", "al") for _h in range(2)]
 
 MASTER = (0, 3, 9)
-CELLS = [(3, 1, 1, 0), (4, 2, 1, 0), (3, 2, 1, 1), (3, 5, 2, 0), (4, 7, 2, 0), (3, 7, 2, 1),
-         (1, 0, 0, 1), (2, 0, 0, 2), (0, 1, 0, 0), (1, 1, 0, 1), (0, 2, 0, 0), (0, 4, 0, 0), (1, 4, 1, 0), (2, 4, 2, 0),
+CELLS = [(1, 0, 0, 1), (2, 0, 0, 2), (0, 1, 0, 0), (1, 1, 0, 1), (0, 2, 0, 0), (0, 4, 0, 0), (1, 4, 1, 0), (2, 4, 2, 0),
          (1, 3, 1, 1), (2, 3, 1, 2), (0, 5, 1, 0), (1, 5, 1, 1), (0, 7, 1, 0), (1, 9, 2, 1), (2, 9, 2, 2)]
-FILLED, FILLER, FIRST = (9, 0, 3, 1, 2, 4, 5, 7), "ssss" "yyyy" "gggg" "yyyy" "vvvv" "ssss" "gggv" "vvvs", 4
-DP = (("SS", "VS", "SS", "VS"), ("VS", "VS", "VS", "VS"))
-DM = (("SS", "VS", "VS", "VS"), ("VS", "VS", "VV", "VV"))
-DORDER, JOIN = ((0, 0), (0, 1), (1, 0), (1, 1)), "11110011"
+FILLED, FILLER, FIRST = (9, 0, 3, 1, 2, 4, 5, 7), "ssss" "yyyy" "gggg" "yyyv" "vvvv" "gggs" "sssg" "vvvv", 4
+DP = (("SS", "VS", "VS", "VS"), ("SS", "VS", "VS", "VS"))
+DM = (("VS", "VS", "SS", "SS"), ("VS", "VS", "VS", "VS"))
+AFIRST, SENDFIRST = (1, 4), 1
+DL = (("SS", "VS", "VV", "VV"), ("SS", "VS", "VV", "VV"))
+DORDER, JOIN = ((0, 0), (0, 1), (1, 0), (1, 1)), "11110010"
+LAST, BYS, DGW, WHOLE, AVG = ((0, 256),), "svvs", "vs", False, "s"
 STORES = ((0, 2), (2, 4), (4, 6), (6, 7), (7, 8))
-PG = ({"b": "sSsSsSsS", "a": "vVvVvVvV"}, {"b": "sssSsSsS", "a": "svvVvVsS"})
-X0, XG, XL, ZCUT = "svsvsvsv", "ssssvssv", "vsvsvsss", 192
-XORDER, DIGITS, DX = (0, 1, 2, 3, 7, 4, 5, 6), 2, "tttttttt"
+PG = ({"a": "vVsSsvss"}, {"a": "vVsSsSsS"})
+X0, XG, XL, ZCUT = "svsvsvsv", "sfssvvvv", "vsvsvsss", 192
+XORDER, DIGITS, DX = (0, 1, 2, 3, 7, 4, 5, 6), 1, "tttttttt"
 
 
-CYCLE, PECYCLE, GATHER, SCATTER, FIXV, FIXS, WAKE = 0.00083, 0.00042, 1.56, 3.5, 0.03, 0.06, 0.19
-DMA0, DMARATE, TRAVEL, EARLY, SWEEPS = 1.6, 250.0, 4.0, 0.0, 3
-INFO, PLAN, STARTS = [], [], 1
+CYCLE, PECYCLE, GATHER, SCATTER, FIXV, FIXS, WAKE = 0.00083, 0.00042, 1.56, 3.5, 0.06, 0.08, 0.15
+DMA0, DMARATE, TRAVEL, EARLY, SWEEPS = 1.8, 250.0, 4.5, 0.0, 3
+CELLKB, LCKB, TRIES, QUICK, SLOW = 65, 110, 24, 0.72, 1.05
+INFO, PLAN, PATIENCE = [], [], (0.05, 0.15)
 
 
 def arrange(ops):
@@ -67,6 +71,9 @@ def arrange(ops):
         if o["sem"] is not None:
             group.setdefault(o["sem"], []).append(i)
     pred = [set(o["after"]) | {j for d in o["deps"] for j in (group[ops[d]["sem"]] if ops[d]["sem"] is not None else [d])} for o in ops]
+    for i, o in enumerate(ops):
+        if "follows" in o:
+            pred[i].add(o["follows"])
     way = [0.0] * len(ops)
     for i in range(len(ops) - 1, -1, -1):
         o = ops[i]
@@ -98,14 +105,79 @@ def arrange(ops):
             eng[i], start[i], end[i] = best[2], best[1], best[0] + (0.0 if back else o["late"]) + 1e-6
         return max(end.values()), start, end, eng
 
+    def play(far, links, onward, back, patience):
+        left, ready, start, end, eng = [len(x) for x in links], {}, {}, {}, {}
+        free, cand = {}, {}
+
+        def offer(i):
+            ready[i] = max([end[d] + gap for d, gap in links[i]] + [0.0]) + (ops[i]["late"] if back else 0.0)
+            for e in ops[i]["alt"]:
+                cand.setdefault(e, set()).add(i)
+                free.setdefault(e, 0.0)
+        for i in range(len(ops)):
+            if not left[i]:
+                offer(i)
+        while len(start) < len(ops):
+            now, e = min((max(free[q], min(ready[j] for j in c)), q) for q, c in cand.items() if c)
+            i = max((j for j in cand[e] if ready[j] <= now), key=lambda j: (far[j], -j))
+            c = ops[i]["alt"][e][1]
+            soon = [j for j in cand[e] if now < ready[j] < now + c and far[j] > far[i]]
+            soon = [j for j in soon if max(ready[j] + far[j], ready[j] + ops[j]["alt"][e][1] + far[i]) < now + c + far[j] - patience]
+            other = [max(free[q], now) for q, x in ops[i]["alt"].items() if q != e and max(free[q], now) + x[1] < now + c - 1e-9]
+            if soon or other:
+                fill = [j for j in cand[e] if ready[j] <= now and j != i and len(ops[j]["alt"]) == 1
+                        and now + ops[j]["alt"][e][1] <= min([ready[k] for k in soon] + [now + c])]
+                if not fill:
+                    if soon:
+                        free[e] = min(ready[j] for j in soon)
+                    else:
+                        cand[e].discard(i)
+                    continue
+                i = max(fill, key=lambda j: (far[j], -j))
+                c = ops[i]["alt"][e][1]
+            for q in ops[i]["alt"]:
+                cand[q].discard(i)
+            eng[i], start[i], free[e] = e, now, now + c
+            end[i] = now + c + (0.0 if back else ops[i]["late"]) + 1e-6
+            for j, _ in onward[i]:
+                left[j] -= 1
+                if not left[j]:
+                    offer(j)
+        return max(end.values()), start, end, eng
+
+    def both(plan):
+        if len(plan[3]) == len(ops):
+            free, end = {}, {}
+            for i in sorted(range(len(ops)), key=lambda j: (plan[1][j], j)):
+                o, e = ops[i], plan[3][i]
+                c = o["alt"][e][1]
+                c = c * QUICK if o["list"] else c * SLOW if e == "d" else c
+                free[e] = max([end[d] + gap for d, gap in before[i]] + [free.get(e, 0.0)]) + c
+                end[i] = free[e] + o["late"] + (0.4 if "follows" in o else 0.0)
+            plan[3]["both"] = plan[0] + max(end.values())
+        return plan[3]["both"]
+
     best = None
-    for first in (range(len(ops)), sorted(range(len(ops)), key=lambda j: (-way[j], j)))[:STARTS]:
-        now = sweep(first, before, False)
+    for patience in PATIENCE:
+        good, far = None, way
         for _ in range(SWEEPS):
-            rev = sweep(sorted(range(len(ops)), key=lambda j: (-now[1][j], -j)), behind, True)
-            now = sweep(sorted(range(len(ops)), key=lambda j: (-rev[1][j], j)), before, False)
-            best = min(best or now, now, key=lambda x: x[0])
-            INFO.append(now[0])
+            now = play(far, before, behind, False, patience)
+            good = min(good or now, now, key=lambda x: x[0])
+            far = play(now[2], behind, before, True, patience)[2]
+        rev = sweep(sorted(range(len(ops)), key=lambda j: (-good[1][j], -j)), behind, True)
+        now = sweep(sorted(range(len(ops)), key=lambda j: (-rev[1][j], j)), before, False)
+        best = min(best or good, good, now, key=both)
+        INFO.append(now[0])
+    seed = 1
+    for k in range(TRIES):
+        if k % 8 == 0:
+            base = sweep(sorted(range(len(ops)), key=lambda j: (-best[1][j], -j)), behind, True)[2]
+        far = {}
+        for i in range(len(ops)):
+            seed = (seed * 1103515245 + 12345) % 2147483648
+            far[i] = base[i] + (0.15, 0.4, 0.8)[k % 3] * seed / 2147483648.0
+        best = min(best, play(far, before, behind, False, PATIENCE[k % len(PATIENCE)]), key=both)
+        INFO.append(both(best))
     for i, o in enumerate(ops):
         o["eng"] = best[3][i]
     return sorted(range(len(ops)), key=lambda j: (best[1][j], j))
@@ -150,7 +222,8 @@ def rank_program(g, core, T, topo):
         deps = [d for d in deps if not (sem is not None and ops[d]["sem"] == sem)]
         if eng == "t":
             deps = [d for d in deps if ops[d]["eng"] != "t"]
-        ops.append({"eng": eng, "alt": alt, "deps": deps, "after": after, "sem": sem, "inc": inc, "late": late})
+        ops.append({"eng": eng, "alt": alt, "deps": deps, "after": after, "sem": sem, "inc": inc, "late": late,
+                    "list": any(isinstance(a, tuple) and len(a) > 3 and a[3] == "list" for a in r)})
         return me
 
     V, S, PE = g.vector, g.scalar, g.tensor
@@ -228,16 +301,17 @@ def rank_program(g, core, T, topo):
     def sel(out, a, pat, o, base, cm):
         op({"g": (lambda: g.affine_select(out[0], a[0], pat, o, 0.0, base, cm), 0.17 + 2 * out[2] * CYCLE)}, [a], [out])
 
-    moved, copies = {}, []
+    moved, copies, low, lead = {}, [], [], []
 
     def dma(q, out, a, sem, kb):
         o, i = (out if isinstance(out, tuple) else (out, [])), (a if isinstance(a, tuple) else (a, []))
-        moved[sem] = moved.get(sem, 0) + kb
         copies.append(op({q: (lambda: (g.sync if q == "y" else g.scalar).dma_start(o[0], i[0]), 0.06)}, [i], [o], sem=sem,
-                         late=DMA0 + moved[sem] / DMARATE, after=copies[-1:] if q == "y" and sem[0] != "o" else []))
+                         late=DMA0, after=copies[-1:] if q == "y" and sem[0] != "o" else []))
+        j = op({"d": (None, kb / DMARATE)}, sem=sem, inc=0)
+        ops[j]["follows"] = copies[-1]
 
     def gather(who, out, w, off):
-        lin(out, ix(w, off), who=who)
+        lin(out, ix(w, off), who="vs" if who == "f" else who)
 
     I, NI, ID = v("ib", 0, 128), v("nib"), F.Identity
     turnb = [0]
@@ -268,8 +342,8 @@ def rank_program(g, core, T, topo):
     ms(v("thi"), 0)
     dma("s", v("li"), T.l0[:], "ldl", 128)
     dma("y", v("tab"), T.x0[:], "ldx", 1024)
-    dma("y", v("thi", 0, 3, None, slice(0, 128, 16)), T.th[:], "ldt", 1024)
-    dma("y", v("zc"), T.z0[:], "ldz", 1100)
+    dma("y", v("thi", 0, 3, None, slice(0, 128, 16)), T.th[:], "ldt", 10)
+    dma("y", v("zc"), T.z0[:], "ldz", 100)
     ms(v("oneb"), 1.0)
     iota(v("pint", 0, 1), [[0, 1]], 0, 1, False)
     iota(v("dupf"), [[1, 16], [0, 2]], 0, 0)
@@ -299,8 +373,7 @@ def rank_program(g, core, T, topo):
         if FILLER[j] in "yg":
             fill(j, j + 1)
     zero(v("eb"), "s")
-    lin(v("ib16"), I, 1.0 / 16.0)
-    lin(v("nib16"), I, -16.0)
+    lin(v("nib256"), I, -256.0)
     lin(v("bo"), v("bob"))
     lin(EW(0), B8)
     lin(NI, I, -1.0)
@@ -321,13 +394,14 @@ def rank_program(g, core, T, topo):
     def digits(a, c0, c1):
         r, d0 = v("r32", c0, c1), v("dig", c0, c1)
         ts(r, a, M16, M16, A.add, A.subtract)
-        lin(v("hh", c0, c1), r, 1.0 / 256.0, 191.53125)
-        lin(d0, v("hh", c0, c1), 1.0, -199.5)
+        lin(v("hh", c0, c1), r, 1.0 / 256.0, 191.53125, DGW)
+        lin(d0, v("hh", c0, c1), 1.0, -199.5, DGW)
         tt(v("dig", 512 + c0, 512 + c1), a, r, A.subtract)
+        low.append(len(ops) - 1)
         b = v(nextb(), c0, c1)
-        mm(b, v("ib16"), r, True, False)
-        mm(b, v("nib16"), d0, False, True)
-        lin(v("dig", 256 + c0, 256 + c1), b, 1.0, -127.5)
+        mm(b, I, r, True)
+        mm(b, v("nib256"), v("hh", c0, c1))
+        lin(v("dig", 256 + c0, 256 + c1), b, 1.0 / 16.0, 3064.5, DGW)
 
     def window(t):
         def row(pl, sh):
@@ -335,14 +409,54 @@ def rank_program(g, core, T, topo):
                 return v("tmp", sh, RG, None, slice(pl, 128, 16))
             return v("win", RG * MASTER[pl] + sh, RG * MASTER[pl] + RG, None, slice(0, 128, 16))
         for pl in (2, 0, 1):
-            dma("y", row(pl, 0), v("dig", 256 * pl, 256 * pl + 256), "la%d%d" % (t, pl), 64)
+            dma("y", row(pl, 0), v("dig", 256 * pl, 256 * pl + 256), "la%d%d" % (t, pl), 110)
         if t == 0:
             cells = sorted(CELLS + [(0, MASTER[pl], pl, 0) for pl in range(3)], key=lambda x: FILLED.index(x[1]))
         else:
             cells = sorted(CELLS, key=lambda x: (2, 0, 1).index(x[2]))
         for pa, rg, pl, sh in cells:
             moved["lb0"] = 256
-            dma("y", v("win", RG * rg, RG * rg + RG - sh, None, slice(pa, 128, 16)), row(pl, sh), "lb%d" % t, 64)
+            dma("y", v("win", RG * rg, RG * rg + RG - sh, None, slice(pa, 128, 16)), row(pl, sh), "lb%d" % t, CELLKB)
+            if t == 0 and pa == 1 and rg in (1, 5):
+                dma("y", v("win", RG * rg, RG * rg + RG, None, slice(4, 128, 16)), v("c19"), "lb0", 64)
+
+    def pairs():
+        for j in range(2):
+            c0, d0 = 256 * j, 256 * j + 256
+            mm(v("pq1", c0, c0 + 255), v("ip16"), v("dig", d0, d0 + 255), j == 0)
+            mm(v("pq1", c0, c0 + 255), I, v("dig", d0 + 1, d0 + 256))
+            mm(v("pq1", c0 + 255, c0 + 256), v("ip16"), v("dig", d0 + 255, d0 + 256))
+            mm(v("pq1", c0 + 255, c0 + 256), v("ib", 1, 129), v("dig", d0, d0 + 1))
+
+    def starts(t):
+        if BYS[0] == "s":
+            act(v("bb"), v("nb", 32, 320), F.Relu, bias=BIG, scale=-4.0)
+        else:
+            ts(v("bb"), v("nb", 32, 320), 0.0, BIG, A.is_equal, A.mult)
+        for j in range(2):
+            if BYS[1 + j] == "s":
+                for c0, c1 in ((0, 255), (255, 256)):
+                    mm(v("pq1", 256 * j + c0, 256 * j + c1), I, v("nb", 32 + c0, 32 + c1))
+        for j in range(2):
+            if BYS[1 + j] == "s":
+                lin(v("va", 288 * j, 288 * j + 256), v("pq1", 256 * j, 256 * j + 256), who="s")
+            else:
+                tt(v("va", 288 * j, 288 * j + 256), v("nb", 32, 288), v("pq1", 256 * j, 256 * j + 256), A.add)
+        scan(v("hc", 0, 288), v("bb"), v("va", 0, 288), BIG, A.add, A.min)
+        scan(v("hc", 575, 287, -1), v("bb"), v("va", 288, 576), BIG, A.add, A.min)
+        vtr(v("ht2"), v("hc", 256, 320))
+        scan(v("car2"), v("cd2"), v("ht2"), BIG, A.add, A.min)
+        ts(v("cr", 0, 2), v("car2", 31, 64, 32), 32 * M16, 32 * M16, A.add, A.subtract)
+        lead[:] = [len(ops) - 1]
+        tt(v("cr", 8, 10), v("car2", 31, 64, 32), v("cr", 0, 2), A.subtract)
+        lead.append(len(ops) - 1)
+        for j in range(2):
+            a, h = v("st", 256 * j, 256 * j + 256), v("st", 512 + 256 * j, 768 + 256 * j)
+            scan(a, v("bb", 0, 256), v("va", 288 * j, 288 * j + 256), col("cr", 8 + j), A.add, A.min)
+            lead.append(len(ops) - 1)
+            lin(h, a, 1.0 / 16.0, 199.5, BYS[3])
+            for src, pa, rg in ((a, 2, (2, 7)[j]), (h, 2, (1, 5)[j])):
+                dma("y", v("win", RG * rg, RG * rg + RG, None, slice(pa, 128, 16)), src, "lc%d" % t, LCKB)
 
     cp(v("nu"), v("li"))
     turn(v("li"), v("dup"), 0, 512)
@@ -368,8 +482,8 @@ def rank_program(g, core, T, topo):
         ts(v("thp"), v("pq0", 0, 8), 0.5, None, A.add)
         ts(col("thb", 0), col("thp", 0), BIG / 2, None, A.mult)
         ts(col("pf", 12), PC, 256.0, None, A.mult)
-        for h in range(2):
-            lin(v("px%d" % h, 256, 384), v("kt", 128 * h, 128 * h + 128), 1.0, col("pf", 12))
+        lin(v("kt"), v("kt"), 1.0, col("pf", 12))
+        lin(v("i32"), I)
         ms(v("nb"), BIG)
         ms(v("three"), 0.0)
         ms(v("zadd"), 0.0)
@@ -386,6 +500,12 @@ def rank_program(g, core, T, topo):
         tt(d, d, e, A.add)
         ts(e, t, PJ, col("pf", 14), A.is_equal, A.mult)
         tt(d, d, e, A.add)
+        for j in range(2):
+            lin(v("cd2", 32 * j, 32 * j + 32), v("cd", 0, 32))
+        lin(col("cd2", 32), col("cd2", 32), 1.0, LOW)
+        ms(v("va"), BIG)
+        lin(v("ip16"), I, 16.0)
+        lin(v("c19"), v("oneb"), -19.0)
         ts(e, t, col("pf", 15), 2 * BIG, A.is_equal, A.mult)
         tt(d, d, e, A.add)
         ts(col("cd", 32), col("pf", 14), -1.0, None, A.mult)
@@ -399,18 +519,16 @@ def rank_program(g, core, T, topo):
         ts(v("pta"), v("lf", 0, 16), col("pf", 28), None, A.add)
 
     def consts_s():
-        for j in range(5):
-            ts(col("pf", 20 + j), PC, float(j), (256.0, 16.0, 1.0, 1.0, 16.0)[j], A.is_equal, A.mult)
-        tt(col("pf", 26), col("pf", 23), col("pf", 24), A.add)
-        tt(col("pf", 25), col("pf", 20), col("pf", 21), A.add)
-        tt(col("pf", 27), col("pf", 25), col("pf", 22), A.add)
-        lin(EW(5), B8, col("pf", 26))
+        ts(col("pf", 20), PC, 0.0, 256.0, A.is_equal, A.mult)
+        ts(col("pf", 21), PC, 1.0, 16.0, A.is_equal, A.mult)
+        ts(col("pf", 22), PC, 4.0, 10.5, A.is_equal, A.mult)
+        ts(col("pf", 23), PC, 2.0, col("pf", 20), A.is_equal, A.add)
+        ts(col("pf", 27), col("pf", 23), col("pf", 21), col("pf", 22), A.add, A.add)
         lin(EW(4), B8, col("pf", 27))
         lin(v("c2040"), v("oneb", 0, 128), 2040.0)
         ztile()
         for w, c in ((1, -1.0), (3, -2.0), (6, 2.0)):
             lin(EW(w), B8, c)
-        lin(v("nib256"), I, -256.0)
         lin(v("ib256"), v("ib"), 256.0)
         lin(v("cm05"), v("oneb"), -0.5)
         lin(v("cb"), v("colf"), 256.0, col("pf", 9))
@@ -485,26 +603,31 @@ def rank_program(g, core, T, topo):
         scan(v("tmp", 256 * c, 256 * c + 256), v("ym16", 0, 256), X(c, 4096, 16), 0.0, A.mult, A.max)
 
     def blocks_a():
-        b1, b2 = "pq0", "pq1"
+        b1 = "pq0"
         mm(v(b1, 0, 256), I, Y, True, False)
         mm(v(b1, 0, 256), NI, v("zc"))
-        mm(v(b2, 0, 256), I, Y, True, False)
-        mm(v(b2, 0, 256), I, v("zc"), False, False)
-        mm(v(b2, 0, 256), I, v("cm05"), False, True)
+        mm(v(b1, 256, 512), I, Y)
+        mm(v(b1, 256, 512), I, v("zc"))
+        mm(v(b1, 256, 512), I, v("cm05"))
         for b in range(16):
-            mm(v(b2, 256, 272), E(0, b), v("tmp", 15 + 16 * b, 4096, 256))
+            mm(v("pb0", 0, 16), E(0, b), v("tmp", 15 + 16 * b, 4096, 256), b == 0)
         act(v("zc"), v(b1, 0, 256), F.Abs)
         ztile()
-        ts(v("avi"), v(b2, 0, 256), 0.5, None, A.mult)
+        if AVG == "s":
+            lin(v("zs"), v(b1, 256, 512), 0.5, M1, "s")
+            lin(v("avg"), v("zs"), 1.0, -M1, "s")
+            return
+        ts(v("avi"), v(b1, 256, 512), 0.5, None, A.mult)
 
     def blocks_b():
-        cp(v("ui", 0, 16), v("pq1", 256, 272))
+        cp(v("ui", 0, 16), v("pb0", 0, 16))
         ts(v("ui", 16, 32), v("ui", 0, 16), 15, None, A.bitwise_and)
         tt(v("uf"), v("ui", 16, 32), v("cb"), A.add)
         cp(v("cu"), v("uf"))
 
     def update():
-        cp(ix(v("tab"), v("cu")), v("avi"))
+        cp(ix(v("tab"), v("cu")), v("avg" if AVG == "s" else "avi"))
+        ops[-1]["after"] += low[-1:] * SENDFIRST
 
     def periods(t):
         scan(v("hb", 0, 288), v("three"), v("nb", 32, 320), BIG, A.add, A.min)
@@ -512,38 +635,34 @@ def rank_program(g, core, T, topo):
         vtr(v("ht", 0, 64), v("hb", 256, 320))
         scan(v("car", 0, 65), v("cd", 0, 65), v("ht", 0, 65), BIG, A.add, A.min)
         scan(v("jj"), v("three", 0, 256), v("nb", 32, 288), col("car", 32), A.add, A.min)
+        ops[-1]["after"] += lead[:AFIRST[0]]
         scan(v("pb0", 255, None, -1), v("nb", 288, 32, -1), v("oneb"), col("car", 64), A.min, A.add)
-        for h in range(2):
-            i2, hf, uu, vv, f2, un, bu, bv, s1, s2, s4 = [half(x, 0, h) for x in "jj sp uu vv f2 hh bu bv s1 s2 s4".split()]
-            J, sp, k = half("pb0", 0, h), half("pb0", 1, h), v("px%d" % h, 256, 384)
-            cl, cl2, t1 = v("pb%d" % (2 + h), 0, 128), v("pb%d" % (2 + h), 128, 256), half("pb1", 0, h)
-            upto = (lambda x: v(x, 0, 128 * h + 128))
-            lin(hf, i2, -0.5, 3.0 * RG)
-            tt(uu, i2, J, A.subtract)
-            tt(cl, hf, J, A.subtract)
-            tt(vv, uu, cl, A.add)
-            act(un, uu, F.Relu, scale=-float(RG))
-            act(bv, vv, F.Relu, bias=2.0 * RG * (3 - 3 * RG), scale=2.0 * RG)
-            act(bu, uu, F.Relu, bias=3.0 * RG, scale=float(RG))
-            tt(sp, hf, k, A.add)
-            tt(sp, sp, un, A.subtract)
-            tt(s1, bv, sp, A.add)
-            ts(half("ob", 0, h), ix(upto("s1"), v("pta", 8 * h, 8 * h + 8)), 9.0 * RG, None, A.min)
-            tt(f2, i2, k, A.add)
-            tt(t1, bu, cl, A.min)
-            lin(cl2, cl, 1.0, 3.0 * RG)
-            tt(t1, f2, t1, A.add)
-            tt(s2, bv, cl2, A.min)
-            tt(s4, s2, t1, A.add)
-            cp(half("oa", 0, h), ix(upto("s4"), v("pta", 8 * h, 8 * h + 8)))
+        ops[-1]["after"] += lead[:AFIRST[1]]
+        i2, hf, uu, vv, bu, bv, t1, s2 = [v(x) for x in "jj sp uu vv bu bv s1 s2".split()]
+        J, xx, f2, cl, cl2 = v("pb0", 0, 256), v("pb0", 256, 512), v("pb1", 0, 256), v("pb2", 0, 256), v("pb3", 0, 256)
+        mm(f2, v("i32"), v("kt"), True)
+        mm(f2, v("i32"), i2)
+        lin(hf, i2, -0.5, 3.0 * RG, "s")
+        tt(uu, i2, J, A.subtract)
+        tt(cl, hf, J, A.subtract)
+        tt(vv, uu, cl, A.add)
+        act(bu, uu, F.Relu, bias=3.0 * RG, scale=float(RG))
+        act(bv, vv, F.Relu, bias=2.0 * RG * (3 - 3 * RG), scale=2.0 * RG)
+        tt(t1, bu, cl, A.min)
+        lin(cl2, cl, 1.0, 3.0 * RG, "s")
+        tt(xx, t1, f2, A.add)
+        for c0, c1 in LAST:
+            tt(v("s2", c0, c1), v("bv", c0, c1), v("pb3", c0, c1), A.min)
+            tt(v("s4", c0, c1), v("s2", c0, c1), v("pb0", 256 + c0, 256 + c1), A.add)
+            for h in range(c0 // 128, c1 // 128):
+                cp(half("oa", 0, h), ix(v("s4", 0, 128 * h + 128), v("pta", 8 * h, 8 * h + 8)))
 
     def pg(w, eng, u0, u1):
         gather(eng, v("g" + w, 512 * u0, 512 * u1), v("win"), v("o" + w, 32 * u0, 32 * u1))
 
     def psum_(w, q, first=False, last=False):
         bn = "px%d" % (q // 2)
-        if w == "b":
-            mm(v(bn, 64 * (q & 1), 64 * (q & 1) + 64), I, v("c2040", 0, 64), first)
+        mm(v(bn, 64 * (q & 1), 64 * (q & 1) + 64), I, v("c2040", 0, 64), first)
         for c in range(16):
             mm(v(bn, 64 * (q & 1), 64 * (q & 1) + 64), E(4 if w == "a" else 5, c), v("g" + w, 1024 * q + c, 1024 * q + 1024, 16),
                False, last and c == 15)
@@ -557,6 +676,7 @@ def rank_program(g, core, T, topo):
         ts(r16, P, M16, M16, A.add, A.subtract)
         lin(hi, r16, 1.0 / 256.0, 191.53125)
         tt(lo, P, r16, A.subtract)
+        low.append(len(ops) - 1)
         d1, d2 = T.cores[(rank + 1) % n], T.cores[(rank + 2) % n]
         e1, e2 = topo.engines(core, d1)[0::2], topo.engines(core, d2)[1::2]
         trs = []
@@ -599,8 +719,11 @@ def rank_program(g, core, T, topo):
                 if md == "VV" and not u1 & 1:
                     ts(v(a, c1 - 1024, c1), v(d, c1 - 1024, c1), 0.0, None, A.max)
 
+    def kinds(k, h):
+        return (DP, DL if rnd[0] == 2 else DM)[k][h]
+
     def spans(k, h):
-        modes, out = (DP, DM)[k][h], []
+        modes, out = kinds(k, h), []
         for q in range(2):
             u = 4 * h + 2 * q
             if modes[2 * q] == modes[2 * q + 1] and JOIN[4 * k + 2 * h + q] == "1":
@@ -624,7 +747,7 @@ def rank_program(g, core, T, topo):
     def dsums(k, h):
         d, a = (("d3", "a3"), ("d4", "a4"))[k]
         wa, wr, wd = ((1, 3, 0), (0, 6, 1))[k]
-        bn, modes = "pq%d" % h, (DP, DM)[k][h]
+        bn, modes = "pq%d" % h, kinds(k, h)
         todo = [(q, d, wd) for q in range(2) if modes[2 * q] == "VV"]
         todo += [(q, a, wr if modes[2 * q] == "VV" else wa) for q in range(2)]
         for j, (q, buf, w) in enumerate(todo):
@@ -639,10 +762,12 @@ def rank_program(g, core, T, topo):
         tt(half("s3", 0, h), half("s2", 0, h), v(bn, 0, 128), A.add)
 
     def threshold(t):
-        b = v(nextb(), 0, 1)
-        act(v("hh"), v("sg"), ID, acc=col("acc", 0))
-        mm(b, v("bo"), col("acc", 0), True, False)
-        cp(col("ai", 0), b)
+        b = v("px1", 256, 384)
+        mm(b, v("bob"), half("sg", 0, 0), True)
+        mm(b, v("bob"), half("sg", 0, 1))
+        a = col("acc", 0)
+        op({"v": (lambda: V.tensor_reduce(a[0], b[0], AxisListType.X, A.add), cv(b))}, [b], [a])
+        cp(col("ai", 0), a)
         ts(col("ai", 8), col("ai", 0), 31, None, A.bitwise_and)
         ts(col("thb", 0), col("ai", 8), col("thp", t), BIG / 2, A.add, A.mult)
 
@@ -653,7 +778,11 @@ def rank_program(g, core, T, topo):
             fill(j, j + 1)
     window(0)
     consts_s()
+    rnd = [0]
     for t in range(3):
+        rnd[0] = t
+        pairs()
+        starts(t)
         periods(t)
         for h in range(2):
             if t > 0 and h == 1:
@@ -662,12 +791,10 @@ def rank_program(g, core, T, topo):
                 blocks_a()
                 blocks_b()
                 update()
-            for w in "ba":
-                for who, u0, u1 in calls(PG[min(t, 1)][w], 4 * h, 4 * h + 4):
-                    pg(w, who, u0, u1)
+            for who, u0, u1 in calls(PG[min(t, 1)]["a"], 4 * h, 4 * h + 4):
+                pg("a", who, u0, u1)
             for q in (2 * h, 2 * h + 1):
-                for w in "ba":
-                    psum_(w, q, first=w == "b" and q == 2 * h)
+                psum_("a", q, first=q == 2 * h)
             send(t, h)
         for k, h in DORDER:
             if k == 1:
@@ -686,8 +813,13 @@ def rank_program(g, core, T, topo):
                 ts(half("nu", 0, h), names, 7.5, None, A.add)
                 for j in range(4 * h, 4 * h + 4):
                     xg(XORDER[j], XORDER[j] + 1, XG[j])
+                    if XG[j] == "v" and j % 4 > DIGITS:
+                        ops[-1]["after"].append(low[-1])
                     if j % 4 == DIGITS:
-                        digits(names, 128 * h, 128 * h + 128)
+                        if not WHOLE:
+                            digits(names, 128 * h, 128 * h + 128)
+                        elif h == 1:
+                            digits(ix(v("s3"), v("ptb")), 0, 256)
                         if h == 1:
                             window(t + 1)
                             threshold(t + 1)
@@ -738,7 +870,7 @@ def rank_program(g, core, T, topo):
     cnt, seen = {}, {}
     for i in order:
         o = ops[i]
-        if o["eng"] == "x":
+        if o["eng"] in "xd":
             continue
         qn = o["eng"]
         q = queue[qn]

from concourse.bass import DstId, RemoteDMATransfer
from concourse.mybir import AluOpType as A, AxisListType, ActivationFunctionType as F

RG = 4096
WIN = 10 * RG
XO, GO = 6 * RG, 8 * RG
BIG = 65536.0
M16 = 201326592.0
M1 = 12582912.0
LOW = 1048576.0
f32, bf, i32, u16 = "float32", "bfloat16", "int32", "uint16"


def sb(n, d):
    return ("sbuf", [128, n], d)


SCRATCH = {
    "win": sb(WIN, bf), "tab": sb(4096, bf), "ga": sb(4096, bf), "gb": sb(4096, bf),
    "d3": sb(4096, bf), "a3": sb(4096, bf), "d4": sb(4096, bf), "a4": sb(4096, bf), "tmp": sb(4096, bf),
    "zb": sb(1024, bf), "ym8": sb(512, bf), "ym16": sb(512, bf), "li": sb(256, i32), "thi": sb(8, i32), "th8": sb(8, f32),
    "thp": sb(8, f32), "thb": sb(8, f32), "zc": sb(256, bf), "z2": sb(2048, bf), "avi": sb(256, i32), "zd": sb(256, bf), "zs": sb(256, f32), "avg": sb(256, bf),
    "pint": sb(8, i32), "pf": sb(32, f32), "colf": sb(16, f32), "dupf": sb(32, f32), "selff": sb(16, f32), "tcol": sb(72, f32),
    "pt": sb(16, u16), "pta": sb(16, u16), "ptb": sb(16, u16), "dup2": sb(32, u16), "lf": sb(64, f32), "dup": sb(32, u16), "selc": sb(16, u16), "sell": sb(16, u16),
    "cb": sb(16, f32), "ib": sb(256, bf), "ib256": sb(256, bf), "nib": sb(128, bf), "nib256": sb(128, bf), "ib2": sb(128, bf),
    "ibh": sb(128, bf), "ib16": sb(128, bf), "nib16": sb(128, bf),
    "eb": sb(7 * 144, bf), "bo": sb(128, f32), "bob": sb(128, bf), "oneb": sb(256, bf),
    "c2040": sb(128, bf), "cm05": sb(256, bf), "dinit": sb(304, bf), "kt": sb(256, f32), "jj": sb(256, f32),
    "three": sb(288, bf), "zadd": sb(288, bf), "cd": sb(136, f32), "ce": sb(72, f32), "nb": sb(320, bf), "hb": sb(576, bf),
    "hc": sb(576, bf), "bb": sb(288, bf), "va": sb(576, bf), "st": sb(1024, bf), "ip16": sb(128, bf), "i32": sb(128, f32), "c19": sb(256, bf),
    "cr": sb(16, f32), "ht": sb(72, bf), "car": sb(72, f32), "ht2": sb(64, bf), "cd2": sb(64, f32), "car2": sb(64, f32), "dsb": sb(256, f32),
    "nu": sb(256, u16), "pu": sb(256, u16), "mu": sb(256, u16), "oa": sb(256, u16), "ob": sb(256, u16), "cu": sb(16, u16),
    "dig": sb(768, bf), "r32": sb(256, bf), "hh": sb(256, bf), "sg": sb(256, bf),
    "f2": sb(256, f32), "uu": sb(256, f32), "sp": sb(256, f32), "vv": sb(256, f32), "bu": sb(256, bf), "bv": sb(256, bf),
    "s1": sb(256, f32), "s2": sb(256, f32), "s3": sb(256, f32), "s4": sb(256, f32), "w1": sb(512, f32), "w2": sb(512, f32),
    "acc": sb(16, f32), "ai": sb(16, i32), "ui": sb(32, i32), "uf": sb(16, f32), "r16": sb(256, bf), "lyf": sb(256, f32),
    "hi": sb(768, bf), "lo": sb(768, bf), "hin": sb(768, bf), "lin": sb(768, bf),
}
BANKS = ("pb0", "pb1", "pb2", "pb3", "px0", "px1", "pq0", "pq1")
for _n in BANKS:
    SCRATCH[_n] = ("psum", [128, 512], f32)
SEMAPHORES = ["cv", "cs", "ct", "cg", "ldx", "ldl", "ldz", "ldt", "oly", "ozy", "oxy", "loc"] + ["fill%d" % _j for _j in range(8)]
for _t in range(3):
    SEMAPHORES += ["la%d%d" % (_t, _p) for _p in range(3)] + ["lb%d" % _t, "lc%d" % _t] + ["%s%d%d" % (_n, _t, _h) for _n in ("ah", "al") for _h in range(2)]

MASTER = (0, 3, 9)
CELLS = [(1, 0, 0, 1), (2, 0, 0, 2), (0, 1, 0, 0), (1, 1, 0, 1), (0, 2, 0, 0), (0, 4, 0, 0), (1, 4, 1, 0), (2, 4, 2, 0),
         (1, 3, 1, 1), (2, 3, 1, 2), (0, 5, 1, 0), (1, 5, 1, 1), (0, 7, 1, 0), (1, 9, 2, 1), (2, 9, 2, 2)]
FILLED, FILLER, FIRST = (9, 0, 3, 1, 2, 4, 5, 7), "ssss" "yyyy" "gggg" "yyyv" "vvvv" "gggs" "sssg" "vvvv", 4
DP = (("SS", "VS", "VS", "VS"), ("SS", "VS", "VS", "VS"))
DM = (("VS", "VS", "SS", "SS"), ("VS", "VS", "VS", "VS"))
AFIRST, SENDFIRST = (1, 4), 1
DL = (("SS", "VS", "VV", "VV"), ("SS", "VS", "VV", "VV"))
DORDER, JOIN = ((0, 0), (0, 1), (1, 0), (1, 1)), "11110010"
LAST, BYS, DGW, WHOLE, AVG = ((0, 256),), "svvs", "vs", False, "s"
STORES = ((0, 2), (2, 4), (4, 6), (6, 7), (7, 8))
PG = ({"a": "vVsSsvss"}, {"a": "vVsSsSsS"})
X0, XG, XL, ZCUT = "svsvsvsv", "sfssvvvv", "vsvsvsss", 192
XORDER, DIGITS, DX = (0, 1, 2, 3, 7, 4, 5, 6), 1, "tttttttt"


CYCLE, PECYCLE, GATHER, SCATTER, FIXV, FIXS, WAKE = 0.00083, 0.00042, 1.56, 3.5, 0.06, 0.08, 0.15
DMA0, DMARATE, TRAVEL, EARLY, SWEEPS = 1.8, 250.0, 4.5, 0.0, 3
CELLKB, LCKB, TRIES, QUICK, SLOW = 65, 110, 24, 0.72, 1.05
INFO, PLAN, PATIENCE = [], [], (0.05, 0.15)


def arrange(ops):
    group = {}
    for i, o in enumerate(ops):
        if o["sem"] is not None:
            group.setdefault(o["sem"], []).append(i)
    pred = [set(o["after"]) | {j for d in o["deps"] for j in (group[ops[d]["sem"]] if ops[d]["sem"] is not None else [d])} for o in ops]
    for i, o in enumerate(ops):
        if "follows" in o:
            pred[i].add(o["follows"])
    way = [0.0] * len(ops)
    for i in range(len(ops) - 1, -1, -1):
        o = ops[i]
        way[i] += min(c for _, c in o["alt"].values()) + o["late"] + 1e-6 + o.get("early", 0.0)
        for d in pred[i]:
            way[d] = max(way[d], way[i] + (-ops[d]["late"] if d in o["after"] else WAKE))
    before = [[(d, -ops[d]["late"] if d in o["after"] else WAKE) for d in pred[i]] for i, o in enumerate(ops)]
    behind = [[] for _ in ops]
    for i, lst in enumerate(before):
        for d, gap in lst:
            behind[d].append((i, gap))

    def sweep(order, links, back):
        busy, start, end, eng = {}, {}, {}, {}
        for i in order:
            o, best = ops[i], None
            ready = max([end[d] + gap for d, gap in links[i]] + [0.0]) + (o["late"] if back else 0.0)
            for e, (_, c) in o["alt"].items():
                at, line = ready, busy.setdefault(e, [])
                k = len(line)
                while k > 0 and line[k - 1][1] > ready:
                    k -= 1
                while k < len(line) and line[k][0] < at + c - 1e-9:
                    at = max(at, line[k][1])
                    k += 1
                if best is None or at + c < best[0]:
                    best = (at + c, at, e, k)
            busy[best[2]].insert(best[3], (best[1], best[0]))
            eng[i], start[i], end[i] = best[2], best[1], best[0] + (0.0 if back else o["late"]) + 1e-6
        return max(end.values()), start, end, eng

    def play(far, links, onward, back, patience):
        left, ready, start, end, eng = [len(x) for x in links], {}, {}, {}, {}
        free, cand = {}, {}

        def offer(i):
            ready[i] = max([end[d] + gap for d, gap in links[i]] + [0.0]) + (ops[i]["late"] if back else 0.0)
            for e in ops[i]["alt"]:
                cand.setdefault(e, set()).add(i)
                free.setdefault(e, 0.0)
        for i in range(len(ops)):
            if not left[i]:
                offer(i)
        while len(start) < len(ops):
            now, e = min((max(free[q], min(ready[j] for j in c)), q) for q, c in cand.items() if c)
            i = max((j for j in cand[e] if ready[j] <= now), key=lambda j: (far[j], -j))
            c = ops[i]["alt"][e][1]
            soon = [j for j in cand[e] if now < ready[j] < now + c and far[j] > far[i]]
            soon = [j for j in soon if max(ready[j] + far[j], ready[j] + ops[j]["alt"][e][1] + far[i]) < now + c + far[j] - patience]
            other = [max(free[q], now) for q, x in ops[i]["alt"].items() if q != e and max(free[q], now) + x[1] < now + c - 1e-9]
            if soon or other:
                fill = [j for j in cand[e] if ready[j] <= now and j != i and len(ops[j]["alt"]) == 1
                        and now + ops[j]["alt"][e][1] <= min([ready[k] for k in soon] + [now + c])]
                if not fill:
                    if soon:
                        free[e] = min(ready[j] for j in soon)
                    else:
                        cand[e].discard(i)
                    continue
                i = max(fill, key=lambda j: (far[j], -j))
                c = ops[i]["alt"][e][1]
            for q in ops[i]["alt"]:
                cand[q].discard(i)
            eng[i], start[i], free[e] = e, now, now + c
            end[i] = now + c + (0.0 if back else ops[i]["late"]) + 1e-6
            for j, _ in onward[i]:
                left[j] -= 1
                if not left[j]:
                    offer(j)
        return max(end.values()), start, end, eng

    def both(plan):
        if len(plan[3]) == len(ops):
            free, end = {}, {}
            for i in sorted(range(len(ops)), key=lambda j: (plan[1][j], j)):
                o, e = ops[i], plan[3][i]
                c = o["alt"][e][1]
                c = c * QUICK if o["list"] else c * SLOW if e == "d" else c
                free[e] = max([end[d] + gap for d, gap in before[i]] + [free.get(e, 0.0)]) + c
                end[i] = free[e] + o["late"] + (0.4 if "follows" in o else 0.0)
            plan[3]["both"] = plan[0] + max(end.values())
        return plan[3]["both"]

    best = None
    for patience in PATIENCE:
        good, far = None, way
        for _ in range(SWEEPS):
            now = play(far, before, behind, False, patience)
            good = min(good or now, now, key=lambda x: x[0])
            far = play(now[2], behind, before, True, patience)[2]
        rev = sweep(sorted(range(len(ops)), key=lambda j: (-good[1][j], -j)), behind, True)
        now = sweep(sorted(range(len(ops)), key=lambda j: (-rev[1][j], j)), before, False)
        best = min(best or good, good, now, key=both)
        INFO.append(now[0])
    seed = 1
    for k in range(TRIES):
        if k % 8 == 0:
            base = sweep(sorted(range(len(ops)), key=lambda j: (-best[1][j], -j)), behind, True)[2]
        far = {}
        for i in range(len(ops)):
            seed = (seed * 1103515245 + 12345) % 2147483648
            far[i] = base[i] + (0.15, 0.4, 0.8)[k % 3] * seed / 2147483648.0
        best = min(best, play(far, before, behind, False, PATIENCE[k % len(PATIENCE)]), key=both)
        INFO.append(both(best))
    for i, o in enumerate(ops):
        o["eng"] = best[3][i]
    return sorted(range(len(ops)), key=lambda j: (best[1][j], j))


def rank_program(g, core, T, topo):
    rank = T.rank_of(core)
    if rank is None:
        return
    n = len(T.cores)
    ops, marks, bank, sent = [], {}, {}, []

    def v(name, a=None, b=None, s=None, p=None):
        r = range(*slice(a, b, s).indices(SCRATCH[name][1][1]))
        lo, hi = min(r[0], r[-1]), max(r[0], r[-1]) + 1
        return (T[name][slice(None) if p is None else p, slice(a, b, s)], [(name, lo // 8 * 8, -(-hi // 8) * 8, p and p.start)], len(r), SCRATCH[name][2])

    def ix(w, o):
        return (w[0].indirect(o[0]), w[1] + o[1], 16 * o[2], "list")

    def op(alt, r=(), w=(), sem=None, inc=16, late=0.0, after=()):
        me, deps, after = len(ops), set(), list(after)
        eng = list(alt)[0] if len(alt) == 1 else "f%d" % me
        rs = [x for a in r if isinstance(a, tuple) for x in a[1]]
        ws = [x for a in w for x in a[1]]
        for lst, wr in ((rs, False), (ws, True)):
            for nm, lo, hi, row in lst:
                for m in marks.setdefault(nm, []):
                    if m[0] < hi and lo < m[1] and (wr or m[3]) and (row is None or m[4] is None or row == m[4]):
                        deps.add(m[2])
                if nm in BANKS:
                    if bank.setdefault(nm, (eng, [], []))[0] != eng:
                        bank[nm] = (eng, bank[nm][2], [])
                    deps.update(bank[nm][1])
                    bank[nm][2].append(me)
        for nm, lo, hi, row in rs:
            marks[nm].append((lo, hi, me, False, row))
        for nm, lo, hi, row in ws:
            keep = [m for m in marks[nm] if m[0] < lo or m[1] > hi or sem is not None]
            marks[nm] = keep + [(lo, hi, me, True, row)]
        deps.discard(me)
        deps = [d for d in deps if not (sem is not None and ops[d]["sem"] == sem)]
        if eng == "t":
            deps = [d for d in deps if ops[d]["eng"] != "t"]
        ops.append({"eng": eng, "alt": alt, "deps": deps, "after": after, "sem": sem, "inc": inc, "late": late,
                    "list": any(isinstance(a, tuple) and len(a) > 3 and a[3] == "list" for a in r)})
        return me

    V, S, PE = g.vector, g.scalar, g.tensor

    def ap(x):
        return x[0] if isinstance(x, tuple) else x

    def cv(out, *a):
        if out[3] == "list" or a and a[0][3] == "list":
            return FIXV + out[2] * CYCLE * (SCATTER if out[3] == "list" else GATHER)
        return FIXV + max(64, out[2] * (0.5 if all(x[3] in (bf, u16) for x in (out,) + a) else 1)) * CYCLE

    def cs(out, a):
        return FIXS + (out[2] * GATHER if a[3] == "list" else max(64, out[2])) * CYCLE

    def ts(out, a, s1, s2, o0, o1=None):
        if o1 is None:
            op({"v": (lambda: V.tensor_scalar(out[0], a[0], ap(s1), None, o0), cv(out, a))}, [a, s1], [out])
        else:
            op({"v": (lambda: V.tensor_scalar(out[0], a[0], ap(s1), ap(s2), o0, o1), cv(out, a))}, [a, s1, s2], [out])

    def tt(out, a, c, o):
        k = 1 if a[3] == "list" or a[1][0][0] in BANKS or c[1][0][0] in BANKS else 2
        op({"v": (lambda: V.tensor_tensor(out[0], a[0], c[0], o), k * cv(out, a, c))}, [a, c], [out])

    def cp(out, a):
        op({"v": (lambda: V.tensor_copy(out[0], a[0]), cv(out, a))}, [a, out] if out[3] == "list" else [a], [(None, out[1][:1])])

    def ms(out, c):
        op({"v": (lambda: V.memset(out[0], c), cv(out))}, (), [out])

    def scan(out, d0, d1, ini, o0, o1):
        op({"v": (lambda: V.tensor_tensor_scan(out[0], d0[0], d1[0], ap(ini), o0, o1), cv(out, d0, d1))}, [d0, d1, ini], [out])

    def vtr(out, a):
        op({"v": (lambda: V.transpose(out[0], a[0]), cv(out, a))}, [a], [out])

    def act(out, a, f, bias=0.0, scale=1.0, acc=None):
        if acc is None:
            op({"s": (lambda: S.activation(out[0], a[0], f, bias=ap(bias), scale=ap(scale)), cs(out, a))}, [a, bias, scale], [out])
        else:
            op({"s": (lambda: S.activation(out[0], a[0], f, bias=ap(bias), scale=ap(scale), accum_out=acc[0]), cs(out, a))},
               [a, bias, scale], [out, acc])

    def lin(out, a, scale=1.0, bias=0.0, who="vs"):
        plain = not isinstance(scale, tuple) and not isinstance(bias, tuple) and scale == 1.0 and bias == 0.0
        alt = {"v": ((lambda: V.tensor_copy(out[0], a[0])) if plain else
                     (lambda: V.tensor_scalar(out[0], a[0], ap(scale), ap(bias), A.mult, A.add)), cv(out, a)),
               "s": ((lambda: S.activation(out[0], a[0], F.Copy)) if plain else
                     (lambda: S.activation(out[0], a[0], F.Identity, bias=ap(bias), scale=ap(scale))), cs(out, a))}
        op({e: alt[e] for e in who}, [a, bias, scale], [out])

    def zero(out, who):
        z = v("zb", 0, out[2])
        alt = {"v": (lambda: V.memset(out[0], 0.0), cv(out)), "s": (lambda: S.activation(out[0], z[0], F.Copy), cs(out, z)),
               "g": (lambda: g.iota(out[0], [[0, out[2]]], 0, 0, allow_small_or_imprecise_dtypes=True), 0.13 + 2 * out[2] * CYCLE)}
        op({who: alt[who]}, [z] if who == "s" else [], [out])

    sums, ends = {}, {}

    def mm(out, l, rh, st=False, sp=None):
        gs, me = sums.setdefault(out[1][0][0], [[]]), len(ops)
        if st:
            gs.append([])
        gs[-1].append(me)
        op({"t": (lambda: PE.matmul(out[0], l[0], rh[0], me in ends["first"], me in ends["last"]),
                  max(64, rh[2]) * (4 if l[3] == f32 else 1) * PECYCLE)}, [l, rh], [out], after=gs[-2])

    def iota(out, pat, base, cm, flt=True):
        if flt:
            op({"g": (lambda: g.iota(out[0], pat, base, cm, allow_small_or_imprecise_dtypes=True), 0.13 + 2 * out[2] * CYCLE)}, (), [out])
        else:
            op({"g": (lambda: g.iota(out[0], pat, base, cm), 0.13 + 2 * out[2] * CYCLE)}, (), [out])

    def sel(out, a, pat, o, base, cm):
        op({"g": (lambda: g.affine_select(out[0], a[0], pat, o, 0.0, base, cm), 0.17 + 2 * out[2] * CYCLE)}, [a], [out])

    moved, copies, low, lead = {}, [], [], []

    def dma(q, out, a, sem, kb):
        o, i = (out if isinstance(out, tuple) else (out, [])), (a if isinstance(a, tuple) else (a, []))
        copies.append(op({q: (lambda: (g.sync if q == "y" else g.scalar).dma_start(o[0], i[0]), 0.06)}, [i], [o], sem=sem,
                         late=DMA0, after=copies[-1:] if q == "y" and sem[0] != "o" else []))
        j = op({"d": (None, kb / DMARATE)}, sem=sem, inc=0)
        ops[j]["follows"] = copies[-1]

    def gather(who, out, w, off):
        lin(out, ix(w, off), who="vs" if who == "f" else who)

    I, NI, ID = v("ib", 0, 128), v("nib"), F.Identity
    turnb = [0]

    def nextb():
        turnb[0] += 1
        return "pb%d" % (turnb[0] % 4)

    def X(a, b, s=None):
        return v("win", XO + a, XO + b, s)

    def G(a, b, s=None):
        return v("win", GO + a, GO + b, s)

    def E(w, c):
        return v("eb", 144 * w + 15 - c, 144 * w + 143 - c)

    def EW(w):
        return v("eb", 144 * w + 15, 144 * w + 143, 16)

    def pc(j):
        return v("pf", j, j + 1)

    def col(name, j):
        return (T[name][:, j:j + 1], [(name, j, j + 1, None)], 1, SCRATCH[name][2])

    ms(v("zb"), 0.0)
    ms(v("thi"), 0)
    dma("s", v("li"), T.l0[:], "ldl", 128)
    dma("y", v("tab"), T.x0[:], "ldx", 1024)
    dma("y", v("thi", 0, 3, None, slice(0, 128, 16)), T.th[:], "ldt", 10)
    dma("y", v("zc"), T.z0[:], "ldz", 100)
    ms(v("oneb"), 1.0)
    iota(v("pint", 0, 1), [[0, 1]], 0, 1, False)
    iota(v("dupf"), [[1, 16], [0, 2]], 0, 0)
    iota(v("selff"), [[32, 16]], 0, 0)
    iota(v("colf"), [[1, 16]], 0, 0)
    sel(v("ib"), v("oneb"), [[0, 2], [-1, 128]], A.is_equal, 0, 1)
    sel(v("bob"), v("oneb", 0, 128), [[-16, 8], [0, 16]], A.is_ge, 0, 1)
    sel(v("bob"), v("bob"), [[16, 8], [0, 16]], A.is_ge, 15, -1)
    iota(v("tcol"), [[1, 72]], 0, 0)
    iota(v("kt"), [[1, 256]], 0, 0)
    iota(v("lf", 0, 16), [[128, 2], [2, 8]], 0, 0)
    iota(v("lf", 16, 32), [[128, 2], [1, 8]], 0, 0)
    iota(v("lf", 32, 64), [[128, 2], [1, 8], [0, 2]], 0, 0)
    B8 = v("bob", 0, 128, 16)
    moved["fill"] = 1200

    def fill(j0, j1):
        for j in range(j0, j1):
            u = 4 * FILLED[j // 4] + j % 4
            if FILLER[j] == "y":
                moved["fill%d" % (j // 4)] = 1200 + 256 * FILLER[:j].count("y")
                dma("y", v("win", 1024 * u, 1024 * u + 1024), v("zb"), "fill%d" % (j // 4), 256)
            else:
                zero(v("win", 1024 * u, 1024 * u + 1024), FILLER[j])

    for j in range(32):
        if FILLER[j] in "yg":
            fill(j, j + 1)
    zero(v("eb"), "s")
    lin(v("nib256"), I, -256.0)
    lin(v("bo"), v("bob"))
    lin(EW(0), B8)
    lin(NI, I, -1.0)
    ts(col("pint", 1), col("pint", 0), 15, None, A.bitwise_and)
    ts(col("pint", 2), col("pint", 0), 31, None, A.bitwise_and)
    ts(col("pint", 3), col("pint", 0), 7, None, A.bitwise_and)
    cp(v("pf", 0, 4), v("pint", 0, 4))
    PC, PJ = col("pf", 1), col("pf", 2)
    ts(v("pf", 8, 12), v("pf", 0, 4), 16.0, None, A.mult)
    ts(v("dup"), v("dupf"), col("pf", 9), None, A.add)
    ts(v("selc"), v("selff"), PJ, None, A.add)
    ts(v("pt"), v("colf"), col("pf", 9), None, A.add)

    def turn(src, dup, c0, c1):
        lin(v("w1", c0, c1), ix(src, dup), who="vs" if src[3] == f32 else "v")
        vtr(v("w2", c0, c1), v("w1", c0, c1))

    def digits(a, c0, c1):
        r, d0 = v("r32", c0, c1), v("dig", c0, c1)
        ts(r, a, M16, M16, A.add, A.subtract)
        lin(v("hh", c0, c1), r, 1.0 / 256.0, 191.53125, DGW)
        lin(d0, v("hh", c0, c1), 1.0, -199.5, DGW)
        tt(v("dig", 512 + c0, 512 + c1), a, r, A.subtract)
        low.append(len(ops) - 1)
        b = v(nextb(), c0, c1)
        mm(b, I, r, True)
        mm(b, v("nib256"), v("hh", c0, c1))
        lin(v("dig", 256 + c0, 256 + c1), b, 1.0 / 16.0, 3064.5, DGW)

    def window(t):
        def row(pl, sh):
            if t == 0:
                return v("tmp", sh, RG, None, slice(pl, 128, 16))
            return v("win", RG * MASTER[pl] + sh, RG * MASTER[pl] + RG, None, slice(0, 128, 16))
        for pl in (2, 0, 1):
            dma("y", row(pl, 0), v("dig", 256 * pl, 256 * pl + 256), "la%d%d" % (t, pl), 110)
        if t == 0:
            cells = sorted(CELLS + [(0, MASTER[pl], pl, 0) for pl in range(3)], key=lambda x: FILLED.index(x[1]))
        else:
            cells = sorted(CELLS, key=lambda x: (2, 0, 1).index(x[2]))
        for pa, rg, pl, sh in cells:
            moved["lb0"] = 256
            dma("y", v("win", RG * rg, RG * rg + RG - sh, None, slice(pa, 128, 16)), row(pl, sh), "lb%d" % t, CELLKB)
            if t == 0 and pa == 1 and rg in (1, 5):
                dma("y", v("win", RG * rg, RG * rg + RG, None, slice(4, 128, 16)), v("c19"), "lb0", 64)

    def pairs():
        for j in range(2):
            c0, d0 = 256 * j, 256 * j + 256
            mm(v("pq1", c0, c0 + 255), v("ip16"), v("dig", d0, d0 + 255), j == 0)
            mm(v("pq1", c0, c0 + 255), I, v("dig", d0 + 1, d0 + 256))
            mm(v("pq1", c0 + 255, c0 + 256), v("ip16"), v("dig", d0 + 255, d0 + 256))
            mm(v("pq1", c0 + 255, c0 + 256), v("ib", 1, 129), v("dig", d0, d0 + 1))

    def starts(t):
        if BYS[0] == "s":
            act(v("bb"), v("nb", 32, 320), F.Relu, bias=BIG, scale=-4.0)
        else:
            ts(v("bb"), v("nb", 32, 320), 0.0, BIG, A.is_equal, A.mult)
        for j in range(2):
            if BYS[1 + j] == "s":
                for c0, c1 in ((0, 255), (255, 256)):
                    mm(v("pq1", 256 * j + c0, 256 * j + c1), I, v("nb", 32 + c0, 32 + c1))
        for j in range(2):
            if BYS[1 + j] == "s":
                lin(v("va", 288 * j, 288 * j + 256), v("pq1", 256 * j, 256 * j + 256), who="s")
            else:
                tt(v("va", 288 * j, 288 * j + 256), v("nb", 32, 288), v("pq1", 256 * j, 256 * j + 256), A.add)
        scan(v("hc", 0, 288), v("bb"), v("va", 0, 288), BIG, A.add, A.min)
        scan(v("hc", 575, 287, -1), v("bb"), v("va", 288, 576), BIG, A.add, A.min)
        vtr(v("ht2"), v("hc", 256, 320))
        scan(v("car2"), v("cd2"), v("ht2"), BIG, A.add, A.min)
        ts(v("cr", 0, 2), v("car2", 31, 64, 32), 32 * M16, 32 * M16, A.add, A.subtract)
        lead[:] = [len(ops) - 1]
        tt(v("cr", 8, 10), v("car2", 31, 64, 32), v("cr", 0, 2), A.subtract)
        lead.append(len(ops) - 1)
        for j in range(2):
            a, h = v("st", 256 * j, 256 * j + 256), v("st", 512 + 256 * j, 768 + 256 * j)
            scan(a, v("bb", 0, 256), v("va", 288 * j, 288 * j + 256), col("cr", 8 + j), A.add, A.min)
            lead.append(len(ops) - 1)
            lin(h, a, 1.0 / 16.0, 199.5, BYS[3])
            for src, pa, rg in ((a, 2, (2, 7)[j]), (h, 2, (1, 5)[j])):
                dma("y", v("win", RG * rg, RG * rg + RG, None, slice(pa, 128, 16)), src, "lc%d" % t, LCKB)

    cp(v("nu"), v("li"))
    turn(v("li"), v("dup"), 0, 512)
    lin(v("s4"), ix(v("w2"), v("selc")), 1.0, -7.5)
    digits(v("s4"), 0, 256)
    for j in range(FIRST):
        if FILLER[j] in "vs":
            fill(j, j + 1)
    ms(v("dinit"), 0.0)
    cp(v("th8"), v("thi"))
    ts(v("dinit", 0, 1), PC, 0.0, -4096 * BIG, A.is_equal, A.mult)
    mm(v("pq0", 0, 8), v("bo"), v("th8"), True, True)

    def ztile():
        for h in range(2):
            c0 = 1024 * h
            lin(v("z2", c0, c0 + 128), ix(v("zc"), v("pt", 8 * h, 8 * h + 8)))
            for w in (128, 256, 512):
                sel(v("z2", c0 + w, c0 + 2 * w), v("z2", c0, c0 + w), [[0, w]], A.is_gt, 1, 0)

    def consts_v():
        t, d, e = v("tcol", 0, 65), v("cd", 0, 65), v("ce", 0, 65)
        ts(v("thp"), v("pq0", 0, 8), 0.5, None, A.add)
        ts(col("thb", 0), col("thp", 0), BIG / 2, None, A.mult)
        ts(col("pf", 12), PC, 256.0, None, A.mult)
        lin(v("kt"), v("kt"), 1.0, col("pf", 12))
        lin(v("i32"), I)
        ms(v("nb"), BIG)
        ms(v("three"), 0.0)
        ms(v("zadd"), 0.0)
        ms(v("three", 0, 256), 2.0)
        ms(v("zadd", 0, 256), 1.0)
        ts(v("zadd", 256, 257), PC, 0.0, BIG, A.is_equal, A.mult)
        tt(col("pf", 13), PJ, PC, A.subtract)
        ts(col("pf", 14), PC, 0.0, -LOW, A.is_gt, A.mult)
        ts(col("pf", 15), PJ, 33.0, None, A.add)
        ts(col("pf", 16), PJ, 16.0, LOW, A.is_lt, A.mult)
        ts(d, t, PJ, 512.0, A.is_lt, A.mult)
        ms(v("cd", 33, 64), -256.0)
        ts(e, t, col("pf", 13), 2 * BIG, A.is_equal, A.mult)
        tt(d, d, e, A.add)
        ts(e, t, PJ, col("pf", 14), A.is_equal, A.mult)
        tt(d, d, e, A.add)
        for j in range(2):
            lin(v("cd2", 32 * j, 32 * j + 32), v("cd", 0, 32))
        lin(col("cd2", 32), col("cd2", 32), 1.0, LOW)
        ms(v("va"), BIG)
        lin(v("ip16"), I, 16.0)
        lin(v("c19"), v("oneb"), -19.0)
        ts(e, t, col("pf", 15), 2 * BIG, A.is_equal, A.mult)
        tt(d, d, e, A.add)
        ts(col("cd", 32), col("pf", 14), -1.0, None, A.mult)
        tt(col("cd", 48), col("cd", 48), col("pf", 16), A.subtract)
        lin(col("pf", 18), PC, -256.0, 3584.0)
        lin(col("pf", 19), col("pf", 16), 1.0 + 4096.0 / LOW, col("pf", 18))
        tt(col("cd", 64), col("cd", 64), col("pf", 19), A.add)
        lin(col("ht", 64), PC, -256.0, 3840.0)
        lin(EW(2), B8, -BIG / 2)
        ts(col("pf", 28), PC, 8.0, col("pf", 11), A.is_ge, A.add)
        ts(v("pta"), v("lf", 0, 16), col("pf", 28), None, A.add)

    def consts_s():
        ts(col("pf", 20), PC, 0.0, 256.0, A.is_equal, A.mult)
        ts(col("pf", 21), PC, 1.0, 16.0, A.is_equal, A.mult)
        ts(col("pf", 22), PC, 4.0, 10.5, A.is_equal, A.mult)
        ts(col("pf", 23), PC, 2.0, col("pf", 20), A.is_equal, A.add)
        ts(col("pf", 27), col("pf", 23), col("pf", 21), col("pf", 22), A.add, A.add)
        lin(EW(4), B8, col("pf", 27))
        lin(v("c2040"), v("oneb", 0, 128), 2040.0)
        ztile()
        for w, c in ((1, -1.0), (3, -2.0), (6, 2.0)):
            lin(EW(w), B8, c)
        lin(v("ib256"), v("ib"), 256.0)
        lin(v("cm05"), v("oneb"), -0.5)
        lin(v("cb"), v("colf"), 256.0, col("pf", 9))
        lin(v("ym16"), v("zb", 0, 512), 1.0, 1.0)
        lin(v("ym16", 0, 512, 16), v("zb", 0, 32))
        lin(col("pf", 29), PC, 8.0)
        ts(v("ptb"), v("lf", 16, 32), col("pf", 29), None, A.add)
        ts(v("dup2"), v("lf", 32, 64), col("pf", 29), None, A.add)
        ts(col("pf", 17), PC, 31.0, PJ, A.mult, A.add)
        ts(v("sell"), v("colf"), col("pf", 17), None, A.add)

    def xg(u0, u1, who):
        gather(who, X(512 * u0, 512 * u1), v("tab"), v("nu", 32 * u0, 32 * u1))

    def calls(who, u0, u1):
        out = []
        for u in range(u0, u1):
            if who[u].isupper():
                out[-1][2] = u + 1
            else:
                out.append([who[u], u, u + 1])
        return out

    def first_x():
        D = v("px0", 0, 256)
        mm(D, I, v("dinit", 0, 256), True, False)
        for who, u0, u1 in calls(X0, 0, 8):
            xg(u0, u1, who)
        for u in range(8):
            bn, c1 = nextb(), int(u == 0)
            mm(v(bn, c1, 512), I, X(512 * u + c1, 512 * u + 512), True, False)
            if c1:
                mm(v(bn, 0, 1), I, X(0, 1))
            mm(v(bn, c1, 512), NI, X(512 * u - 1 + c1, 512 * u + 511), False, True)
            act(G(512 * u, 512 * u + 512), v(bn), F.Abs)
            for c in (2 * u, 2 * u + 1):
                mm(D, E(2, c), G(256 * c, 256 * c + 256))
        begins(0, 256, D)

    def begins(c0, c1, D):
        out, th = v("nb", 32 + c0, 32 + c1), col("thb", 0)
        op({"v": (lambda: V.tensor_scalar(out[0], D[0], th[0], 0.0, A.add, A.max), cv(out, D)),
            "s": (lambda: S.activation(out[0], D[0], F.Relu, bias=th[0]), cs(out, D))}, [D, th], [out])

    def piece(u):
        c0 = 512 * u
        if DX[u] == "v":
            tt(v("d3", c0, c0 + 512), X(c0, c0 + 512), X(c0 - 16, c0 + 496), A.subtract)
            act(G(c0, c0 + 512), v("d3", c0, c0 + 512), F.Abs)
            return
        bn = nextb()
        if u > 0:
            mm(v(bn), I, X(c0, c0 + 512), True, False)
            mm(v(bn), NI, X(c0 - 16, c0 + 496), False, True)
        else:
            mm(v(bn, 0, 16), I, X(0, 16), True, False)
            mm(v(bn, 16, 512), I, X(16, 512), False, False)
            mm(v(bn, 16, 512), NI, X(0, 496), False, False)
            mm(v(bn, 0, 16), NI, X(4079, 4095), False, True)
        act(G(c0, c0 + 512), v(bn), F.Abs)

    def dsum(q):
        out = v("px0", 64 * q, 64 * q + 64) if q < 3 else v("px1", 0, 64)
        if q == 0:
            mm(out, I, v("dinit", 0, 64))
        for c in range(16):
            mm(out, E(2, c), G(1024 * q + c, 1024 * q + 1024, 16), q & 1 and c == 0)

    Y = v("tmp", 15, 4096, 16)

    def yscan(c):
        scan(v("tmp", 256 * c, 256 * c + 256), v("ym16", 0, 256), X(c, 4096, 16), 0.0, A.mult, A.max)

    def blocks_a():
        b1 = "pq0"
        mm(v(b1, 0, 256), I, Y, True, False)
        mm(v(b1, 0, 256), NI, v("zc"))
        mm(v(b1, 256, 512), I, Y)
        mm(v(b1, 256, 512), I, v("zc"))
        mm(v(b1, 256, 512), I, v("cm05"))
        for b in range(16):
            mm(v("pb0", 0, 16), E(0, b), v("tmp", 15 + 16 * b, 4096, 256), b == 0)
        act(v("zc"), v(b1, 0, 256), F.Abs)
        ztile()
        if AVG == "s":
            lin(v("zs"), v(b1, 256, 512), 0.5, M1, "s")
            lin(v("avg"), v("zs"), 1.0, -M1, "s")
            return
        ts(v("avi"), v(b1, 256, 512), 0.5, None, A.mult)

    def blocks_b():
        cp(v("ui", 0, 16), v("pb0", 0, 16))
        ts(v("ui", 16, 32), v("ui", 0, 16), 15, None, A.bitwise_and)
        tt(v("uf"), v("ui", 16, 32), v("cb"), A.add)
        cp(v("cu"), v("uf"))

    def update():
        cp(ix(v("tab"), v("cu")), v("avg" if AVG == "s" else "avi"))
        ops[-1]["after"] += low[-1:] * SENDFIRST

    def periods(t):
        scan(v("hb", 0, 288), v("three"), v("nb", 32, 320), BIG, A.add, A.min)
        scan(v("hb", 575, 287, -1), v("zadd"), v("nb", 287, None, -1), BIG, A.add, A.min)
        vtr(v("ht", 0, 64), v("hb", 256, 320))
        scan(v("car", 0, 65), v("cd", 0, 65), v("ht", 0, 65), BIG, A.add, A.min)
        scan(v("jj"), v("three", 0, 256), v("nb", 32, 288), col("car", 32), A.add, A.min)
        ops[-1]["after"] += lead[:AFIRST[0]]
        scan(v("pb0", 255, None, -1), v("nb", 288, 32, -1), v("oneb"), col("car", 64), A.min, A.add)
        ops[-1]["after"] += lead[:AFIRST[1]]
        i2, hf, uu, vv, bu, bv, t1, s2 = [v(x) for x in "jj sp uu vv bu bv s1 s2".split()]
        J, xx, f2, cl, cl2 = v("pb0", 0, 256), v("pb0", 256, 512), v("pb1", 0, 256), v("pb2", 0, 256), v("pb3", 0, 256)
        mm(f2, v("i32"), v("kt"), True)
        mm(f2, v("i32"), i2)
        lin(hf, i2, -0.5, 3.0 * RG, "s")
        tt(uu, i2, J, A.subtract)
        tt(cl, hf, J, A.subtract)
        tt(vv, uu, cl, A.add)
        act(bu, uu, F.Relu, bias=3.0 * RG, scale=float(RG))
        act(bv, vv, F.Relu, bias=2.0 * RG * (3 - 3 * RG), scale=2.0 * RG)
        tt(t1, bu, cl, A.min)
        lin(cl2, cl, 1.0, 3.0 * RG, "s")
        tt(xx, t1, f2, A.add)
        for c0, c1 in LAST:
            tt(v("s2", c0, c1), v("bv", c0, c1), v("pb3", c0, c1), A.min)
            tt(v("s4", c0, c1), v("s2", c0, c1), v("pb0", 256 + c0, 256 + c1), A.add)
            for h in range(c0 // 128, c1 // 128):
                cp(half("oa", 0, h), ix(v("s4", 0, 128 * h + 128), v("pta", 8 * h, 8 * h + 8)))

    def pg(w, eng, u0, u1):
        gather(eng, v("g" + w, 512 * u0, 512 * u1), v("win"), v("o" + w, 32 * u0, 32 * u1))

    def psum_(w, q, first=False, last=False):
        bn = "px%d" % (q // 2)
        mm(v(bn, 64 * (q & 1), 64 * (q & 1) + 64), I, v("c2040", 0, 64), first)
        for c in range(16):
            mm(v(bn, 64 * (q & 1), 64 * (q & 1) + 64), E(4 if w == "a" else 5, c), v("g" + w, 1024 * q + c, 1024 * q + 1024, 16),
               False, last and c == 15)

    def half(name, t, h):
        return v(name, 256 * t + 128 * h, 256 * t + 128 * h + 128)

    def send(t, h):
        bn = "px%d" % h
        P, r16, hi, lo = v(bn, 0, 128), half("r16", 0, h), half("hi", t, h), half("lo", t, h)
        ts(r16, P, M16, M16, A.add, A.subtract)
        lin(hi, r16, 1.0 / 256.0, 191.53125)
        tt(lo, P, r16, A.subtract)
        low.append(len(ops) - 1)
        d1, d2 = T.cores[(rank + 1) % n], T.cores[(rank + 2) % n]
        e1, e2 = topo.engines(core, d1)[0::2], topo.engines(core, d2)[1::2]
        trs = []
        for d, es, src, dst, sm in ((d1, e1, hi, "hin", "ah"), (d2, e2, lo, "lin", "al")):
            rid, pid = topo.addr(d)[0:2]
            trs.append(RemoteDMATransfer(dst_ids=[DstId(rid=rid, pnc=pid)], dma_engine_mask=sum(1 << e for e in es),
                                         remote_sem=T.sem["%s%d%d" % (sm, t, h)], src=src[0], dst=half(dst, t, h)[0]))
        sent.append(op({"g": (lambda: g.remote_dma_fused(trs, local_sem=T.sem.loc), 0.2)}, [hi, lo], [], sem="loc",
                       inc=len(e1) + len(e2), after=sent[-1:]))
        p1, p2 = T.cores[(rank - 1) % n], T.cores[(rank - 2) % n]
        for nm, sm, es in (("hin", "ah", topo.engines(p1, core)[0::2]), ("lin", "al", topo.engines(p2, core)[1::2])):
            op({"x": (None, 0.0)}, [], [half(nm, t, h)], sem="%s%d%d" % (sm, t, h), inc=len(es), late=TRAVEL, after=sent[-1:])
        ts(half("pu", 0, h), P, 7.5, None, A.add)
        M, D = v(bn, 128, 256), v(bn, 384, 512)
        mm(M, I, r16, True, False)
        mm(D, NI, lo, False, False)
        for o in (M, D):
            mm(o, v("nib256"), hi, False, False)

    def arrive(t, h):
        bn = "px%d" % h
        for c0 in (128, 384):
            mm(v(bn, c0, c0 + 128), v("ib256", 112, 240), half("hin", t, h), False, False)
            mm(v(bn, c0, c0 + 128), v("ib", 96, 224), half("lin", t, h), False, c0 == 384)

    def moff(h):
        ts(half("mu", 0, h), v("px%d" % h, 128, 256), 7.5, None, A.add)

    def dgather(k, h, who):
        off, d, a = (("pu", "d3", "a3"), ("mu", "d4", "a4"))[k]
        for md, u0, u1 in spans(k, h):
            c0, c1 = 512 * u0, 512 * u1
            src = ix(v("tab"), v(off, 32 * u0, 32 * u1))
            if md[0] != who:
                continue
            if who == "S":
                act(v(d, c0, c1), src, F.Copy)
            else:
                tt(v(d, c0, c1), src, v("z2", 1024 * h, 1024 * h + c1 - c0), A.subtract)
                if md == "VV" and not u1 & 1:
                    ts(v(a, c1 - 1024, c1), v(d, c1 - 1024, c1), 0.0, None, A.max)

    def kinds(k, h):
        return (DP, DL if rnd[0] == 2 else DM)[k][h]

    def spans(k, h):
        modes, out = kinds(k, h), []
        for q in range(2):
            u = 4 * h + 2 * q
            if modes[2 * q] == modes[2 * q + 1] and JOIN[4 * k + 2 * h + q] == "1":
                out.append((modes[2 * q], u, u + 2))
            else:
                out += [(modes[2 * q], u, u + 1), (modes[2 * q + 1], u + 1, u + 2)]
        return out

    def dabs(k, h):
        d, a = (("d3", "a3"), ("d4", "a4"))[k]
        for md, u0, u1 in spans(k, h):
            if md == "SS":
                for c0 in range(512 * u0, 512 * u1, 512):
                    b = v(nextb())
                    mm(b, I, v(d, c0, c0 + 512), True, False)
                    mm(b, NI, v("z2", 1024 * h, 1024 * h + 512), False, True)
                    act(v(a, c0, c0 + 512), b, F.Abs)
            elif md == "VS":
                act(v(a, 512 * u0, 512 * u1), v(d, 512 * u0, 512 * u1), F.Abs)

    def dsums(k, h):
        d, a = (("d3", "a3"), ("d4", "a4"))[k]
        wa, wr, wd = ((1, 3, 0), (0, 6, 1))[k]
        bn, modes = "pq%d" % h, kinds(k, h)
        todo = [(q, d, wd) for q in range(2) if modes[2 * q] == "VV"]
        todo += [(q, a, wr if modes[2 * q] == "VV" else wa) for q in range(2)]
        for j, (q, buf, w) in enumerate(todo):
            c0 = 2048 * h + 1024 * q
            for c in range(16):
                mm(v(bn, 64 * q, 64 * q + 64), E(w, c), v(buf, c0 + c, c0 + 1024, 16), k == 0 and j == 0 and c == 0)

    def choose(h):
        bn = "px%d" % h
        ts(half("sg", 0, h), v("pq%d" % h, 0, 128), 0.0, None, A.is_lt)
        tt(half("s2", 0, h), half("sg", 0, h), v(bn, 384, 512), A.mult)
        tt(half("s3", 0, h), half("s2", 0, h), v(bn, 0, 128), A.add)

    def threshold(t):
        b = v("px1", 256, 384)
        mm(b, v("bob"), half("sg", 0, 0), True)
        mm(b, v("bob"), half("sg", 0, 1))
        a = col("acc", 0)
        op({"v": (lambda: V.tensor_reduce(a[0], b[0], AxisListType.X, A.add), cv(b))}, [b], [a])
        cp(col("ai", 0), a)
        ts(col("ai", 8), col("ai", 0), 31, None, A.bitwise_and)
        ts(col("thb", 0), col("ai", 8), col("thp", t), BIG / 2, A.add, A.mult)

    consts_v()
    first_x()
    for j in range(FIRST, 32):
        if FILLER[j] in "vs":
            fill(j, j + 1)
    window(0)
    consts_s()
    rnd = [0]
    for t in range(3):
        rnd[0] = t
        pairs()
        starts(t)
        periods(t)
        for h in range(2):
            if t > 0 and h == 1:
                for c in range(16):
                    yscan(c)
                blocks_a()
                blocks_b()
                update()
            for who, u0, u1 in calls(PG[min(t, 1)]["a"], 4 * h, 4 * h + 4):
                pg("a", who, u0, u1)
            for q in (2 * h, 2 * h + 1):
                psum_("a", q, first=q == 2 * h)
            send(t, h)
        for k, h in DORDER:
            if k == 1:
                arrive(t, h)
                moff(h)
            dgather(k, h, "S")
            dgather(k, h, "V")
            dabs(k, h)
            dsums(k, h)
            if k == 1:
                choose(h)
                names = ix(half("s3", 0, 0) if h == 0 else v("s3"), v("ptb", 8 * h, 8 * h + 8))
                if t == 2:
                    turn(half("s3", 0, 0) if h == 0 else v("s3"), v("dup2", 16 * h, 16 * h + 16), 256 * h, 256 * h + 256)
                    continue
                ts(half("nu", 0, h), names, 7.5, None, A.add)
                for j in range(4 * h, 4 * h + 4):
                    xg(XORDER[j], XORDER[j] + 1, XG[j])
                    if XG[j] == "v" and j % 4 > DIGITS:
                        ops[-1]["after"].append(low[-1])
                    if j % 4 == DIGITS:
                        if not WHOLE:
                            digits(names, 128 * h, 128 * h + 128)
                        elif h == 1:
                            digits(ix(v("s3"), v("ptb")), 0, 256)
                        if h == 1:
                            window(t + 1)
                            threshold(t + 1)
                for j in ((1, 2, 3), (0, 4, 5, 6, 7))[h]:
                    piece(j)
                    if j in (0, 3, 5, 7):
                        dsum(j // 2)
        if t < 2:
            begins(0, 192, v("px0", 0, 192))
            begins(192, 256, v("px1", 0, 64))
    ts(v("nu"), ix(v("w2"), v("sell")), 7.5, None, A.add)
    lin(v("lyf"), ix(v("w2"), v("sell")), 1.0, 7.5)
    dma("y", T.ly[:], v("lyf"), "oly", 128)
    for u in range(8):
        xg(u, u + 1, XL[u])
    for u0, u1 in STORES:
        moved["oxy"] = 0
        dma("y", T.xy[:, 512 * u0:512 * u1], X(512 * u0, 512 * u1), "oxy", 128 * (u1 - u0))
    for u in range(8):
        scan(v("tmp", 512 * u, 512 * u + 512), v("ym16"), X(512 * u, 512 * u + 512), 0.0, A.mult, A.max)
    for bn, c0, c1 in (("pb0", 0, ZCUT), ("pb1", ZCUT, 256)):
        mm(v(bn, c0, c1), NI, v("zc", c0, c1), True, False)
        mm(v(bn, c0, c1), I, v("tmp", 15 + 16 * c0, 16 * c1, 16), False, True)
        act(v("zd", c0, c1), v(bn, c0, c1), F.Abs)
    dma("s", T.zy[:], v("zd"), "ozy", 64)

    queue = {"v": V, "s": S, "t": PE, "g": g, "r": g, "y": g.sync}
    esem = {"v": "cv", "s": "cs", "t": "ct", "g": "cg"}
    if not PLAN:
        PLAN.extend([arrange(ops), [o["eng"] for o in ops]])
    order = PLAN[0]
    for o, e in zip(ops, PLAN[1]):
        o["eng"] = e
    place = {i: j for j, i in enumerate(order)}
    ends["first"] = {min(x, key=place.get) for gs in sums.values() for x in gs if x}
    ends["last"] = {max(x, key=place.get) for gs in sums.values() for x in gs if x}
    total, need = {}, set()
    for o in ops:
        if o["sem"] is not None:
            total[o["sem"]] = total.get(o["sem"], 0) + o["inc"]
        best = {}
        for d in o["deps"]:
            e = ops[d]["eng"]
            if ops[d]["sem"] is None and (e not in best or place[d] > place[best[e]]):
                best[e] = d
        o["deps"] = [d for d in o["deps"] if ops[d]["sem"] is not None] + list(best.values())
        need.update(best.values())
    cnt, seen = {}, {}
    for i in order:
        o = ops[i]
        if o["eng"] in "xd":
            continue
        qn = o["eng"]
        q = queue[qn]
        for d in o["deps"]:
            p = ops[d]
            sm, val = (p["sem"], total[p["sem"]]) if p["sem"] is not None else (esem[p["eng"]], p["n"])
            if seen.get((qn, sm), 0) < val:
                q.wait_ge(T.sem[sm], val)
                seen[(qn, sm)] = val
        ins = o["alt"][qn][0]()
        if o["sem"] == "loc":
            continue
        if o["sem"] is not None:
            ins.then_inc(T.sem[o["sem"]], 16)
        elif i in need:
            sm = esem[o["eng"]]
            cnt[sm] = cnt.get(sm, 0) + 1
            o["n"] = cnt[sm]
            ins.then_inc(T.sem[sm], 1)
    total.update(cnt)
    for sm, val in total.items():
        g.wait_ge(T.sem[sm], val)
